import numpy as np, ml_dtypes
CORES = [24,25,26,27,28,29,30,31]
N = 8
BF = ml_dtypes.bfloat16
def gentries(a):
    return np.ascontiguousarray(a.reshape(8, 16, -1).transpose(0, 2, 1)).reshape(8, -1)
def gtable(e):
    e = np.asarray(e); return np.ascontiguousarray(e.reshape(8, -1, 16).transpose(0, 2, 1)).reshape(128, -1).astype(np.int32)
W, K, R, B, S, HOP, T = 2048, 2048, 768, 4, 1, 3, 4
LO = 640
def parts(rng):
    sh = (N, 8, 16, W)
    s = np.minimum(15, np.floor(16 * rng.random(sh) ** 2)); a = rng.integers(32, 257, sh) * 0.00390625
    m = np.exp2(-rng.choice(np.arange(5), sh, p=np.array([0.05, 0.1, 0.2, 0.3, 0.35])).astype(np.float64))
    x = rng.integers(-256, 256, sh); c = rng.integers(0, W, (N, 8, K))
    u = np.where(rng.random((N, 8, T, K)) < 0.5, np.floor(np.exp2(8 * rng.random((N, 8, T, K)))), rng.integers(0, 256, (N, 8, T, K)))
    z = rng.integers(0, 256, (N, 8, T, K))
    r = np.ascontiguousarray(np.argsort(rng.random((N, 8, T - 1, W // 2)), axis=-1)[..., :R])
    return s, a, m, x, c, np.clip(u, 0, 255), z, r
def pack(s, a, m, x, c, u, z, r):
    b = lambda v, p, n: np.ascontiguousarray(np.asarray(v, np.float32).reshape(N, p, n)).astype(BF)
    return {"sg": b(s, 128, W), "al": b(a, 128, W), "mj": b(m, 128, W), "nx": b(x, 128, W), "ce": np.stack([gtable(v) for v in c]),
            "uu": b(u, 8, T * K), "zz": b(z, 8, T * K), "rp": np.stack([gtable(v.reshape(8, -1)) for v in r])}
def two(rng, shape, lo, hi):
    return np.where(rng.random(shape) < 0.5, lo, hi)
def setup_inputs(rng):
    return pack(*parts(rng))
def setup_inputs_spread(rng):
    s, a, m, x, c, u, z, r = parts(rng); sh = (N, 8, 16, W); col = (N, 8, 1, W)
    s = np.minimum(15, np.floor(16 * rng.random(sh) * np.exp2(-3 * rng.random(col))))
    a = np.clip(np.exp2(-2 * rng.random(col)) * (0.5 + 0.5 * rng.random(sh)), 0.125, 1.0)
    m = np.exp2(-np.clip(rng.integers(0, 5, col) + rng.integers(-1, 2, sh), 0, 4).astype(np.float64))
    x = np.clip(np.floor((2 * rng.random(sh) - 1) * 256 * np.exp2(-6 * rng.random(col))), -256, 255)
    u = np.clip(np.floor(np.exp2(8 * rng.random((N, 8, 1, K))) * rng.random((N, 8, T, K))), 0, 255)
    z = np.clip(np.floor(256 * rng.random((N, 8, T, K)) ** 2), 0, 255)
    return pack(s, a, m, x, c, u, z, r)
def setup_inputs_ends(rng):
    s, a, m, x, c, u, z, r = parts(rng)
    s = two(rng, s.shape, 0, 15); a = two(rng, a.shape, 0.125, 1.0); m = two(rng, m.shape, 0.0625, 1.0); x = two(rng, x.shape, -256, 255)
    c = two(rng, c.shape, 0, W - 1); u = two(rng, u.shape, 0, 255); z = two(rng, z.shape, 0, 255)
    s[:, :, 0] = 0; s[:, :, 15] = 15; a[:, :, 15] = 1.0; m[:, :, 15] = 1.0
    c[..., K - 1] = W - 1; z[..., 15] = 0; z[..., K - 1] = 0
    places = np.concatenate([np.arange(R // 2), np.arange(W // 2 - R // 2, W // 2)])
    r = places[np.argsort(rng.random((N, 8, T - 1, R)), axis=-1)]
    return pack(s, a, m, x, c, u, z, r)
def setup_inputs_corners(rng):
    s, a, m, x, c, u, z, r = parts(rng); o = int(rng.integers(0, 4)); sh = (16, W)
    for q in range(N):
        for g in range(8):
            kind = (q + g + o) % 4
            if kind == 0:
                e = rng.integers(0, 4, sh); s[q, g] = 2 ** e; m[q, g] = np.exp2(-np.clip(e + rng.integers(-1, 2, sh), 0, 4).astype(np.float64))
            if kind == 1:
                s[q, g] = np.where(rng.random(sh) < 0.9, 15, s[q, g]); m[q, g] = np.where(rng.random(sh) < 0.9, 1.0, m[q, g])
            if kind == 2: m[q, g] = np.where(rng.random(sh) < 0.9, 0.0625, m[q, g])
            if kind == 3: x[q, g] = np.where(rng.random(sh) < 0.5, two(rng, sh, -256, 255), x[q, g])
    c = np.where(rng.random(c.shape) < 0.3, two(rng, c.shape, 0, W - 1), c)
    u = np.clip(rng.integers(0, 17, u.shape) * 2 ** rng.integers(0, 5, u.shape) + rng.integers(-1, 2, u.shape), 0, 255)
    z = np.clip(16 * rng.integers(0, 17, z.shape) + rng.integers(-1, 2, z.shape), 0, 255)
    return pack(s, a, m, x, c, u, z, r)
def setup_inputs_crowd(rng):
    s, a, m, x, c, u, z, r = parts(rng)
    c[:] = rng.integers(0, W, (N, 8, 1)); c[:, 1::4, K - 1] = (c[:, 1::4, K - 1] + rng.integers(1, W, (N, 2))) % W
    few = rng.integers(0, W, (N, 2, 4)); few[:, 0, 0] = W - 1; few[:, 0, 1] = 0
    c[:, 3::4] = np.take_along_axis(few, rng.integers(0, 4, (N, 2, K)), 2)
    u[:, :6] = u[:, :6, :, :1].copy(); z[:, :5] = z[:, :5, :, :1].copy()
    m[:, ::2] = m[:, ::2, :1].copy(); s[:, ::4] = s[:, ::4, :1].copy()
    h = W // 2; h0 = int(rng.integers(0, N)); st = int(rng.integers(1, 101)) * (2 * int(rng.integers(0, 2)) - 1)
    v = (int(rng.integers(0, h)) + st * np.arange(T + 1)) % h; odd = rng.integers(0, 2, T + 1)
    for t in range(T):
        for i in range(2): x[..., 2 * v[t] + i] = 2 * st + odd[t + 1] - i
    for i in range(2):
        e = 2 * v[1:] + i
        m[..., e] = 0.0625; s[..., e] = rng.integers(1, 16, (N, 8, 16, T)); s[:, :, 15, e] = 15
        a[..., e] = rng.integers(192, 257, (N, 8, 16, T)) * 0.00390625
    first = 255 * int(rng.integers(0, 2))
    for q in (h0, (h0 + HOP) % N):
        c[q] = 2 * v[0] + odd[0]
        z[q, :, 0] = first; z[q, :, 1] = 0; z[q, :, 2] = 255; z[q, :, 3:4] = 0
        z[q, 3::4, 1:4, K - 1] = 255 - z[q, 3::4, 1:4, K - 1]
    c[h0, 1::4, K - 1] = (c[h0, 1::4, K - 1] + rng.integers(1, W, 2)) % W
    return pack(s, a, m, x, c, u, z, r)
def setup_inputs_calm(rng):
    s, a, m, x, c, u, z, r = parts(rng)
    s = 8 + rng.integers(0, 2, s.shape); m = two(rng, m.shape, 0.0625, 0.125)
    for q in range(N): m[q, int(rng.integers(0, 8))] = 0.0625
    u = np.where(rng.random(u.shape) < 0.5, 8 * rng.integers(0, 32, u.shape), rng.integers(0, 256, u.shape))
    z = rng.choice(np.array([0, 127, 128, 143, 144, 255]), z.shape)
    h = W // 2; qa = int(rng.integers(0, N)); qb = (qa - HOP) % N; cell = np.arange(W); low = cell // h * h
    for q in (qa, qb): x[q] = np.clip(cell + x[q], low, low + h - 1) - cell
    s[qa, :, :, h:] = 8; c[qb] = rng.integers(h, W, (8, K))
    return pack(s, a, m, x, c, u, z, r)
def check_ranges(d):
    bad = []
    for k, lo, hi in (("sg", 0, 15), ("al", 0.125, 1), ("mj", 0.0625, 1), ("nx", -256, 255), ("ce", 0, W - 1), ("uu", 0, 255), ("zz", 0, 255), ("rp", 0, W // 2 - 1)):
        v = np.asarray(d[k]).astype(np.float64)
        if not (np.min(v) >= lo and np.max(v) <= hi): bad.append("range of " + k)
        elif k != "al" and k != "mj" and np.any(v != np.floor(v)): bad.append("whole numbers of " + k)
    if not np.all(np.isin(np.asarray(d["mj"]).astype(np.float64), np.array([0.0625, 0.125, 0.25, 0.5, 1.0]))): bad.append("powers of two of mj")
    e = np.sort(np.stack([gentries(np.asarray(v)) for v in d["rp"]]).reshape(N, 8, T - 1, R), axis=-1)
    if np.any(e[..., 1:] == e[..., :-1]): bad.append("distinct pairs of rp")
    return bad
def move(v, n):
    v = np.roll(v, n * HOP, axis=0); h = K // 2
    return np.concatenate([v[..., :h], np.roll(v[..., h:], n, axis=1)], axis=-1)
def reference(sg, al, mj, nx, ce, uu, zz, rp):
    s, a, m = [v.astype(np.float64).reshape(N, 8, 16, W) for v in (sg, al, mj)]; x = nx.astype(np.float32).astype(np.int64).reshape(N, 8, 16, W)
    u, z = [v.astype(np.float64).reshape(N, 8, T, K) for v in (uu, zz)]
    c = np.stack([gentries(v) for v in ce]).astype(np.int64); pairs = np.stack([gentries(v) for v in rp]).astype(np.int64).reshape(N, 8, T - 1, R)
    w = np.ones((N, 8, 16, K)); tally = np.zeros((N, 8, 16, K))
    qi = np.arange(N)[:, None, None]; gi = np.arange(8)[None, :, None]; slot = np.arange(K)[None, None, :]; hero = slot % 16
    for t in range(T):
        p = np.minimum(np.floor(u[:, :, t] * m[qi, gi, hero, c]), 15).astype(np.int64)
        d = (c + x[qi, gi, p, c]) & (W - 1); dd = d[:, :, None, :]
        rho = np.take_along_axis(s, dd, 3) * np.take_along_axis(m, dd, 3)
        real = 256 * rho[qi, gi, hero, slot] > z[:, :, t]
        w = np.clip(w * np.where(real[:, :, None, :], 2 * np.take_along_axis(a, dd, 3) * rho, 2 * np.maximum(1 - rho, 0)), 0.125, 4.0)
        tally = tally + w
        if t < T - 1:
            e = (2 * pairs[:, :, t] + (d[..., LO:LO + R] & 1))[:, :, None, :]; old = np.take_along_axis(m, e, 3)
            np.put_along_axis(m, e, np.where(rho[..., LO:LO + R] > 1, np.maximum(old * 0.5, 0.0625), old), 3)
        c = np.where(real, d ^ 1, d)
        if t < T - 1 and (t + 1) % S == 0: c, w, tally, u, z = [move(v, 1) for v in (c, w, tally, u, z)]
    return {"tl": move(tally, -(B - 1)).reshape(N, 128, K).astype(np.float32)}

def check_inputs(d):
    bad = list(check_ranges(d))
    if not bad:
        for name, y in reference(**d).items():
            for q in range(N):
                v = np.abs(np.asarray(y[q], np.float64)); s = np.sqrt(np.mean(v * v))
                if v.max() > 7 * s or s < 2.0 ** 0: bad.append('%s of rank %d is uneven or too small' % (name, q))
    return bad

@@ -1,0 +1,367 @@
+import math
+from concourse.bass import DstId, RemoteDMATransfer
+from concourse.mybir import AluOpType as OP, ActivationFunctionType as AF
+
+W = 2048; H = 1024; Q = 512; NR = 8; HOP = 3; LO = 640; R = 768
+CM = 2.1689453125
+QS = 0.13548188464186972
+CFG = {"ps": (1, 2, 3), "fs": (1, 2), "tl": "pr1", "kb": (4, 5, 4, 5), "pb0": (2, 3, 0, 1),
+       "first": "a0 a1 a2 e0 e1 e2 e3 p0 V0 V1 V2 V3 p1 b0 a3 K0 K1 p2 x0 k0 k1 b1 p3 K2 K3 b2 b3 c0 c1 w0 l0 k2 k3 z0 c2 s0 d0 c3 w1",
+       "ord0": "u0 u1 a0 p0 a1 p1 b0 u2 a2 b1 F F F F c0 p2 u3 c1 a3 w0 p3 b2 b3 s0 d0 c2 c3 w1 F s1 d1 h0 h1",
+       "ord1": "u0 u1 a0 p0 a1 p1 b0 u2 a2 b1 F F F F F F c0 p2 u3 c1 a3 p3 w0 b2 b3 c2 s0 d0 c3 w1 F s1 d1 h0 h1",
+       "ord2": "u0 u1 a0 p0 a1 p1 b0 u2 a2 b1 F F F F F F c0 p2 u3 c1 a3 p3 w0 b2 b3 c2 s0 d0 c3 w1 F s1 d1 h0 h1"}
+
+SCRATCH = {
+    "io": ("sbuf", [128, 528], "int32"), "ia": ("sbuf", [128, 528], "int32"),
+    "gw": ("sbuf", [128, 176], "bfloat16"), "rm": ("sbuf", [128, 16], "float32"),
+    "iw": ("sbuf", [128, 144], "float32"), "zw": ("sbuf", [128, 192], "bfloat16"),
+    "bw": ("sbuf", [128, 16, 176], "bfloat16"), "dd": ("sbuf", [128, 16, 128], "bfloat16"),
+    "ib": ("sbuf", [128, 128], "bfloat16"), "nb": ("sbuf", [128, 128], "bfloat16"), "em": ("sbuf", [128, 128], "bfloat16"),
+    "az": ("sbuf", [128, 144], "float16"), "qa": ("sbuf", [128, 4], "float32"), "lq": ("sbuf", [128, 4], "float32"),
+    "cei": ("sbuf", [128, 128], "int32"), "rpi": ("sbuf", [128, 144], "int32"), "rp2": ("sbuf", [128, 144], "int32"),
+    "ut": ("sbuf", [128, 512], "bfloat16"), "lu": ("sbuf", [128, 512], "float32"),
+    "z8": ("sbuf", [8, 8192], "bfloat16"), "zo": ("sbuf", [128, 512], "bfloat16"),
+    "mt": ("sbuf", [128, W], "bfloat16"), "nt": ("sbuf", [128, W], "bfloat16"), "st": ("sbuf", [128, W], "bfloat16"),
+    "at": ("sbuf", [128, W + 16], "bfloat16"), "et": ("sbuf", [128, W], "float32"), "rt": ("sbuf", [128, W], "bfloat16"),
+    "lg": ("sbuf", [128, W], "bfloat16"), "sb": ("sbuf", [128, W], "bfloat16"),
+    "pr": ("sbuf", [128, W], "float16"), "ag": ("sbuf", [128, W], "bfloat16"),
+    "rg0": ("sbuf", [128, W], "bfloat16"), "rg1": ("sbuf", [128, W], "bfloat16"),
+    "c2": ("sbuf", [128, 128], "float32"), "ci": ("sbuf", [128, 128], "int32"), "cm": ("sbuf", [128, 128], "int32"),
+    "du": ("sbuf", [128, 128], "uint16"), "par": ("sbuf", [128, 128], "int32"), "lo": ("sbuf", [128, 128], "float32"),
+    "ei": ("sbuf", [128, 48], "int32"), "eu": ("sbuf", [128, 48], "uint16"),
+    "nl0": ("sbuf", [128, 128], "bfloat16"), "nl1": ("sbuf", [128, 128], "bfloat16"), "sn": ("sbuf", [128, 128], "bfloat16"),
+    "n2k": ("sbuf", [128, 128], "float32"), "xx": ("sbuf", [128, 128], "float32"),
+    "ixf": ("sbuf", [128, 128], "float32"), "ix": ("sbuf", [128, 128], "uint16"),
+    "fac": ("sbuf", [128, R], "float32"), "mn": ("sbuf", [128, R], "float32"), "mlo": ("sbuf", [128, R], "float32"),
+    "fsn": ("sbuf", [128, R], "bfloat16"), "lm": ("sbuf", [128, W], "float32"), "ls": ("sbuf", [128, W], "float32"),
+    "ta": ("sbuf", [128, W], "float32"), "fl": ("sbuf", [128, H], "float32"),
+    "td": ("dram", [128, H], "float32"), "fd": ("dram", [2, 128, Q], "float32"),
+}
+for _t in range(4):
+    SCRATCH["uh%d" % _t] = ("sbuf", [128, 1024], "bfloat16")
+    SCRATCH["cu%d" % _t] = ("sbuf", [128, 128], "uint16")
+    SCRATCH["wo%d" % _t] = ("sbuf", [128, W], "float32")
+    if _t:
+        SCRATCH["zl%d" % _t] = ("sbuf", [128, 128], "bfloat16")
+        SCRATCH["cs%d" % _t] = ("sbuf", [128, 128], "uint16")
+        SCRATCH["wi%d" % _t] = ("sbuf", [128, W], "float32")
+        SCRATCH["lr%d" % _t] = ("sbuf", [128, W], "float32")
+        SCRATCH["wd%d" % _t] = ("dram", [128, H], "float32")
+for _b in range(8):
+    SCRATCH["b%d" % _b] = ("psum", [128, Q], "float32")
+
+SEMAPHORES = (["eV", "eS", "eP", "eG", "sent", "outs", "accU", "accL", "aTU", "aTL", "rT"]
+              + ["l_" + n for n in ("ce", "uu", "mj", "nx", "sg", "zz", "al", "rp")]
+              + ["%s%d" % (n, t) for n in ("aU", "aZ", "aC", "aWU", "aWL", "rW", "cL", "sL") for t in (1, 2, 3)]
+              + ["aF%d" % q for q in range(4)])
+
+
+def rank_program(g, core, T, topo):
+    rank = T.rank_of(core)
+    if rank is None:
+        return
+    qs = {"V": g.vector, "S": g.scalar, "P": g.tensor, "G": g, "Y": g.sync}
+    cnt = {}
+    waited = {e: {} for e in qs}
+    wr = {}; rd = {}
+
+    def wait(e, tok):
+        s, v = tok
+        if s == "eP" and e == "P":
+            return
+        if waited[e].get(s, 0) < v:
+            qs[e].wait_ge(T.sem[s], v); waited[e][s] = v
+
+    def deps(e, reads, writes):
+        need = {}
+        def add(tok):
+            need[tok[0]] = max(need.get(tok[0], 0), tok[1])
+        for k in reads:
+            if k in wr: add(wr[k])
+            if k[0] == "b" and len(k) == 2:
+                for tok in rd.get(k, []):
+                    if tok[0] != "e" + e: add(tok)
+        for k in writes:
+            if k in wr: add(wr[k])
+            for tok in rd.get(k, []): add(tok)
+        for s in need: wait(e, (s, need[s]))
+
+    def mark(tok, reads, writes):
+        for k in reads: rd.setdefault(k, []).append(tok)
+        for k in writes:
+            wr[k] = tok; rd[k] = []
+
+    def op(e, reads, writes, fn):
+        deps(e, reads, writes)
+        s = "e" + e; cnt[s] = cnt.get(s, 0) + 1
+        fn().then_inc(T.sem[s], 1)
+        mark((s, cnt[s]), reads, writes)
+
+    def dmas(e, sem, reads, writes, pairs, **kw):
+        deps(e, reads, writes)
+        for o, i in pairs:
+            qs[e].dma_start(o, i, **kw).then_inc(T.sem[sem], 16)
+            cnt[sem] = cnt.get(sem, 0) + 16
+        mark((sem, cnt[sem]), reads, writes)
+
+    def arrive(sem, key):
+        cnt[sem] = 16; wr[key] = (sem, 16); rd[key] = []
+
+    def send(hops, sem, reads, dst, srcs):
+        to = T.cores[(rank + hops) % NR]
+        rid, pid, _ = topo.addr(to)
+        m = topo.mask(core, to)
+        deps("G", reads, [])
+        if len(srcs) == 1:
+            g.remote_dma(dst, srcs[0], T.sem[sem], T.sem.sent, pid, rid, m)
+        else:
+            g.remote_dma_fused([RemoteDMATransfer(dst_ids=[DstId(rid=rid, pnc=pid)], dma_engine_mask=m, remote_sem=T.sem[sem],
+                                                  srcs=srcs, dsts=[dst], alu_op=1)], local_sem=T.sem.sent)
+        cnt["sent"] = cnt.get("sent", 0) + len(topo.engines(core, to))
+
+    V = g.vector; S = g.scalar; P = g.tensor
+    def ts(o, i, a, b, o0, o1, r, w):
+        if o1 is None: op("V", r, w, lambda: V.tensor_scalar(o, i, a, None, o0))
+        else: op("V", r, w, lambda: V.tensor_scalar(o, i, a, b, o0, o1))
+    def tt(o, a, b, o0, r, w): op("V", r, w, lambda: V.tensor_tensor(o, a, b, o0))
+    def cp(o, i, r, w): op("V", r, w, lambda: V.tensor_copy(o, i))
+    def act(o, i, f, r, w, **kw): op("S", r, w, lambda: S.activation(o, i, f, **kw))
+    def mm(o, l, x, a, z, r, w): op("P", r, w, lambda: P.matmul(o, l, x, a, z))
+    def B(b): return T["b%d" % b]
+    def qc(q): return slice(Q * q, Q * q + Q)
+    def ql(q): return slice(32 * q, 32 * q + 32)
+    def allq(n): return [n + str(q) for q in range(4)]
+    def hq(n, h): return [n + str(2 * h), n + str(2 * h + 1)]
+    PS = CFG["ps"]; PB = [2, 3, 2, 3]
+
+    for t in (1, 2, 3):
+        arrive("aU%d" % t, "uh%d" % t); arrive("aZ%d" % t, "zl%d" % t); arrive("aC%d" % t, "cu%d" % t)
+        arrive("aWU%d" % t, "wd%d" % t); arrive("aWL%d" % t, "wiL%d" % t)
+    arrive("aTU", "td"); arrive("aTL", "taL")
+    for q in range(4): arrive("aF%d" % q, "f%d" % q)
+
+    dmas("Y", "l_ce", [], ["cei"], [(T.cei[:], T.ce[:])])
+    dmas("S", "l_uu", [], ["ut"], [(T.ut[:], T.uu[:])])
+    dmas("Y", "l_mj", [], ["mt"], [(T.mt[:], T.mj[:])])
+    dmas("Y", "l_nx", [], ["nt"], [(T.nt[:], T.nx[:])])
+    dmas("Y", "l_sg", [], ["st"], [(T.st[:], T.sg[:])])
+    dmas("Y", "l_zz", [], ["z8"], [(T.z8[:], T.zz[:])])
+    dmas("Y", "l_al", [], ["at"], [(T.at[:, 0:W], T.al[:])])
+    dmas("Y", "l_rp", [], ["rpi"], [(T.rpi[:], T.rp[:])])
+
+    IO = T["io"]
+    op("G", [], ["io2"], lambda: g.iota(IO[:, 512:528], [[-1, 16]], 16, 1))
+    op("G", [], ["io1"], lambda: g.iota(IO[:, 0:176], [[-16, 11], [0, 16]], 48 + 128, 1))
+    op("G", [], ["io3"], lambda: g.iota(IO[:, 176:320], [[1, 144]], 256 - 16, -1))
+    op("V", [], ["dd"], lambda: V.memset(T.dd[:, 0:8, :], 1.0))
+    op("G", ["dd"], ["bw%d" % s for s in range(8, 16)],
+       lambda: g.affine_select(T.bw[:, 8:16, 48:176], T.dd[:, 0:8, :], [[-1, 8], [-16, 8], [0, 16]], OP.is_equal, 0.0, -8, 1))
+    op("G", [], ["io4"], lambda: g.iota(IO[:, 320:512], [[1, 192]], 2048 + 128 - 63, -16))
+    op("G", ["dd"], ["bwx"],
+       lambda: g.affine_select(T.bw[:, 8:16, 0:48], T.dd[:, 0:8, 0:48], [[-1, 8], [-16, 3], [0, 16]], OP.is_equal, 0.0, -88, 1))
+    ts(T.ia[:, 512:528], IO[:, 512:528], 15, None, OP.bitwise_and, None, ["io2"], ["ia2"])
+    ts(T.qa[:, 0:1], T.ia[:, 512:513], -1.0 / 32, 1e-17, OP.add, OP.max, ["ia2"], ["qa"])
+    act(T.lq[:, 0:1], T.qa[:, 0:1], AF.Ln, ["qa"], ["lq"], scale=QS)
+    ts(T.ia[:, 0:176], IO[:, 0:176], 127, None, OP.bitwise_and, None, ["io1"], ["ia1"])
+    ts(T.rm[:], T.ia[:, 512:528], 0.0, None, OP.is_equal, None, ["ia2"], ["rm"])
+    ts(T.gw[:], T.ia[:, 0:176], 16.0, None, OP.is_lt, None, ["ia1"], ["gw"])
+    ts(T.ia[:, 176:320], IO[:, 176:320], 127, None, OP.bitwise_and, None, ["io3"], ["ia3"])
+    def bw_(s): ts(T.bw[:, s, :], T.gw[:], T.rm[:, s:s + 1], None, OP.mult, None, ["gw", "rm"], ["bw%d" % s])
+    ts(T.iw[:], T.ia[:, 176:320], 0.0, None, OP.is_equal, None, ["ia3"], ["iw"])
+    bw_(0)
+    tt(T.em[:], T.iw[:, 16:144], T.iw[:, 15:143], OP.subtract, ["iw"], ["em"])
+    bw_(1)
+    cp(T.cu0[:], T.cei[:], ["cei"], ["cu0"])
+    tt(T.em[:, 0:128:16], T.iw[:, 16:144:16], T.iw[:, 31:144:16], OP.add, ["iw"], ["em"])
+    for s in range(2, 8): bw_(s)
+    BW = ["bw%d" % s for s in range(16)]
+    op("G", BW, ["dd"], lambda: g.affine_select(T.dd[:], T.bw[:, :, 48:176], [[0, 16], [-1, 128]], OP.is_equal, 0.0, 0, 1))
+    act(T.lu[:], T.ut[:], AF.Ln, ["ut"], ["lu"], scale=1.0 / 16, bias=1e-5)
+    act(T.uh0[:, 0:512], T.lu[:], AF.Copy, ["lu"], ["uhi"])
+    cp(T.ib[:], T.iw[:, 16:144], ["iw"], ["ib"])
+    tt(T.uh0[:, 512:1024], T.lu[:], T.uh0[:, 0:512], OP.subtract, ["lu", "uhi"], ["uh0"])
+
+    def a_(t, q):
+        o = T["cu%d" % t][:, ql(q)]
+        if t == 0: act(T.lg[:, qc(q)], T.mt[:].indirect(o), AF.Ln, ["mt", "cu0"], ["lg%d" % q], scale=CM)
+        else: act(T.lg[:, qc(q)], T.lm[:].indirect(o), AF.Identity, ["lm", "cu%d" % t], ["lg%d" % q], bias=math.log(CM))
+    def pu(t, q, a, z):
+        b = PB[q]; o = 48 - (16 * t if q >= 2 else 0)
+        for j in range(2):
+            mm(B(b)[:], T.bw[:, 4 * t + q, o:o + 128], T["uh%d" % t][:, qc(j)], a and j == 0, z and j == 1,
+               ["uh%d" % t, "uhi", "bw%d" % (4 * t + q)] + (["bwx"] if t else []), ["b%d" % b])
+    def ps(t, q):
+        b = PB[q]
+        for i in range(16):
+            mm(B(b)[:, i:Q:16], T.bw[:, i, 48:176], T.lg[:, Q * q + i:Q * q + Q:16], t == 0 and i == 0, t > 0 and i == 15,
+               ["bw%d" % i, "lg%d" % q], ["b%d" % b])
+    def p1(t, q): ps(t, q); pu(t, q, False, True)
+    def b_(t, q):
+        act(T.sb[:, qc(q)], B(PB[q])[:], AF.Sign, ["b%d" % PB[q], "lq"], ["sb%d" % q], scale=-1.0, bias=T.lq[:, 0:1])
+    def c_(t, q):
+        tt(T.pr[:, qc(q)], T.et[:].indirect(T["cu%d" % t][:, ql(q)]), T.sb[:, qc(q)], OP.mult, allq("et") + ["cu%d" % t, "sb%d" % q], ["pr%d" % q])
+    def c2_(t): ts(T.c2[:], T["cu%d" % t][:], 2048.0, None, OP.add, None, ["cu%d" % t], ["c2"])
+    def way(h):
+        for i in range(16):
+            mm(B(6 + h)[:, 128:192], T.az[:, 15 - i:143 - i], T.pr[:, H * h + i:H * h + H:16], i == 0, i == 15, ["az"] + hq("pr", h), ["b%d" % (6 + h)])
+    def sm(h):
+        c = slice(64 * h, 64 * h + 64)
+        tt(T.ci[:, c], B(6 + h)[:, 128:192], T.c2[:, c], OP.add, ["b%d" % (6 + h), "c2"], ["ci%d" % h])
+        ts(T.cm[:, c], T.ci[:, c], W - 1, None, OP.bitwise_and, None, ["ci%d" % h], ["cm%d" % h])
+        cp(T.du[:, c], T.cm[:, c], ["cm%d" % h], ["du%d" % h])
+    def d_(t, h):
+        n = "rg%d" % (t % 2); o = T.du[:, 64 * h:64 * h + 64]
+        if t == 0: act(T[n][:, H * h:H * h + H], T.rt[:].indirect(o), AF.Copy, allq("rt") + ["du%d" % h], hq(n, h))
+        else: act(T[n][:, H * h:H * h + H], T["lr%d" % t][:].indirect(o), AF.Exp, ["lr%d" % t, "du%d" % h], hq(n, h))
+    def hero(t, h):
+        n = "rg%d" % (t % 2); c = slice(64 * h, 64 * h + 64)
+        zl = T.zo[:, c] if t == 0 else T["zl%d" % t][:, c]
+        mm(B(6)[:, c], T.nb[:], zl, True, False, ["nb", "zl%d" % t], ["b6"])
+        for i in range(16):
+            mm(B(6)[:, c], T.dd[:, i, :], T[n][:, H * h + i:H * h + H:16], False, i == 15, ["dd"] + hq(n, h), ["b6"])
+    def lists(t):
+        ts(T.par[:], T.cm[:], 1, None, OP.bitwise_and, None, ["cm0", "cm1"], ["par"])
+        tt(T.ei[:], T.par[:, 40:88], T.rp2[:, 48 * t:48 * t + 48], OP.add, ["par", "rp2"], ["ei"])
+        tt(T.lo[:], T.cm[:], T.par[:], OP.subtract, ["cm0", "cm1", "par"], ["lo"])
+        cp(T.eu[:], T.ei[:], ["ei"], ["eu"])
+    def post(t):
+        n = "nl%d" % (t % 2); th = 1.0 / 512
+        if t in PS:
+            act(T.sn[:], B(6)[:, 0:128], AF.Sign, ["b6"], ["sn"], scale=-1.0, bias=th)
+            act(T[n][:], T.sn[:], AF.Relu, ["sn"], [n])
+            act(T.n2k[:], T.sn[:], AF.Relu, ["sn"], ["n2k"], scale=float(W))
+        else:
+            ts(T[n][:], B(6)[:, 0:128], th, None, OP.is_le, None, ["b6"], [n])
+            ts(T.n2k[:], B(6)[:, 0:128], th, float(W), OP.is_le, OP.mult, ["b6"], ["n2k"])
+        if t in CFG["fs"]: act(T.fac[:], T.fsn[:], AF.Relu, ["fsn"], ["fac"], scale=math.log(2.0))
+        if t < 3:
+            tt(T.xx[:], T.par[:], T[n][:], OP.is_equal, ["par", n], ["xx"])
+            for h in range(2):
+                c = slice(64 * h, 64 * h + 64); o = B(7)[:, 256 + 64 * h:320 + 64 * h]
+                l = T.iw[:, 0:128] if h else T.iw[:, 16:144]
+                mm(o, l, T.lo[:, c], True, False, ["iw", "lo"], ["b7"])
+                mm(o, l, T.xx[:, c], False, True, ["xx"], ["b7"])
+        tt(T.ixf[:], T.cm[:], T.n2k[:], OP.max, ["cm0", "cm1", "n2k"], ["ixf"])
+        cp(T.ix[:], T.ixf[:], ["ixf"], ["ix"])
+        if t < 3:
+            s = "cs%d" % (t + 1)
+            cp(T[s][:], B(7)[:, 256:384], ["b7"], [s])
+            send(HOP, "aC%d" % (t + 1), [s], T["cu%d" % (t + 1)][:], [T[s][:]])
+    def rn(t, q, b):
+        n = "rg%d" % (t % 2); m = "nl%d" % (t % 2); k = "b%d" % b
+        mm(B(b)[:], T.nb[:], T[n][:, qc(q)], True, False, ["nb", n + str(q)], [k])
+        for i in range(16):
+            mm(B(b)[:, i:Q:16], T.bw[:, i, 48:176], T[m][:, ql(q)], False, i == 15, [m], [k])
+    def fg(h):
+        act(T.ag[:, H * h:H * h + H], T.at[:].indirect(T.ix[:, 64 * h:64 * h + 64]), AF.Copy, ["at", "atx", "ix"], hq("ag", h), scale=-2.0)
+    def fq(q):
+        act(T.ag[:, qc(q)], T.at[:].indirect(T.ix[:, ql(q)]), AF.Copy, ["at", "atx", "ix"], ["ag%d" % q], scale=-2.0)
+    def e_(t, q, b):
+        if t: tt(B(b)[:], T["wi%d" % t][:, qc(q)], B(b)[:], OP.mult, ["wi%s%d" % ("U" if q >= 2 else "L", t)], ["b%d" % b])
+    def f_(q, b): tt(B(b)[:], T.ag[:, qc(q)], B(b)[:], OP.mult, ["ag%d" % q], ["b%d" % b])
+    def g_(t, q, b): ts(T["wo%d" % t][:, qc(q)], B(b)[:], 0.125, 4.0, OP.max, OP.min, ["b%d" % b], ["wo%d_%d" % (t, q)])
+    def fac(t):
+        n = "rg%d" % (t % 2)
+        if t in CFG["fs"]: act(T.fsn[:], T[n][:, LO:LO + R], AF.Sign, [n + "1", n + "2"], ["fsn"], bias=-1.0625)
+        else: ts(T.fac[:], T[n][:, LO:LO + R], 1.0, math.log(2.0), OP.is_gt, OP.mult, [n + "1", n + "2"], ["fac"])
+    def reports(t):
+        tt(T.mn[:], T.lm[:].indirect(T.eu[:]), T.fac[:], OP.subtract, ["lm", "eu", "fac"], ["mn"])
+        tt(T.lm[:].indirect(T.eu[:]), T.mn[:], T.mlo[:], OP.max, ["eu", "mn", "mlo"], ["lm"])
+        k = "lr%d" % (t + 1)
+        dmas("G", "sL%d" % (t + 1), ["lm"], [k], [(T[k][:], T.lm[:])], accum_op=OP.add)
+    def kp(q, b): mm(B(b)[:], T.ib[:], T.mt[:, qc(q)], True, True, ["ib", "mt"], ["b%d" % b])
+    def k_(q, b): tt(T.rt[:, qc(q)], T.st[:, qc(q)], B(b)[:], OP.mult, ["st", "b%d" % b], ["rt%d" % q])
+    def zl_(t):
+        for h in range(2):
+            for i in range(16):
+                o = 63 - (16 * t if h else 0) - i; c0 = W * t + H * h
+                mm(B(7)[:, 384 + 64 * h:448 + 64 * h], T.zw[0:8, o:o + 128], T.z8[0:8, c0 + i:c0 + H:16], i == 0, i == 15, ["zw", "z8"], ["b7"])
+        act(T.zo[:, 128 * t:128 * t + 128], B(7)[:, 384:512], AF.Copy, ["b7"], ["zo%d" % t if t else "zl0"], scale=1.0 / 256)
+    def turn(dst, src, n, sem, rk, wk):
+        dmas("Y", sem, [rk], [wk], [(dst[16 * n:128, H:W], src[0:128 - 16 * n, :]), (dst[0:16 * n, H:W], src[128 - 16 * n:128, :])])
+    def send_w(t, h):
+        wo = T["wo%d" % t]; c = slice(H * h, H * h + H); ks = ["wo%d_%d" % (t, 2 * h), "wo%d_%d" % (t, 2 * h + 1)]
+        if h:
+            send(HOP, "aWU%d" % (t + 1), ks, T["wd%d" % (t + 1)][:], [wo[:, c]])
+            turn(T["wi%d" % (t + 1)], T["wd%d" % (t + 1)], 1, "rW%d" % (t + 1), "wd%d" % (t + 1), "wiU%d" % (t + 1))
+        else:
+            send(HOP, "aWL%d" % (t + 1), ks, T["wi%d" % (t + 1)][:, c], [wo[:, c]])
+    def send_t(h):
+        c = slice(H * h, H * h + H); ks = ["wo1_%d" % (2 * h), "wo1_%d" % (2 * h + 1)]
+        if h:
+            send(2 * HOP, "aTU", ks + ["wiU1"], T.td[:], [T.wo1[:, c], T.wi1[:, c]])
+            turn(T.ta, T.td, 2, "rT", "td", "taU")
+        else:
+            send(2 * HOP, "aTL", ks + ["wiL1", CFG["tl"]], T.ta[:, c], [T.wo1[:, c], T.wi1[:, c]])
+    def fill(t): dmas("Y", "cL%d" % t, ["ls"], ["lr%d" % t], [(T["lr%d" % t][:], T.ls[:])])
+
+    def ep(q, b): mm(B(b)[:], T.em[:], T.nt[:, qc(q)], True, True, ["em", "nt"], ["b%d" % b])
+    KB = CFG["kb"]
+    def consts():
+        ts(T.az[:], T.iw[:], 0.0, None, OP.mult, None, ["iw"], ["az"])
+        ts(T.ia[:, 320:512], IO[:, 320:512], 127, None, OP.bitwise_and, None, ["io4"], ["ia4"])
+        ts(T.zw[:], T.ia[:, 320:512], 0.0, None, OP.is_equal, None, ["ia4"], ["zw"])
+        ts(T.az[:, 15:143:16], T.gw[:, 48:176:16], -0.5, None, OP.mult, None, ["gw"], ["az"])
+        c2_(0)
+    def lns():
+        act(T.ls[:], T.st[:], AF.Ln, ["st"], ["ls"], bias=1e-18)
+        fill(1); fill(2); fill(3)
+    PB[:] = CFG["pb0"]
+    for x in CFG["first"].split():
+        k = int(x[1])
+        {"a": lambda: a_(0, k), "p": lambda: p1(0, k), "b": lambda: b_(0, k), "c": lambda: c_(0, k), "w": lambda: way(k), "s": lambda: sm(k),
+         "d": lambda: d_(0, k), "e": lambda: ep(k, 4 + k), "K": lambda: kp(k, KB[k]), "k": lambda: k_(k, KB[k]), "x": consts, "l": lns, "z": lambda: zl_(0),
+         "S": lambda: act(T.et[:, qc(k)], B(4 + k)[:], AF.Copy, ["b%d" % (4 + k)], ["et%d" % k]),
+         "V": lambda: cp(T.et[:, qc(k)], B(4 + k)[:], ["b%d" % (4 + k)], ["et%d" % k])}[x[0]]()
+    PB[:] = (2, 3, 2, 3)
+    for t in (1, 2, 3): send(HOP * t, "aU%d" % t, ["uh0"], T["uh%d" % t][:], [T.uh0[:]])
+    ts(T.nb[:], T.iw[:, 16:144], -1.0, None, OP.mult, None, ["iw"], ["nb"])
+    ts(T.rp2[:], T.rpi[:], 2.0, None, OP.mult, None, ["rpi"], ["rp2"])
+    sm(1); d_(0, 1); lists(0)
+    op("V", [], ["atx"], lambda: V.memset(T.at[:, W:W + 16], -1.0))
+    op("V", [], ["mlo"], lambda: V.memset(T.mlo[:], math.log(0.0625)))
+    act(T.lm[:], T.mt[:], AF.Ln, ["mt"], ["lm"])
+    hero(0, 0); hero(0, 1); fac(0)
+
+    for t in range(3):
+        n = t + 1
+        post(t)
+        if t:
+            send_w(t - 1, 0)
+        fg(1); rn(t, 2, 0); zl_(n); rn(t, 3, 1); rn(t, 0, 4); rn(t, 1, 5); fg(0)
+        send(HOP * n, "aZ%d" % n, ["zo%d" % n], T["zl%d" % n][:], [T.zo[:, 128 * n:128 * n + 128]])
+        reports(t)
+        def up():
+            send_w(t, 1)
+            if t == 1: send_t(1)
+        rest = [lambda: e_(t, 2, 0), lambda: e_(t, 3, 1), lambda: f_(2, 0), lambda: f_(3, 1), lambda: g_(t, 2, 0), lambda: (g_(t, 3, 1), up()),
+                lambda: e_(t, 0, 4), lambda: e_(t, 1, 5), lambda: f_(0, 4), lambda: f_(1, 5), lambda: g_(t, 0, 4), lambda: g_(t, 1, 5)]
+        if t == 0: rest = rest[2:6] + rest[8:]
+        c2_(n)
+        for x in CFG["ord%d" % t].split():
+            if x == "F": rest.pop(0)()
+            else:
+                k = int(x[1])
+                {"a": lambda: a_(n, k), "u": lambda: pu(n, k, True, False), "p": lambda: ps(n, k), "b": lambda: b_(n, k), "c": lambda: c_(n, k),
+                 "w": lambda: way(k), "s": lambda: sm(k), "d": lambda: d_(n, k), "h": lambda: hero(n, k)}[x[0]]()
+        for fn in rest: fn()
+        if n < 3: lists(n); fac(n)
+
+    send_t(0); send_w(2, 0)
+    post(3)
+    dmas("G", "accU", ["wiU3"], ["taU"], [(T.ta[:, H:W], T.wi3[:, H:W])], accum_op=OP.add)
+    dmas("G", "accL", ["wiL3"], ["taL"], [(T.ta[:, 0:H], T.wi3[:, 0:H])], accum_op=OP.add)
+    bank = {2: 4, 3: 5, 0: 0, 1: 1}
+    for q in (2, 3, 0, 1):
+        rn(3, q, bank[q]); fq(q)
+    def home(q):
+        dst = T.fd[q - 2] if q >= 2 else T.fl[:, qc(q)]
+        send(-3 * HOP, "aF%d" % q, ["wo3_%d" % q, "taU" if q >= 2 else "taL"], dst, [T.wo3[:, qc(q)], T.ta[:, qc(q)]])
+    for a, b in ((2, 3), (0, 1)):
+        e_(3, a, bank[a]); e_(3, b, bank[b]); f_(a, bank[a]); f_(b, bank[b])
+        g_(3, a, bank[a]); home(a); g_(3, b, bank[b]); home(b)
+    for q in (2, 3):
+        dmas("Y", "outs", ["f%d" % q], [], [(T.tl[0:80, qc(q)], T.fd[q - 2, 48:128, :]), (T.tl[80:128, qc(q)], T.fd[q - 2, 0:48, :])])
+    dmas("S", "outs", ["f0"], [], [(T.tl[:, qc(0)], T.fl[:, qc(0)])])
+    dmas("Y", "outs", ["f1"], [], [(T.tl[:, qc(1)], T.fl[:, qc(1)])])
+    for s in cnt: wait("G", (s, cnt[s]))

@@ -2,366 +2,509 @@ import math
 from concourse.bass import DstId, RemoteDMATransfer
 from concourse.mybir import AluOpType as OP, ActivationFunctionType as AF
 
-W = 2048; H = 1024; Q = 512; NR = 8; HOP = 3; LO = 640; R = 768
-CM = 2.1689453125
-QS = 0.13548188464186972
-CFG = {"ps": (1, 2, 3), "fs": (1, 2), "tl": "pr1", "kb": (4, 5, 4, 5), "pb0": (2, 3, 0, 1),
-       "first": "a0 a1 a2 e0 e1 e2 e3 p0 V0 V1 V2 V3 p1 b0 a3 K0 K1 p2 x0 k0 k1 b1 p3 K2 K3 b2 b3 c0 c1 w0 l0 k2 k3 z0 c2 s0 d0 c3 w1",
-       "ord0": "u0 u1 a0 p0 a1 p1 b0 u2 a2 b1 F F F F c0 p2 u3 c1 a3 w0 p3 b2 b3 s0 d0 c2 c3 w1 F s1 d1 h0 h1",
-       "ord1": "u0 u1 a0 p0 a1 p1 b0 u2 a2 b1 F F F F F F c0 p2 u3 c1 a3 p3 w0 b2 b3 c2 s0 d0 c3 w1 F s1 d1 h0 h1",
-       "ord2": "u0 u1 a0 p0 a1 p1 b0 u2 a2 b1 F F F F F F c0 p2 u3 c1 a3 p3 w0 b2 b3 c2 s0 d0 c3 w1 F s1 d1 h0 h1"}
+W = 2048; NR = 8; HOP = 3; R = 768
+ROT = 32
+U0 = 32; U1 = 96
+R0 = 8
+PK = 64 + 1024
+LN2H = 0.693359375
+H2 = [(0, 64), (64, 128)]
+CFG = {
+    "cp": H2,
+    "gp": {},
+    "rp": [(8, 56)], "sp": [(8, 24), (24, 40), (40, 56)],
+    "wp": [(0, 32), (32, 64), (64, 96), (96, 128)],
+    "fp": [(0, 32), (32, 64), (64, 96), (96, 120), (120, 128)],
+    "send": [H2, H2, H2], "tp": H2, "home": [(0, 64), (64, 96), (96, 120), (120, 128)],
+    "tm": "f2", "lo": "zns", "nadd": 1, "dv": 12, "fine": "uRklsi",
+    "sg": ["0123", "12", "12", "123"],
+    "vg": ["a0 c0", "", "", ""],
+    "after": {"al1": "ft", "al2": "lr3", "al3": "fac0", "f2": "lr1_0"},
+    "pc": -25, "pr": 12, "pw": 115, "ps": 100, "pu": [-5, 35, 60], "pt": 50, "pl": 8, "pn": 14,
+    "cyc": 0.85e-3, "pe": 0.43e-3, "ga": 1.56, "sc": 3.8, "wake": 0.08, "fix": 2.2, "bw": 550e3, "fixv": 0.05, "fixs": 0.07, "gdma": 1.5, "gis": 0.8, "rbw": 450e3,
+    "win": 0.05, "al": 0.2, "lead": 0.3,
+    "ord": {
+        "V": ["a0 s0 s1 s1c s1b s0c s0b o1 o0 c0 K0 z0 K2 z1 K1 i1 i0 K3 i0b i0c l0 l0b l0c l1 i1b l0d l1b i1c r0 m0 x0 S0 t0 x1 S1 t1 S2 f0 f1 k0 k1 v1+ f2 v0+",
+              "s0 s0b s0c f3' o0 k3' s1 s1b s1c o1 k2' z0 i0 i0b i0c l0 z1 l0d l0b i1 l0c i1b l1 i1c r0 l1b m0 x0 S0 t0 x1 S1 t1 S2 e0 e1 f0 f1 k0 v0+ k1",
+              "s0 s0b s0c e2' v1 o0 e3' s1 s1c s1b f3' o1 f2' z0 k2' i0 i0b l0 i0c k3' z1 l0b l0d i1 l0c i1b i1c r0 l1 m0 l1b x0 S0 t0 x1 S1 t1 S2 e0 e2 f0 f2 k0 v0+ k2",
+              "s0 v1 s0b s0c e1' o0 f1' s1 s1c s1b k1' o1 e3' z0 i0 i0b i0c l0 z1 i1 i1b i1c l1 f3' l0b l1b k3' x0 t0 x1 e0 e1 t1 f0 f1 k0 k1 e2 f2 e3 k2 f3 k3 f3x k3x"],
+        "S": ["M0 a1 u1 u1b M1 c1 N1 N0 u1b+ u1+ E0 d0 d1 g0 u1b++ u1++ g1 A0 A1 A2 A3", "a0 a1 c0 c1 d0 d1 g0 u1b++ u1++ g1 A2 A1",
+              "a0 a1 c0 c1 d0 d1 g0 g1 A1 A2", "a0 a1 c0 c1 d0 d1 g0 g1 A1 A2 A3"],
+        "P": ["K0 K1 u0 K3 u0b u0c u0d h0 K2 h1 u0+ o1 o0 u0b+ q1 u0c+ q0 y0 y1 u0d+ z1 z0 u0++ u0b++ u0c++ u0d++ g0 R1 R0 g1 x0 R2 x1 R1b R0b R2b R3 u0+++ u0b+++ R3b u0c+++",
+              "h0 u0d++ o0 h1 o1 q0 y0 q1 z0 y1 z1 R0 g0 R1 g1 x0 R2 x1 R2b R0b R1b",
+              "h0 R3' o0 h1 q0 R3b' o1 y0 z0 q1 y1 z1 g0 R1 g1 x0 R0 x1 R2 R0b R2b R3 R1b R3b",
+              "h0 o0 h1 q0 o1 y0 q1 z0 y1 z1 R1 g0 g1 x0 R1b R0 x1 R0b R3 R2 R3b R2b"],
+        "G": ["u1+ t0 t1 L0 W0 u1++ W1 u1+++", "t0 t1 L0 T0 W0 W1 T1", "t0 t1 L0 W0 T0 W1 T1", "W0 W1 W2 W3"]},
+}
+
+CFG.update(ct=1, dc=3, mid=1, ff=0.3, qs=0)
+CFG["ord"] = {'V': ['C0 C1 Z0 C2 C3 Z2 Z1 Z3 C5 D1 s1 s1c s1b K2 s0 o1 s0b K0 s0c o0 c0 K1 z0 K3 i0 i0b z1 i0c D3 l0 C7 i1 l0b i1b l1 C6 i1c D2 r0 l0d l0c m0 x0 l1b t0 S0 x1 t1 S1 S2 f1 k1 f2 f0 k0 f3', "s0 v0 s0b s0c v1 o0 k3' s1 s1b s1c o1 k2' z0 i0 i0b i0c l0 l0b z1 l0c l0d i1 i1b i1c l1 r0 l1b m0 x0 S0 x1 t0 S1 t1 S2 e0 e1 f0 f1 k0 k1", "s0 v0 s0c s0b e2' o0 e3' s1 v1 s1c s1b f3' o1 f2' z0 k2' i0 i0b i0c k3' z1 l0 l0b i1 l0c i1b l0d l1 i1c l1b r0 x0 m0 t0 S0 x1 S1 t1 S2 e0 e2 v0+ f2 f0", "s0 v1 s0b s0c e1' o0 f1' k0' s1 s1b s1c k1' o1 z0 k2' i0 i0b l0 i0c e3' z1 f3' l0b i1 i1b i1c x0 k3' l1 t0 e1 l1b e0 f1 x1 f0 k1 k0 t1 e2 e3 f2 k2 f3 k3 f3x k3x"], 'S': ['C1 C2 a0 a1 C3 u1b u1 M0 c1 u1b+ u1+ M1 N0 d0 d1 g0 N1 g1 E0 A1 u1b++ A0 A2 A3 u1++', 'a0 a1 c0 c1 d0 d1 g0 g1 u1b++ A2 A1', 'a0 a1 c0 c1 d0 u1+ g0 d1 g1 A1 A2', 'a0 a1 c0 c1 d0 g0 d1 A1 g1 A2 A3'], 'P': ['u0 K1 K2 u0b u0c u0d h0 h1 K0 u0+ o1 u0b+ o0 u0c+ q0 u0d+ q1 K3 y0 y1 z0 z1 g0 g1 x0 u0++ u0b++ u0c++ x1 u0d++ R1 R0 R3 R1b R2 R2b R0b u0+++ R3b', 'h0 u0b++ o0 h1 q0 o1 y0 q1 z0 y1 z1 u0c++ R0 g0 u0d++ g1 x0 x1 R0b R1 R1b R3 R3b R2 R2b', 'h0 o0 h1 q0 o1 y0 q1 z0 y1 z1 g0 x0 R0 g1 x1 R1 R2 R2b R1b R3 R0b', "h0 o0 h1 q0 R3b' o1 y0 q1 z0 y1 z1 g0 R1 R1b x0 R0 R2 g1 R0b R3 R2b x1 R3b"], 'G': ['C0 C1 C4 C2 u1+ C3 t0 t1 L0 W0 W1', 't0 t1 u1+ L0 W0 T0 W1', "t0 u1+ t1 L0 T1' W0 T0 W1 T1 W0+ W1+ W2+ W3+", '']}
+
+H4 = [(0, 32), (32, 64), (64, 96), (96, 128)]; H5 = [(0, 32), (32, 64), (64, 96), (96, 112), (112, 128)]
+CFG.update({'fp': H5, 'send': [H4, H4, H4], 'tp': H4, 'home': H5, 'tm': 'f2', 'lo': 'zsnra', 'dv': 12, 'sg': ['01', '0123', '0123', '0123'], 'vg': ['a0 c0', '', '', ''],
+            'after': {'al1': 'ft', 'al2': 'fac1', 'al3': 'fac0', 'f2': 'lr1_0'}, 'fix': 2.0, 'bw': 500e3, 'fixv': 0.06, 'gdma': 1.0, 'gis': 0.5, 'rbw': 500e3,
+            'al': 0.3, 'ct': 1, 'dc': 0, 'mid': 2, 'ff': 0.3, 'qs': 0})
+CFG["ord"] = {'V': ['C0 C1 C2 D1 C4 C3 D2 K2 C5 a0 s1 K1 s0 s0c K0 s1c s1b s0b o1 C6 o0 K3 c0 z0 C7 i0 i0b l0 i0c l0d z1 D3 i1 i1b l0b i1c l1 l0c r0 m0 x0 S0 x1 t0 l1b S1 t1 S2 e2 f1 f0 k0', "s0 s0b s0c k1' o0 f2' s1 s1c s1b k2' o1 e3' z0 f3' i0 i0b l0 i0c l0b z1 k3' i1 l0d i1b l0c i1c l1 r0 l1b m0 x0 S0 t0 x1 S1 t1 S2 e0 e1 f0 e2 k0", "s0 f1' s0c s0b k1' o0 s1 f2' s1b s1c e3' o1 k2' z0 f3' i0 i0b l0 i0c l0d z1 k3' i1 i1b l1 i1c l0b r0 l0c m0 x0 S0 t0 x1 l1b S1 t1 S2 e0 e1 f0 k0", "s0 s0c s0b f1' o0 k1' s1 s1b s1c e2' o1 f2' z0 k2' i0 i0b l0 i0c e3' l0b z1 f3' i1 i1b l1 i1c k3' x0 l1b t0 e0 e1 f0 x1 k0 f1 t1 k1 e2 f2 k2 e3 f3 k3 f3x k3x"], 'S': ['C1 C2 a1 u1 u1b M0 C3 M1 u1b+ u1+ N0 c1 N1 d0 d1 g0 u1b++ g1 E0 A0 j0 j1 A1', 'a0 a1 u1+ c0 c1 d0 d1 g0 u1b++ u1++ g1 j0 A1 A0 A2 j1', "a0 a1 A3' c0 c1 d0 d1 g0 g1 j0 A0 A1 j1 A2", "a0 a1 c0 A3' c1 d0 g0 d1 A0 g1 A1 A2 A3"], 'P': ['K2 K1 K0 u0 u0b u0c u0d h1 u0+ u0b+ h0 K3 o1 o0 u0c+ u0d+ q0 u0++ q1 y0 z0 y1 z1 u0b++ g0 u0c++ u0d++ g1 x0 x1 R3 R1 R1b R0 R0b R2', "h0 R2b' o0 h1 R3b' u0++ o1 q0 y0 u0b++ q1 z0 y1 z1 u0c++ g0 u0d++ R0 g1 x0 R1 x1 R0b R2 R1b R2b", "h0 R3' h1 o0 R3b' o1 q0 y0 z0 q1 y1 z1 g0 R0 g1 x0 x1 R0b R3 R1 R1b R2 R3b", "h0 o0 h1 R2b' q0 o1 y0 z0 q1 y1 z1 g0 R0 R0b x0 R1 R1b g1 R3 x1 R2 R2b R3b"], 'G': ['C0 C1 C3 C4 C2 u1+ t0 t1 j0 j1 L0 u1++ W0 W1 W2', "t0 W3' t1 j1 j0 L0 T1 T0 W0 W1 W2 W3 u1++ T3", "t0 j0 t1 T2' j1 L0 W0 W1 W2 T0 T2 W3 T3 T1 W0+ W1+ W2+ W3+ W4+", '']}
+
+CFG.update(ydma=1.0, oq="YSYSY", lo="Sm Yc Yu Sz Ys Y0 Y1 Y2 Y3 Yr Ya"); CFG["after"]["al1"] = "ft3"
+CFG["ord"] = {'V': ['C0 C1 C2 D1 C4 C3 C5 D2 a0 s1 K0 K1 s1b s0 s1c K2 s0c s0b o1 K3 o0 c0 C6 z0 i0 i0b C7 i0c z1 D3 i1 l0 i1b l0b i1c l0d r0 l1 l0c l1b m0 x0 S0 t0 x1 S1 t1 S2 e2 f0 f1 k0', "s0 s0c s0b k1' o0 f2' s1 s1b s1c k2' o1 e3' z0 f3' i0 i0b l0 i0c l0b l0d z1 k3' i1 i1b l0c i1c r0 l1 m0 l1b x0 S0 t0 x1 S1 t1 S2 e2 e0 f0 e1 k0", "s0 s0c s0b f1' o0 k1' s1 f2' s1b s1c e3' o1 k2' z0 f3' i0 i0b l0 i0c z1 k3' i1 l0b i1b l1 i1c l0c r0 l0d m0 x0 S0 t0 l1b x1 S1 t1 S2 e0 f0 e1 k0", "s0 s0b s0c f1' o0 k1' s1 e2' s1c s1b f2' o1 z0 k2' i0 i0b i0c e3' z1 l0 i1 f3' i1b l1 i1c l0b x0 k3' l1b t0 e0 e1 f0 x1 k0 f1 t1 k1 e2 f2 k2 e3 f3 k3 f3x k3x"], 'S': ['C1 C3 C2 a1 u1 u1b M0 M1 u1+ u1b+ c1 N1 N0 d0 d1 g0 E0 g1 u1b++ j0 A1 A0 j1 u1++', 'a0 a1 c0 c1 d0 d1 g0 g1 u1b++ u1++ A0 A1 j1 j0 A3', "a0 a1 A2' c0 c1 d0 d1 g0 g1 j0 A0 A1 j1 A2", "a0 a1 c0 A3' c1 d0 g0 d1 A0 g1 A1 A2 A3 O1 O3"], 'P': ['K0 K3 K2 K1 u0 u0b u0c u0d h1 u0+ u0b+ h0 u0c+ o1 o0 u0d+ q0 u0++ y0 q1 z0 y1 u0b++ z1 u0c++ g0 u0d++ g1 x0 R3 x1 R1 R1b R0 R0b R2 u0+++', "h0 R2b' o0 h1 R3b' o1 q0 y0 u0b++ z0 q1 y1 u0c++ z1 u0d++ g0 g1 x0 R2 R1 x1 R2b R0 R0b R1b", "h0 o0 h1 R3' R3b' q0 o1 y0 q1 z0 y1 z1 g0 g1 x0 R1 R0 x1 R1b R0b R2 R2b", "h0 o0 h1 R3' o1 q0 y0 q1 z0 R3b' y1 z1 g0 R0 R0b x0 R1 R1b g1 R2 x1 R3 R2b R3b"], 'G': ['C0 C1 C2 C3 C4 u1+ t0 j0 t1 j1 L0 u1++ W1 W0 W2 W3', 't0 t1 j0 j1 L0 T0 W0 T1 u1++ W2 W1 T3 W3', "t0 j0 t1 j1 L0 T2' W0 T0 W1 T1 W2 T2 W3 T3 W0+ W1+ W2+ W3+ W4+", '']}
+
+CFG.update(pe0=20, sg=["12", "123", "12", "123"])
+CFG["ord"] = {'V': ['C0 C1 C2 D2 C3 D1 C4 a0 s1 C5 s0 s0b K0 s0c s1c s1b o0 K2 D3 o1 c0 K1 C7 z0 K3 i0 i0b i0c z1 C6 l0 i1 l0b l0d i1b i1c l1 l0c r0 l1b m0 x0 S0 t0 x1 S1 t1 S2 e0 f0 k0 f1', "s0 s0b s0c k1' o0 f2' s1 s1c s1b k2' o1 e3' z0 f3' i0 i0b l0 i0c z1 k3' i1 l0b i1b i1c l0c l1 r0 l0d m0 l1b x0 S0 t0 x1 S1 t1 S2 e0 e2 f0 e1 k0", "s0 s0c s0b f1' o0 k1' f2' s1 s1c s1b e3' o1 k2' z0 f3' i0 i0b l0 i0c l0b z1 k3' i1 l0c i1b i1c l1 r0 l0d m0 l1b x0 S0 t0 x1 S1 t1 S2 e0 e1 f0 k0", "s0 s0b s0c f1' o0 e2' k1' s1 s1b s1c f2' o1 z0 k2' i0 i0b i0c e3' z1 f3' i1 l0 i1b l0b l1 i1c x0 k3' t0 l1b e0 f0 e1 x1 k0 f1 t1 k1 e2 f2 k2 e3 f3 k3 f3x k3x"], 'S': ['C1 a1 C2 u1 u1b M0 M1 C3 u1b+ u1+ c1 N0 N1 d0 d1 g0 E0 g1 j0 u1b++ A1 u1++ j1 A2', 'a0 a1 c0 c1 d0 d1 g0 g1 u1b++ u1++ j0 A1 j1 A2', "a0 a1 A3' c0 c1 d0 d1 g0 g1 A1 j0 A2 j1", 'a0 a1 c0 c1 d0 g0 d1 A1 g1 A2 A3 O1 O3'], 'P': ['K3 K0 K1 u0 K2 u0b u0c u0d h1 u0+ h0 u0b+ u0c+ o0 o1 u0d+ q0 q1 y0 z0 y1 u0++ z1 u0b++ u0c++ g0 u0d++ g1 x0 R0 x1 R0b R1 R2 R3 R2b R1b', "h0 u0++ o0 h1 R3b' o1 q0 y0 q1 z0 y1 z1 u0b++ u0c++ g0 u0d++ g1 x0 x1 R2 R2b R0 R0b R1 R1b R3", "h0 o0 h1 q0 R3b' o1 y0 z0 q1 y1 z1 g0 R1 g1 x0 R0 x1 R2 R1b R2b R0b R3 R3b", 'h0 o0 q0 h1 o1 y0 z0 q1 y1 z1 g0 R0 x0 R1 R0b R1b g1 R3 x1 R2 R2b R3b'], 'G': ['C0 C1 C3 C2 u1+ C4 t0 j0 t1 j1 L0 W1 W0 W2 u1++ W3', 't0 t1 j0 j1 L0 T0 W0 W1 W2 T1 u1++ T3 W3', "t0 T2' t1 j0 j1 L0 T0 W0 W1 T1 W2 T2 W3 T3 W0+ W1+ W2+ W3+ W4+", '']}
+
+CFG.update(sg=["12", "12", "12", "123"])
+CFG["ord"] = {'V': ['C0 C1 C2 C3 C5 C4 a0 s1 D1 K0 s0 D2 s0c s0b D3 s1b s1c o0 K2 K1 o1 c0 K3 C7 z0 i0 i0b l0 i0c z1 i1 C6 i1b l0b l1 i1c l1b l0c r0 l0d m0 x0 S0 t0 x1 S1 t1 S2 e0 f1 f0 k1 f2', "s0 s0c s0b k0' o0 s1 s1c s1b k2' o1 e3' z0 f3' i0 i0b l0 i0c l0b z1 k3' i1 i1b l0c i1c l1 l0d l1b r0 m0 x0 S0 t0 x1 S1 t1 S2 e0 e2 e1 f0 f2 k0", "s0 s0c s0b f1' o0 k1' s1 s1c s1b e3' o1 k2' z0 f3' i0 i0b i0c l0 l0b z1 k3' i1 i1b l1 i1c r0 l0c l0d l1b m0 x0 S0 t0 x1 S1 t1 S2 e0 f0 e1 k0", "s0 s0b s0c f1' o0 k1' s1 s1b s1c e2' o1 f2' z0 k2' i0 i0b i0c e3' z1 f3' l0 i1 l1 i1b l0b i1c x0 k3' t0 e0 l1b f0 e1 k0 x1 f1 t1 k1 e2 f2 k2 e3 f3 k3 f3x k3x"], 'S': ['C1 C2 a1 u1 u1b M0 M1 N0 u1b+ u1+ c1 C3 N1 d0 d1 g0 E0 g1 j0 u1++ A1 u1b++ j1 A2', 'a0 a1 c0 c1 d0 d1 g0 u1b++ u1++ g1 j0 A1 A2 j1', 'a0 a1 c0 c1 d0 d1 g0 g1 j0 A1 j1 A2', 'a0 a1 c0 c1 d0 g0 d1 A1 g1 A2 A3 O1 O3'], 'P': ['K2 K0 K1 K3 u0 u0b u0c u0d h1 h0 u0+ o0 u0b+ u0c+ o1 u0d+ q0 q1 y0 u0++ z0 y1 u0b++ z1 g0 g1 x0 u0c++ u0d++ R0 x1 R1 R2 R2b R1b R0b R3 R3b', 'h0 o0 h1 u0++ o1 q0 y0 q1 z0 y1 u0b++ z1 u0c++ u0d++ g0 R0 g1 x0 R2 x1 R2b R1 R1b R0b R3', "h0 o0 h1 R3b' o1 q0 y0 q1 z0 y1 z1 R0 R1 g0 g1 x0 R0b x1 R2 R2b R1b", "h0 o0 h1 q0 R3' o1 y0 q1 z0 y1 R3b' z1 g0 R0 x0 R1 R0b R1b g1 R2 x1 R2b R3 R3b"], 'G': ['C0 C1 C3 C2 u1+ C4 t0 j0 t1 j1 L0 W0 W1 W2 u1++ W3', 't0 t1 j0 j1 L0 T0 W0 W1 W2 T1 u1++ T3 W3', "t0 T2' t1 j0 j1 L0 T0 W0 W1 T1 W2 T2 W3 T3 W0+ W1+ W2+ W3+ W4+", '']}
+
+CFG["ord"]["V"][0] = "C0 C1 C2 D2 C3 D1 C4 a0 s1 C5 s0 s0b K0 s0c s1c s1b o0 K2 D3 o1 c0 K1 C7 z0 K3 i0 i0b i0c z1 C6 l0 i1 l0b l0d i1b i1c l1 l0c r0 l1b m0 x0 S0 t0 x1 S1 t1 S2 e0 f1 f0 k1 f2"
+CFG["ord"]["S"][0] = "C1 a1 C2 u1 u1b M0 M1 C3 u1b+ u1+ c1 N0 N1 d0 d1 g0 E0 g1 j0 u1b++ A1 u1++ j1 A2"
+CFG["ord"]["P"][0] = "K3 K0 K1 u0 K2 u0b u0c u0d h1 u0+ h0 u0b+ u0c+ o0 o1 u0d+ q0 q1 y0 z0 y1 u0++ z1 u0b++ u0c++ g0 u0d++ g1 x0 R0 x1 R0b R1 R1b R2 R2b R3 R3b"
+CFG["ord"]["G"][0] = "C0 C1 C3 C2 u1+ C4 t0 j0 t1 j1 L0 W1 W0 W2 u1++ W3"
 
 SCRATCH = {
-    "io": ("sbuf", [128, 528], "int32"), "ia": ("sbuf", [128, 528], "int32"),
-    "gw": ("sbuf", [128, 176], "bfloat16"), "rm": ("sbuf", [128, 16], "float32"),
-    "iw": ("sbuf", [128, 144], "float32"), "zw": ("sbuf", [128, 192], "bfloat16"),
+    "io": ("sbuf", [128, 400], "int32"), "ia": ("sbuf", [128, 416], "int32"),
+    "rm": ("sbuf", [128, 16], "float32"), "m4": ("sbuf", [128, 4], "float32"), "mz": ("sbuf", [128, 4], "float32"), "cl": ("sbuf", [128, 4], "float32"),
+    "iw": ("sbuf", [128, 192], "bfloat16"), "ir": ("sbuf", [128, 192], "bfloat16"), "nw": ("sbuf", [128, 192], "bfloat16"), "kw": ("sbuf", [128, 192], "bfloat16"),
+    "hw": ("sbuf", [128, 192], "float16"), "h2": ("sbuf", [128, 144], "bfloat16"), "cq": ("sbuf", [128, 128], "bfloat16"),
+    "nv": ("sbuf", [128, 192], "bfloat16"), "cz": ("sbuf", [128, 128], "bfloat16"),
+    "fk": ("sbuf", [128, 128], "float32"), "rw": ("sbuf", [128, 140], "float16"), "on": ("sbuf", [128, 512], "bfloat16"), "ok": ("sbuf", [128, 128], "bfloat16"),
+    "zw": ("sbuf", [128, 4, 192], "bfloat16"), "sq": ("sbuf", [128, 4, 128], "bfloat16"), "dq": ("sbuf", [128, 4, 128], "bfloat16"),
     "bw": ("sbuf", [128, 16, 176], "bfloat16"), "dd": ("sbuf", [128, 16, 128], "bfloat16"),
-    "ib": ("sbuf", [128, 128], "bfloat16"), "nb": ("sbuf", [128, 128], "bfloat16"), "em": ("sbuf", [128, 128], "bfloat16"),
-    "az": ("sbuf", [128, 144], "float16"), "qa": ("sbuf", [128, 4], "float32"), "lq": ("sbuf", [128, 4], "float32"),
     "cei": ("sbuf", [128, 128], "int32"), "rpi": ("sbuf", [128, 144], "int32"), "rp2": ("sbuf", [128, 144], "int32"),
-    "ut": ("sbuf", [128, 512], "bfloat16"), "lu": ("sbuf", [128, 512], "float32"),
-    "z8": ("sbuf", [8, 8192], "bfloat16"), "zo": ("sbuf", [128, 512], "bfloat16"),
-    "mt": ("sbuf", [128, W], "bfloat16"), "nt": ("sbuf", [128, W], "bfloat16"), "st": ("sbuf", [128, W], "bfloat16"),
-    "at": ("sbuf", [128, W + 16], "bfloat16"), "et": ("sbuf", [128, W], "float32"), "rt": ("sbuf", [128, W], "bfloat16"),
-    "lg": ("sbuf", [128, W], "bfloat16"), "sb": ("sbuf", [128, W], "bfloat16"),
-    "pr": ("sbuf", [128, W], "float16"), "ag": ("sbuf", [128, W], "bfloat16"),
-    "rg0": ("sbuf", [128, W], "bfloat16"), "rg1": ("sbuf", [128, W], "bfloat16"),
-    "c2": ("sbuf", [128, 128], "float32"), "ci": ("sbuf", [128, 128], "int32"), "cm": ("sbuf", [128, 128], "int32"),
-    "du": ("sbuf", [128, 128], "uint16"), "par": ("sbuf", [128, 128], "int32"), "lo": ("sbuf", [128, 128], "float32"),
+    "uz": ("sbuf", [128, W], "bfloat16"),
+    "mt": ("sbuf", [128, W], "bfloat16"), "st": ("sbuf", [128, W], "bfloat16"), "rt": ("sbuf", [128, W], "bfloat16"),
+    "ft": ("sbuf", [128, 4 * W], "bfloat16"), "at": ("sbuf", [128, 4, W + 16], "bfloat16"),
+    "mg": ("sbuf", [128, W], "bfloat16"), "cg": ("sbuf", [128, W], "bfloat16"), "ag": ("sbuf", [128, W], "bfloat16"),
+    "zc": ("sbuf", [128, 512], "float16"),
+    "xf": ("sbuf", [128, 128], "float32"), "pb": ("sbuf", [128, 128], "bfloat16"), "qo": ("sbuf", [128, 128], "bfloat16"), "of": ("sbuf", [128, 128], "uint16"),
+    "ci": ("sbuf", [128, 128], "int32"), "cm": ("sbuf", [128, 128], "int32"), "du": ("sbuf", [128, 128], "uint16"),
+    "par": ("sbuf", [128, 128], "int32"), "lo": ("sbuf", [128, 128], "float16"), "xx": ("sbuf", [128, 128], "bfloat16"),
     "ei": ("sbuf", [128, 48], "int32"), "eu": ("sbuf", [128, 48], "uint16"),
-    "nl0": ("sbuf", [128, 128], "bfloat16"), "nl1": ("sbuf", [128, 128], "bfloat16"), "sn": ("sbuf", [128, 128], "bfloat16"),
-    "n2k": ("sbuf", [128, 128], "float32"), "xx": ("sbuf", [128, 128], "float32"),
-    "ixf": ("sbuf", [128, 128], "float32"), "ix": ("sbuf", [128, 128], "uint16"),
-    "fac": ("sbuf", [128, R], "float32"), "mn": ("sbuf", [128, R], "float32"), "mlo": ("sbuf", [128, R], "float32"),
-    "fsn": ("sbuf", [128, R], "bfloat16"), "lm": ("sbuf", [128, W], "float32"), "ls": ("sbuf", [128, W], "float32"),
-    "ta": ("sbuf", [128, W], "float32"), "fl": ("sbuf", [128, H], "float32"),
-    "td": ("dram", [128, H], "float32"), "fd": ("dram", [2, 128, Q], "float32"),
+    "fac": ("sbuf", [128, R], "float16"), "mn": ("sbuf", [128, R], "float32"), "mlo": ("sbuf", [128, 384], "float32"),
+    "lm": ("sbuf", [128, W], "float32"), "lr1": ("sbuf", [128, W], "float32"), "lr2": ("sbuf", [128, W], "float32"), "lr3": ("sbuf", [128, W], "float32"),
+    "fl": ("sbuf", [128, W], "float32"), "ta": ("sbuf", [128, W], "float32"), "tb": ("sbuf", [128, W], "float32"),
 }
 for _t in range(4):
-    SCRATCH["uh%d" % _t] = ("sbuf", [128, 1024], "bfloat16")
+    SCRATCH["pk%d" % _t] = ("sbuf", [128, 2, PK], "bfloat16")
     SCRATCH["cu%d" % _t] = ("sbuf", [128, 128], "uint16")
+    SCRATCH["cx%d" % _t] = ("sbuf", [128, 2, 128], "uint16")
+    SCRATCH["cf%d" % _t] = ("sbuf", [128, 128], "float32")
     SCRATCH["wo%d" % _t] = ("sbuf", [128, W], "float32")
+    SCRATCH["uo%d" % _t] = ("sbuf", [128, 2, 128], "bfloat16")
     if _t:
-        SCRATCH["zl%d" % _t] = ("sbuf", [128, 128], "bfloat16")
-        SCRATCH["cs%d" % _t] = ("sbuf", [128, 128], "uint16")
+        SCRATCH["ul%d" % _t] = ("sbuf", [128, 2, 128], "bfloat16")
+        SCRATCH["ct%d" % _t] = ("sbuf", [128, 128], "float32")
         SCRATCH["wi%d" % _t] = ("sbuf", [128, W], "float32")
-        SCRATCH["lr%d" % _t] = ("sbuf", [128, W], "float32")
-        SCRATCH["wd%d" % _t] = ("dram", [128, H], "float32")
 for _b in range(8):
-    SCRATCH["b%d" % _b] = ("psum", [128, Q], "float32")
+    SCRATCH["b%d" % _b] = ("psum", [128, 4, 128] if _b == 3 else [128, 512], "float32")
 
-SEMAPHORES = (["eV", "eS", "eP", "eG", "sent", "outs", "accU", "accL", "aTU", "aTL", "rT"]
-              + ["l_" + n for n in ("ce", "uu", "mj", "nx", "sg", "zz", "al", "rp")]
-              + ["%s%d" % (n, t) for n in ("aU", "aZ", "aC", "aWU", "aWL", "rW", "cL", "sL") for t in (1, 2, 3)]
-              + ["aF%d" % q for q in range(4)])
+SEMAPHORES = (["eV", "eS", "eP", "eG", "sent", "outs"]
+              + ["l_" + n for n in ("cei", "u8", "mt", "ft0", "ft1", "ft2", "ft3", "st", "z8", "rpi", "at0", "al1", "al2", "al3")]
+              + ["%s%d" % (n, t) for n in ("aU", "cL") for t in (1, 2, 3)] + ["sL%d_%d" % (t, j) for t in (1, 2, 3) for j in range(2)]
+              + ["%s%d_%d" % (n, t, k) for n in ("aC", "aD", "aW", "aT", "aM") for t in (1, 2, 3) for k in range(4)] + ["aF%d" % k for k in range(6)])
+
+
+def order_of(nodes, first):
+    C = CFG; n = len(nodes); wake = C["wake"]
+    pred = [x["deps"] | x.get("soft", set()) for x in nodes]
+    succ = [[] for _ in nodes]; left = [len(p) for p in pred]
+    for i in range(n):
+        for d in pred[i]: succ[d].append(i)
+    tail = [-x["rank"] for x in nodes]
+    for i in range(n - 1, -1, -1):
+        if not C["ord"]: tail[i] = max([tail[i]] + [tail[j] for j in succ[i]])
+        elif not nodes[i]["tag"]: tail[i] = max([-999] + [tail[j] for j in succ[i]])
+    ready = {e: {} for e in "VSPGY"}; free = {e: 0.0 for e in ready}; fin = [0.0] * n; dma = 0.0; out = []
+    for i in range(n):
+        if not left[i]: ready[nodes[i]["e"]][i] = 0.0
+    def at(q, j):
+        return max(ready[q][j], dma - 0.7 * C["fix"] - C["lead"]) if nodes[j]["dma"] else ready[q][j]
+    while len(out) < n:
+        if len(out) < first:
+            i = len(out); e = nodes[i]["e"]
+        else:
+            e = min((q for q in ready if ready[q]), key=lambda q: max(free[q], min(at(q, j) for j in ready[q])))
+            t0 = max(free[e], min(at(e, j) for j in ready[e]))
+            i = max((j for j in ready[e] if at(e, j) <= t0 + C["win"]), key=lambda j: (tail[j], -j))
+            d = max(nodes[i]["dur"], nodes[i]["dma"])
+            for j in ready[e]:
+                if tail[j] > tail[i] and at(e, j) <= t0 + C["al"] * d: i = j
+        x = nodes[i]; t = max(free[e], ready[e].pop(i)); free[e] = fin[i] = t + x["dur"]
+        if x["dma"]:
+            dma = max(t + 0.7 * C["fix"], dma) + x["dma"]; fin[i] = dma + 0.3 * C["fix"]
+        out.append(i)
+        for j in succ[i]:
+            left[j] -= 1
+            if not left[j]:
+                q = nodes[j]["e"]
+                ready[q][j] = max([fin[d] + (0.0 if q == nodes[d]["e"] == "P" else wake) for d in nodes[j]["deps"]] + [0.0])
+    return out
 
 
 def rank_program(g, core, T, topo):
     rank = T.rank_of(core)
     if rank is None:
         return
+    C = CFG; CP = C["cp"]; WP = C["wp"]
     qs = {"V": g.vector, "S": g.scalar, "P": g.tensor, "G": g, "Y": g.sync}
-    cnt = {}
-    waited = {e: {} for e in qs}
-    wr = {}; rd = {}
+    nodes = []; wr = {}; rd = {}; pr = [999]; sent = [0]; tag = [None]
 
-    def wait(e, tok):
-        s, v = tok
-        if s == "eP" and e == "P":
-            return
+    def node(e, reads, writes, dur, calls, sem=None, dma=0.0, inc=1):
+        deps = set()
+        for k in reads:
+            if k in wr: deps.add(wr[k])
+            if k[0] == "b" and len(k) == 2:
+                deps.update(j for j in rd.get(k, []) if nodes[j]["e"] != e)
+        for k in writes:
+            if k in wr: deps.add(wr[k])
+            deps.update(rd.get(k, []))
+        for k in reads: rd.setdefault(k, []).append(len(nodes))
+        for k in writes:
+            wr[k] = len(nodes); rd[k] = []
+        nodes.append({"e": e, "deps": deps, "dur": dur, "calls": calls, "sem": sem or "e" + e, "dma": dma, "inc": inc, "rank": pr[0], "tag": tag[0]})
+
+    def dmas(e, sem, reads, writes, size, pairs, **kw):
+        node(e, reads, writes, (C["gdma"] if e == "G" else C["ydma"]) * len(pairs), [(lambda o=o, i=i: qs[e].dma_start(o, i, **kw)) for o, i in pairs],
+             sem, size / C["bw"] * (2 if kw else 1), 16)
+
+    def send(hops, sem, reads, writes, size, dst, srcs, fold=1, more=()):
+        dsts = [(hops, dst)] + list(more); to = [T.cores[(rank + h) % NR] for h, _ in dsts]
+        m = topo.mask(core, to[0])
+        for x in to: m &= topo.mask(core, x)
+        ne = bin(m).count("1")
+        def call():
+            if len(srcs) == 1:
+                g.remote_dma(dst, srcs[0], T.sem[sem], T.sem.sent, topo.addr(to[0])[1], topo.addr(to[0])[0], m)
+            else:
+                g.remote_dma_fused([RemoteDMATransfer(dst_ids=[DstId(rid=topo.addr(x)[0], pnc=topo.addr(x)[1]) for x in to], dma_engine_mask=m,
+                                                      remote_sem=T.sem[sem], srcs=srcs, dsts=[d for _, d in dsts], alu_op=fold)], local_sem=T.sem.sent)
+        node("G", reads, writes, C["gis"] + (0 if sent[0] else 2), [call], sem, size * (len(dsts) + C["ff"] * (len(srcs) - 1)) / C["rbw"] + 0.05, -ne * len(dsts))
+        sent[0] += ne
+
+    V = g.vector; S = g.scalar; P = g.tensor; cyc = C["cyc"]
+    def name(t, k): tag[0] = (t, k)
+    def vs(e, r, w, n, fn): node(e, r, w, n * cyc + C["fixv" if e == "V" else "fixs"], [fn])
+    def ts(o, i, a, b, o0, o1, r, w, n=16):
+        if o1 is None: vs("V", r, w, n, lambda: V.tensor_scalar(o, i, a, None, o0))
+        else: vs("V", r, w, n, lambda: V.tensor_scalar(o, i, a, b, o0, o1))
+    def tt(o, a, b, o0, r, w, n=16): vs("V", r, w, n, lambda: V.tensor_tensor(o, a, b, o0))
+    def cp(o, i, r, w, n=16): vs("V", r, w, n, lambda: V.tensor_copy(o, i))
+    def fill_(o, v, w, n=16): vs("V", [], w, n, lambda: V.memset(o, v))
+    def act(o, i, f, r, w, n=16, **kw): vs("S", r, w, n, lambda: S.activation(o, i, f, **kw))
+    def mms(l, r, w, n): node("P", r, w, n * C["pe"], [(lambda x=x: P.matmul(*x)) for x in l])
+    def iota(o, pat, base, ch, w, n): node("G", [], w, 0.13 + 2 * n * cyc, [lambda: g.iota(o, pat, base, ch)])
+    def pick(o, i, pat, base, r, w, n): node("G", r, w, 0.17 + 2 * n * cyc, [lambda: g.affine_select(o, i, pat, OP.is_equal, 0.0, base, 1)])
+    def B(b): return T["b%d" % b]
+    def ks(n, p): return ["%s:%d" % (n, j) for j in range(p[0] // 8, (p[1] + 7) // 8)]
+    def lc(p): return slice(p[0], p[1])
+    def wc(p): return slice(16 * p[0], 16 * p[1])
+    def wn(p): return 16 * (p[1] - p[0])
+    def gn(p): return wn(p) * C["ga"]
+    def up(p): return U0 <= p[0] < U1
+    def cut(p, at): return [(a, b) for a, b in zip([p[0]] + [x for x in at if p[0] < x < p[1]], [x for x in at if p[0] < x < p[1]] + [p[1]])]
+    def after(k): return [C["after"][k]] if k in C["after"] else []
+    ALL = (0, 128); HALF = 128 * W * 2
+
+    LOADS = {"c": ("cei", 65536, T.cei[:], T.ce), "m": ("mt", HALF, T.mt[:], T.mj), "u": ("u8", HALF // 4, T.uz[0:32, :], T.uu),
+             "z": ("z8", HALF // 4, T.uz[64:96, :], T.zz), "s": ("st", HALF, T.st[:], T.sg), "r": ("rpi", 73728, T.rpi[:], T.rp), "a": ("at0", HALF, T.at[:, 0, 0:W], T.al)}
+    for j in range(4):
+        LOADS[str(j)] = ("ft%d" % j, HALF, T.ft[j:128:4, :], T.nx)
+    for e, x in C["lo"].split():
+        k, n, o, i = LOADS[x]; dmas(e, "l_" + k, [], [k], n, [(o, i[:])])
+    first = len(nodes)
+    def load_al(t):
+        n = 16 * t
+        dmas("Y", "l_al%d" % t, after("al%d" % t), ["at%d" % t], HALF, [(T.at[0:128 - n, t, 0:W], T.al[n:128, :]), (T.at[128 - n:128, t, 0:W], T.al[0:n, :])])
+
+    IO = T["io"]; IA = T.ia; AND = OP.bitwise_and; EQ = OP.is_equal; ID = T.iw[:, 16:144]; dv = C["dv"]
+    name(0, "C0")
+    fill_(T.on[:], 1.0, ["on"], 256)
+    fill_(T.ok[:], 128.0, ["ok"], 64)
+    fill_(T.mz[0:64, :], 1.0, ["mz0"]); fill_(T.mz[64:128, :], -1.0 / 128, ["mz1"])
+    iota(IO[:, 16:208], [[1, 192]], 240, -1, ["ioC"], 192)
+    iota(IO[:, 0:16], [[-1, 16]], 16, 1, ["ioA"], 16)
+    iota(IO[:, 208:400], [[1, 192]], 512 - 63, -4, ["ioD"], 192)
+    name(0, "C1")
+    for i in range(dv, 16, 4):
+        pick(T.dd[:, i:i + 4, :], T.on[:], [[-256, 4], [-16, 8], [255, 16]], -256 * i, ["on"], ["dd%d" % j for j in range(i, i + 4)], 512)
+    ts(IA[:, 16:208], IO[:, 16:208], 127, None, AND, None, ["ioC"], ["iaC"], 192)
+    ts(IA[:, 400:404], IO[:, 0:4], 3, None, AND, None, ["ioA"], ["ia3"])
+    ts(T.iw[:], IA[:, 16:208], 0.0, None, EQ, None, ["iaC"], ["iw"], 192)
+    ts(T.m4[:], IA[:, 400:404], 0.0, None, EQ, None, ["ia3"], ["m4"])
+    for o, i, sc, k, n in ((T.fk[:], ID, W, "fk", 128), (T.kw[:], T.iw[:], W, "kw", 192), (T.nv[:], T.iw[:], -W, "nv", 192), (T.cz[:], ID, -128 * 768, "cz", 128)):
+        act(o, i, AF.Copy, ["iw"], [k], n, scale=float(sc))
+    name(0, "C2")
+    for b in range(4):
+        pick(T.sq[:, b, :], T.ok[:], [[-16, 8], [0, 4], [-1, 4]], -4 * b, ["ok"], ["sq%d" % b], 128)
+    ts(IA[:, 208:400], IO[:, 208:400], 127, None, AND, None, ["ioD"], ["iaD"], 192)
+    tt(T.mz[:], T.mz[:], T.m4[:], OP.mult, ["m4", "mz0", "mz1"], ["mz"])
+    for a in range(4): act(T.dq[:, a, :], T.iw[:, 16 - a:144 - a], AF.Copy, ["iw", "m4"], ["dq%d" % a], 128, scale=T.m4[:, 0:1])
+    act(T.cq[:], ID, AF.Copy, ["iw"], ["cq"], 128, scale=-128.0)
+    for t in range(4):
+        ts(T.zw[:, t, :], IA[:, 208:400], float(-4 * t % 128), T.mz[:, t:t + 1], EQ, OP.mult, ["iaD", "mz"], ["zw%d" % t], 192)
+        name(0, "D%d" % (t + 1))
+    name(0, "C3")
+    for i in range(0, 16, 4):
+        pick(T.bw[:, i:i + 4, 0:128], T.on[:], [[-1, 4], [-16, 8], [0, 16]], -i, ["on"], ["bw%d" % i], 512)
+    cp(T.cu0[:, 0:128 - ROT], T.cei[:, ROT:128], ["cei"], ks("cu0", (0, 128 - ROT)), 96)
+    cp(T.cu0[:, 128 - ROT:128], T.cei[:, 0:ROT], ["cei"], ks("cu0", (128 - ROT, 128)), 32)
+    ts(T.cf0[:], T.cu0[:], 1.0 / W, None, OP.mult, None, ks("cu0", ALL), ks("cf0", ALL), 128)
+    act(T.nw[:], T.iw[:], AF.Copy, ["iw"], ["nw"], 192, scale=-1.0)
+    act(T.h2[:], T.iw[:, 0:144], AF.Copy, ["iw"], ["h2"], 144, scale=0.5)
+    name(0, "C4")
+    for i in range(0, 16, 8):
+        pick(T.bw[:, i:i + 8, 128:176], T.on[:, 0:384], [[-1, 8], [-16, 3], [0, 16]], -i, ["on"], ["bx%d" % i], 384)
+    if dv:
+        ts(IA[:, 0:16], IO[:, 0:16], 15, None, AND, None, ["ioA"], ["iaA"])
+        ts(T.rm[:], IA[:, 0:16], 0.0, None, EQ, None, ["iaA"], ["rm"])
+    for i in range(dv): ts(T.dd[:, i, :], ID, T.rm[:, i:i + 1], None, OP.mult, None, ["iw", "rm"], ["dd%d" % i], 64)
+    name(0, "C5")
+    ts(IA[:, 404:405], IO[:, 0:1], 12, None, AND, None, ["ioA"], ["ia12"])
+    cp(T.hw[:], T.iw[:], ["iw"], ["hw"], 96)
+    cp(T.cl[:, 0:1], IA[:, 404:405], ["ia12"], ["q4"])
+    ts(T.cl[:, 1:2], IA[:, 404:405], 128.0, -256.0, OP.mult, OP.add, ["ia12"], ["cl1"])
+    ts(T.cl[:, 2:3], IA[:, 404:405], 128.0, 256.0, OP.mult, OP.add, ["ia12"], ["cl2"])
+    ts(T.rw[:], IO[:, 16:156], T.cl[:, 0:1], 252.0, OP.add, EQ, ["ioC", "q4"], ["rw"], 140)
+    name(0, "C6")
+    nlo = max(wn(h) for h in C["sp"])
+    fill_(T.mlo[:, 0:nlo], math.log(0.0625), ["mlo"], nlo)
+    fill_(T.at[:, :, W:W + 16], -1.0, ["ax"], 32)
+    name(0, "C8")
+    if C["dc"]: fill_(T.lob[:], 0.125, ["lob"], 512); fill_(T.hib[:], 4.0, ["hib"], 512)
+    name(0, "C7")
+    ts(T.rp2[:], T.rpi[:], 2.0, None, OP.mult, None, ["rpi"], ["rp2"], 144)
+    DD = ["dd%d" % i for i in range(16)]; BW = ["bw0", "bw4", "bw8", "bw12", "bx0", "bx8"]
+
+    for q in range(4):
+        c = slice(512 * q, 512 * q + 512); b = 4 + q; name(0, "K%d" % q)
+        mms([(B(b)[:], ID, T.mt[:, c], True, True)], ["iw", "mt"], ["b%d" % b], 512)
+        tt(T.rt[:, c], T.st[:, c], B(b)[:], OP.mult, ["st", "b%d" % b], ["rt%d" % q], 512)
+    pr[0] = C["pl"]
+    for h in range(2):
+        c = slice(1024 * h, 1024 * h + 1024); name(0, "M%d" % h)
+        act(T.lm[:, c], T.mt[:, c], AF.Ln, ["mt", "fn"], ["lm%d" % h], 1024 + (0 if h else 1500))
+    pr[0] = C["pn"]
+    for h in range(2):
+        c = slice(1024 * h, 1024 * h + 1024); name(0, "N%d" % h)
+        act(T.lr3[:, c], T.st[:, c], AF.Ln, ["st", "fn", "lm0"], ["ls%d" % h] + (["lr3"] if h else []), 1024, bias=1e-18)
+    def exp_():
+        name(0, "E0"); pr[0] = C["pe0"]
+        act(T.ir[:], T.iw[:], AF.Exp, ["iw"] + after("e0"), ["ir", "fn", "fx"], 2000, scale=100.0, bias=-100.0)
+    pr[0] = 999; tag[0] = None
+    def fill(t): dmas("Y", "cL%d" % t, ["ls0", "ls1", "lr3"] + after("f%d" % t), ["lr%d" % t], 2 * HALF, [(T["lr%d" % t][:], T.lr3[:])])
+    LM = ["lm0", "lm1"]
+
+    def uz_(t):
+        n = 64 if t else 128; uo = "uo%d" % t; name(t, "u0")
+        for j in range(2):
+            p0 = 64 * j
+            for h in range(2 if t else 1):
+                for i0 in range(0, 16, 16 if t else 8):
+                    mms([(B(3)[:, j, n * h:n * h + n], T.zw[p0:p0 + 32, t, 63 - 16 * t * h - i:191 - 16 * t * h - i],
+                          T.uz[p0:p0 + 32, 16 * n * h + i:16 * n * (h + 1):16], i == 0, i == 15) for i in range(i0, i0 + (16 if t else 8))],
+                        ["zw%d" % t, "z8" if j else "u8"], ["b3"], 1024)
+                    nodes[-1]["own"] = j == 1 and h == i0 == 0
+        name(t, "u1")
+        act(T[uo][:, :, 0:128 - ROT], B(3)[:, 0:2, ROT:128], AF.Copy, ["b3"], [uo + "a"], 192)
+        act(T[uo][:, :, 128 - ROT:128], B(3)[:, 0:2, 0:ROT], AF.Copy, ["b3"], [uo + "b"], 64)
+        if t: send(HOP * t, "aU%d" % t, [uo + "a", uo + "b"], ["ul%d" % t], 65536, T["ul%d" % t][:], [T[uo][:]])
+    def ul(t, j, p): return (T["ul%d" % t] if t else T.uo0)[:, j, lc(p)], (["ul%d" % t] if t else ["uo0a", "uo0b"])
+
+    def gather(t, tok, p, out, win, off, f, r, w, sc=1.0, bias=0.0):
+        for h in cut(p, C["gp"].get(tok[0], [])):
+            o = out(h); x = win.indirect(off[:, lc(h)]); k = ks(w, h)
+            if f == AF.Exp: act(o, x, f, r + ["fx"], k, gn(h), bias=bias)
+            elif "%s%d" % (tok[0], h[0]) not in C["vg"][t].split(): act(o, x, f, r, k, gn(h), scale=sc)
+            elif sc == 1.0: cp(o, x, r, k, gn(h))
+            else: ts(o, x, sc, None, OP.mult, None, r, k, gn(h))
+    def hero(src, k, first): return [(B(k)[:, 0:64], T.dd[:, i, :], src(i), first and i == 0, i == 15) for i in range(16)]
+    def sr_(b, p): return T[b][:, p[0] // 64, p[0] % 64:p[0] % 64 + p[1] - p[0]]
+    def rho(b, p): return T[b][:, p[0] // 64, 64 + 16 * (p[0] % 64):64 + 16 * (p[0] % 64) + wn(p)]
+    def alp(b, p): return T.ag[:, wc(p)]
+    def way(t, k):
+        p = CP[k]; c = lc(p); n = p[1] - p[0]; s = str(k); b = "b" + s; cu = "cu%d" % t; cf = "cf%d" % t; n64 = max(n, 64)
+        name(t, "a" + s)
+        if t == 0: gather(t, "a", p, lambda h: T.mg[:, wc(h)], T.mt[:], T[cu], AF.Copy, ks(cu, p) + ["mt"], "mg")
+        else: gather(t, "a", p, lambda h: T.mg[:, wc(h)], T.lm[:], T[cu], AF.Exp, ks(cu, p) + LM, "mg", bias=3.2e-4)
+        name(t, "h" + s)
+        mms(hero(lambda i: T.mg[:, 16 * p[0] + i:16 * p[1]:16], k, True), DD + ks("mg", p), [b], 16 * n64)
+        u, ur = ul(t, 0, p)
+        name(t, "v" + s)
+        if t and not C["ct"]: ts(T[cf][:, c], T[cu][:, c], 1.0 / W, None, OP.mult, None, ks(cu, p), ks(cf, p), n)
+        name(t, "s" + s)
+        tt(T.xf[:, c], B(k)[:, 0:n], u, OP.mult, [b] + ur, ["xf" + s], n)
+        ts(T.pb[:, c], T.xf[:, c], 15.0, 191.53125, OP.min, OP.add, ["xf" + s], ["pb" + s], n)
+        if C["qs"]: act(T.qo[:, c], T.pb[:, c], AF.Identity, ["pb" + s], ["qo" + s], n, bias=574.5)
+        else: ts(T.qo[:, c], T.xf[:, c], 15.0, 766.03125, OP.min, OP.add, ["xf" + s], ["qo" + s], n)
+        o = B(k)[:, 400:400 + n]; z = B(k)[:, 80:80 + 4 * n]
+        name(t, "o" + s)
+        mms([(o, T.fk[:], T[cf][:, c], True, False), (o, T.kw[:, 16:144], T.pb[:, c], False, False), (o, T.nv[:, 16:144], T.qo[:, c], False, True)],
+            ["fk", "kw", "nv", "pb" + s, "qo" + s] + ks(cf, p), [b], 6 * n64)
+        ts(T.of[:, c], o, 576.0 * W, None, OP.add, None, [b], ["of" + s], n)
+        name(t, "q" + s)
+        mms([(z, T.cz[:], T.on[:, 0:4 * n], True, False)] + [(B(k)[:, 80 + j:80 + 4 * n:4], T.sq[:, j, :], T.qo[:, c], False, False) for j in range(4)],
+            ["sq%d" % j for j in range(4)] + ["cz", "on", "qo" + s], [b], 4 * n64 + 4 * n)
+        name(t, "c" + s)
+        gather(t, "c", p, lambda h: T.cg[:, wc(h)], T.ft[:], T.of, AF.Copy, ["ft0", "ft1", "ft2", "ft3", "of" + s], "cg")
+        name(t, "y" + s)
+        mms([(z, T.dq[:, a, :], T.cg[:, 16 * p[0] + a:16 * p[1]:4], False, a == 3) for a in range(4)], ["dq%d" % a for a in range(4)] + ks("cg", p), [b], 16 * n)
+        name(t, "z" + s)
+        ts(T.zc[:, 4 * p[0]:4 * p[1]], z, T.cl[:, 1:2], T.cl[:, 2:3], OP.max, OP.min, [b, "cl1", "cl2"], ["zc" + s], 4 * n)
+        o = B(k)[:, 0:n]
+        mms([(o, T.fk[:], T[cf][:, c], True, False), (o, T.cq[:], T.qo[:, c], False, False)]
+            + [(o, T.rw[:, 12 - 4 * j:140 - 4 * j], T.zc[:, 4 * p[0] + j:4 * p[1]:4], False, j == 3) for j in range(4)],
+            ["fk", "cq", "rw", "qo" + s, "zc" + s] + ks(cf, p), [b], 9 * n64)
+        name(t, "i" + s)
+        ts(T.ci[:, c], o, 128.0 * 768 - 256, None, OP.add, None, [b], ["ci" + s], n)
+        ts(T.cm[:, c], T.ci[:, c], W - 1, None, AND, None, ["ci" + s], ["cm" + s], n)
+        cp(T.du[:, c], T.cm[:, c], ["cm" + s], ["du" + s], n)
+        name(t, "l" + s)
+        ts(T.par[:, c], T.ci[:, c], 1, None, AND, None, ["ci" + s], ["par" + s], n)
+        if k == 0 and t < 3:
+            tt(T.ei[:], T.par[:, R0:R0 + 48], T.rp2[:, 48 * t:48 * t + 48], OP.add, ["par0", "rp2"], ["ei"], 96)
+            cp(T.eu[:], T.ei[:], ["ei"], ["eu"], 48)
+        tt(T.lo[:, c], T.cm[:, c], T.par[:, c], OP.subtract, ["cm" + s, "par" + s], ["lo" + s], 2 * n)
+    def collide(t, k):
+        p = CP[k]; c = lc(p); n = p[1] - p[0]; s = str(k); b = "b" + s; pk = "pk%d" % t; rg = "rg%d" % t; sr = "sr%d" % t; m = t + 1; n64 = max(n, 64)
+        name(t, "d" + s)
+        if t == 0: gather(t, "d", p, lambda h: rho(pk, h), T.rt[:], T.du, AF.Copy, ["rt0", "rt1", "rt2", "rt3", "du" + s], rg, sc=2.0)
+        else: gather(t, "d", p, lambda h: rho(pk, h), T["lr%d" % t][:], T.du, AF.Exp, ["lr%d_%d" % (t, j) for j in range(C["nadd"])] + ["du" + s], rg, bias=math.log(2.0) + 3.2e-4)
+        z, zr = ul(t, 1, p)
+        name(t, "g" + s)
+        mms([(B(k)[:, 0:n], ID, z, True, False)] + hero(lambda i: T[pk][:, k, 64 + i:1088:16], k, False), DD + ["iw"] + zr + ks(rg, p), [b], 17 * n64)
+        act(sr_(pk, p), B(k)[:, 0:n], AF.Sign, [b], ks(sr, p), n, bias=-1.0 / 256)
+        name(t, "x" + s)
+        tt(T.xx[:, c], T.par[:, c], sr_(pk, p), OP.mult, ["par" + s] + ks(sr, p), ["xx" + s], 2 * n)
+        l = []
+        for h in cut(p, [U0, U1]) if t < 3 else []:
+            o = B(k)[:, 80 + h[0] - p[0]:80 + h[1] - p[0]]; j = 0 if up(h) else 16
+            l += [(o, T.hw[:, j:j + 128], T.lo[:, lc(h)], True, False), (o, T.h2[:, 16:144], T.on[:, lc(h)], False, False),
+                  (o, T.h2[:, j:j + 128], sr_(pk, h), False, False), (o, T.nw[:, j:j + 128], T.xx[:, lc(h)], False, True)]
+        for h in cut(p, [U0, U1] if t else []):
+            o = B(k)[:, 80 + n + h[0] - p[0]:80 + n + h[1] - p[0]]; j = 16 + (16 * t if up(h) else 0)
+            l += [(o, T.hw[:, j:j + 128], T.lo[:, lc(h)], True, False), (o, T.kw[:, 16:144], T.on[:, lc(h)], False, False),
+                  (o, T.iw[:, j:j + 128], T.xx[:, lc(h)], False, False), (o, T.nv[:, j:j + 128], sr_(pk, h), False, True)]
+        mms(l, ["hw", "iw", "nw", "kw", "nv", "h2", "on", "lo" + s, "xx" + s] + ks(sr, p), [b], 64 * len(l))
+        cx = "cx%d" % t; name(t, "t" + s)
+        if t == 3: ts(T[cx][:, 1, c], B(k)[:, 80 + n:80 + 2 * n], float(W), None, OP.min, None, [b], ks(cx, p), n)
+        else:
+            ts(T[cx][:, :, c], B(k)[:, 80:80 + 2 * n], float(W), None, OP.min, None, [b], ks(cx, p), 2 * n)
+            send(HOP, "aC%d_%d" % (m, k), ks(cx, p), ks("cu%d" % m, p), 256 * n, T["cu%d" % m][:, c], [T[cx][:, 0, c]])
+            if C["ct"]:
+                name(t, "j" + s)
+                act(T["ct%d" % m][:, c], B(k)[:, 80:80 + n], AF.Copy, [b], ["ct%d" % m + s], n, scale=1.0 / W)
+                send(HOP, "aD%d_%d" % (m, k), ["ct%d" % m + s], ks("cf%d" % m, p), 512 * n, T["cf%d" % m][:, c], [T["ct%d" % m][:, c]])
+    def reports(t):
+        rg = "rg%d" % t
+        def rl(h): return slice(h[0] - R0, h[1] - R0)
+        def rc(h): return slice(16 * (h[0] - R0), 16 * (h[1] - R0))
+        for j, h in enumerate(C["rp"]):
+            name(t, "r%d" % j)
+            ts(T.fac[:, rc(h)], rho("pk%d" % t, h), 2.0, LN2H, OP.is_gt, OP.mult, ks(rg, h), ks("fac", h) + ["fac%d" % t], wn(h) / 2)
+            name(t, "m%d" % j)
+            tt(T.mn[:, rc(h)], T.lm[:].indirect(T.eu[:, rl(h)]), T.fac[:, rc(h)], OP.subtract, LM + ["eu"] + ks("fac", h), ks("mn", h), gn(h))
+        for j, h in enumerate(C["sp"]):
+            name(t, "S%d" % j)
+            tt(T.lm[:].indirect(T.eu[:, rl(h)]), T.mn[:, rc(h)], T.mlo[:, 0:wn(h)], OP.max, ["eu", "mlo"] + ks("mn", h), LM, wn(h) * C["sc"])
+        k = "lr%d" % (t + 1); n = C["nadd"]
+        for j in range(n):
+            c = slice(W // n * j, W // n * (j + 1)); name(t, "L%d" % j)
+            dmas("G", "sL%d_%d" % (t + 1, j), LM + [k] + (["lr1", "lr2"] if t == 2 else []), ["%s_%d" % (k, j)], 2 * HALF // n,
+                 [(T[k][:, c], T.lm[:, c])], accum_op=OP.add)
+    def weights(t, w):
+        p = WP[w]; b = 4 + w; n = wn(p); j = 16 * t if up(p) else 0; k = "b%d" % b; c = wc(p); a = t if up(p) else 0
+        pk = "pk%d" % t; rg = "rg%d" % t; sr = "sr%d" % t; ag = "ag"; wi = "wi%d" % t; wo = "wo%d" % t; ix = "cx%d" % t
+        l = [(B(b)[:, i:n:16], T.bw[:, i, j:j + 128], sr_(pk, p), False, i == 15) for i in range(16)]
+        name(t, "R%d" % w)
+        mms([(B(b)[:, 0:n], T.nw[:, 16:144], T.on[:, 0:n], True, False), (B(b)[:, 0:n], T.ir[:, 16 + j:144 + j], rho(pk, p), False, False)],
+            ["ir", "nw", "on"] + ks(rg, p), [k], 2 * n)
+        mms(l, BW + ks(sr, p), [k], 1024)
+        win = T.at[:, a, :].indirect(T[ix][:, 1, lc(p)]); r = ["at%d" % a, "ax"] + ks(ix, p); sg = str(w) in C["sg"][t]
+        name(t, "A%d" % w)
+        if sg: act(alp(pk, p), win, AF.Copy, r, ks(ag, p), gn(p))
+        name(t, "e%d" % w)
+        if sg and t: tt(B(b)[:, 0:n], T[wi][:, c], B(b)[:, 0:n], OP.mult, ks(wi, p), [k], n)
+        elif t: tt(T[wo][:, c], win, T[wi][:, c], OP.mult, r + ks(wi, p), ks(wo, p), gn(p))
+        elif not sg: cp(T[wo][:, c], win, r, ks(wo, p), gn(p))
+        for h in [p] if t < 3 else [h for h in C["fp"] if p[0] <= h[0] < p[1]]:
+            o = B(b)[:, 16 * (h[0] - p[0]):16 * (h[1] - p[0])]
+            name(t, "f%d" % w + "x" * (h[0] > p[0]))
+            if t < C["dc"]:
+                tt(T[wo][:, wc(h)], alp(pk, h) if sg else T[wo][:, wc(h)], o, OP.mult, [k] + ks(ag if sg else wo, h), ks(wo, h), wn(h))
+                continue
+            tt(o, alp(pk, h) if sg else T[wo][:, wc(h)], o, OP.mult, ks(ag if sg else wo, h), [k], wn(h))
+            name(t, "k%d" % w + "x" * (h[0] > p[0]))
+            ts(T[wo][:, wc(h)], o, 0.125, 4.0, OP.max, OP.min, [k], ks(wo, h), wn(h))
+    def onward(t):
+        m = t + 1; tm = C["tm"]
+        for j, p in enumerate(C["send"][t]):
+            c = wc(p); name(t, "W%d" % j)
+            if C["dc"]:
+                n = wn(p); mid = T.wm[4 * t + j]; key = ["wm%d_%d" % (t, j)]; keep = ["tb", "ta"][t:t + 1]
+                send(C["mid"], "aM%d_%d" % (m, j), ks("wo%d" % t, p) + ["lob"], key, 512 * n, mid, [T["wo%d" % t][:, c], T.lob[:, 0:n]], 2)
+                name(t, "X%d" % j)
+                send(HOP - C["mid"], "aW%d_%d" % (m, j), key + ["hib"], ks("wi%d" % m, p) + [k for x in keep for k in ks(x, p)], 512 * n,
+                     T["wi%d" % m][:, c], [mid, T.hib[:, 0:n]], 3, [(HOP * (3 - t) - C["mid"], T[x][:, c]) for x in keep])
+                continue
+            send(HOP, "aW%d_%d" % (m, j), ks("wo%d" % t, p), ks("wi%d" % m, p), 512 * wn(p), T["wi%d" % m][:, c], [T["wo%d" % t][:, c]])
+        pr[0] += C["pt"]
+        for j, p in enumerate([] if C["dc"] else C["tp"]):
+            c = wc(p); n = 512 * wn(p); name(t, "T%d" % j)
+            if t == 1 and tm == "f2": send(HOP, "aT1_%d" % j, ks("wo1", p) + ks("wi1", p), ks("tb", p), n, T.tb[:, c], [T.wo1[:, c], T.wi1[:, c]])
+            elif t == 1: send(2 * HOP, "aT1_%d" % j, ks("wo1", p) + ks("wi1", p), ks("ta", p), n, T.ta[:, c], [T.wo1[:, c], T.wi1[:, c]])
+            if t == 2 and tm == "f2": send(HOP, "aT2_%d" % j, ks("wo2", p) + ks("tb", p), ks("ta", p), n, T.ta[:, c], [T.wo2[:, c], T.tb[:, c]])
+            if t == 2 and tm == "acc": dmas("G", "aT2_%d" % j, ks("wi3", p), ks("ta", p), n, [(T.ta[:, c], T.wi3[:, c])], accum_op=OP.add)
+    def home():
+        for j, p in enumerate(C["home"]):
+            c = wc(p); s0 = 16 * ((p[0] + ROT) % 128); src = ["wo3", "ta"] + (["wi3", "tb"] if C["dc"] else ["wi3"] if C["tm"] == "f3" else [])
+            name(3, "W%d" % j)
+            send(-3 * HOP, "aF%d" % j, [k for n in src for k in ks(n, p)], ks("fl", p), 512 * wn(p), T.fl[:, c], [T[n][:, c] for n in src])
+            e = C["oq"][j]; tag[0] = (3, "O%d" % j) if e == "S" else None
+            dmas(e, "outs", ks("fl", p), [], 512 * wn(p), [(T.tl[:, s0:s0 + wn(p)], T.fl[:, c])])
+
+    uz_(0)
+    pr[0] = C["pu"][0]; uz_(1)
+    pr[0] = 999; tag[0] = None; fill(1)
+    for t in range(4):
+        for k in range(len(CP)): pr[0] = 100 * t + 10 * k; way(t, k)
+        for k in range(len(CP)): pr[0] = 100 * t + 10 * k + C["pc"]; collide(t, k)
+        if t == 0: exp_()
+        pr[0] = 100 * t + C["pr"]
+        if t < 3: reports(t)
+        pr[0] = 999; tag[0] = None
+        if t < 3: load_al(t + 1)
+        if t == 0: fill(2)
+        for n in (2, 3) if t == 0 else (): pr[0] = C["pu"][n - 1]; uz_(n)
+        for w in range(len(WP)): pr[0] = 100 * t + C["pw"] + w; weights(t, w)
+        pr[0] = 100 * t + C["ps"]
+        if t < 3: onward(t)
+        else: home()
+
+    place = {}; seen = {}
+    for x in nodes:
+        if x["tag"]:
+            k = (x["e"],) + x["tag"]; seen[k] = seen.get(k, -1) + 1
+            if seen[k] and x["tag"][1][0] in C["fine"]: x["tag"] = (x["tag"][0], x["tag"][1] + "-bcdefg"[seen[k]])
+    for e in C["ord"]:
+        for t, line in enumerate(C["ord"][e]):
+            for j, x in enumerate(line.split()): place[(e, t - x.count("'") + x.count("+"), x.strip("'+"))] = 100 * t + j
+    last = {}
+    for i in sorted((i for i, x in enumerate(nodes) if x["tag"] and place), key=lambda i: (place[(nodes[i]["e"],) + nodes[i]["tag"]], i)):
+        x = nodes[i]; x["rank"] = place[(x["e"],) + x["tag"]]
+        if x["e"] in last: x["soft"] = {last[x["e"]]}
+        last[x["e"]] = i
+    cnt = {}; tok = {}; waited = {e: {} for e in qs}
+    def wait(e, s, v):
         if waited[e].get(s, 0) < v:
             qs[e].wait_ge(T.sem[s], v); waited[e][s] = v
-
-    def deps(e, reads, writes):
-        need = {}
-        def add(tok):
-            need[tok[0]] = max(need.get(tok[0], 0), tok[1])
-        for k in reads:
-            if k in wr: add(wr[k])
-            if k[0] == "b" and len(k) == 2:
-                for tok in rd.get(k, []):
-                    if tok[0] != "e" + e: add(tok)
-        for k in writes:
-            if k in wr: add(wr[k])
-            for tok in rd.get(k, []): add(tok)
-        for s in need: wait(e, (s, need[s]))
-
-    def mark(tok, reads, writes):
-        for k in reads: rd.setdefault(k, []).append(tok)
-        for k in writes:
-            wr[k] = tok; rd[k] = []
-
-    def op(e, reads, writes, fn):
-        deps(e, reads, writes)
-        s = "e" + e; cnt[s] = cnt.get(s, 0) + 1
-        fn().then_inc(T.sem[s], 1)
-        mark((s, cnt[s]), reads, writes)
-
-    def dmas(e, sem, reads, writes, pairs, **kw):
-        deps(e, reads, writes)
-        for o, i in pairs:
-            qs[e].dma_start(o, i, **kw).then_inc(T.sem[sem], 16)
-            cnt[sem] = cnt.get(sem, 0) + 16
-        mark((sem, cnt[sem]), reads, writes)
-
-    def arrive(sem, key):
-        cnt[sem] = 16; wr[key] = (sem, 16); rd[key] = []
-
-    def send(hops, sem, reads, dst, srcs):
-        to = T.cores[(rank + hops) % NR]
-        rid, pid, _ = topo.addr(to)
-        m = topo.mask(core, to)
-        deps("G", reads, [])
-        if len(srcs) == 1:
-            g.remote_dma(dst, srcs[0], T.sem[sem], T.sem.sent, pid, rid, m)
-        else:
-            g.remote_dma_fused([RemoteDMATransfer(dst_ids=[DstId(rid=rid, pnc=pid)], dma_engine_mask=m, remote_sem=T.sem[sem],
-                                                  srcs=srcs, dsts=[dst], alu_op=1)], local_sem=T.sem.sent)
-        cnt["sent"] = cnt.get("sent", 0) + len(topo.engines(core, to))
-
-    V = g.vector; S = g.scalar; P = g.tensor
-    def ts(o, i, a, b, o0, o1, r, w):
-        if o1 is None: op("V", r, w, lambda: V.tensor_scalar(o, i, a, None, o0))
-        else: op("V", r, w, lambda: V.tensor_scalar(o, i, a, b, o0, o1))
-    def tt(o, a, b, o0, r, w): op("V", r, w, lambda: V.tensor_tensor(o, a, b, o0))
-    def cp(o, i, r, w): op("V", r, w, lambda: V.tensor_copy(o, i))
-    def act(o, i, f, r, w, **kw): op("S", r, w, lambda: S.activation(o, i, f, **kw))
-    def mm(o, l, x, a, z, r, w): op("P", r, w, lambda: P.matmul(o, l, x, a, z))
-    def B(b): return T["b%d" % b]
-    def qc(q): return slice(Q * q, Q * q + Q)
-    def ql(q): return slice(32 * q, 32 * q + 32)
-    def allq(n): return [n + str(q) for q in range(4)]
-    def hq(n, h): return [n + str(2 * h), n + str(2 * h + 1)]
-    PS = CFG["ps"]; PB = [2, 3, 2, 3]
-
-    for t in (1, 2, 3):
-        arrive("aU%d" % t, "uh%d" % t); arrive("aZ%d" % t, "zl%d" % t); arrive("aC%d" % t, "cu%d" % t)
-        arrive("aWU%d" % t, "wd%d" % t); arrive("aWL%d" % t, "wiL%d" % t)
-    arrive("aTU", "td"); arrive("aTL", "taL")
-    for q in range(4): arrive("aF%d" % q, "f%d" % q)
-
-    dmas("Y", "l_ce", [], ["cei"], [(T.cei[:], T.ce[:])])
-    dmas("S", "l_uu", [], ["ut"], [(T.ut[:], T.uu[:])])
-    dmas("Y", "l_mj", [], ["mt"], [(T.mt[:], T.mj[:])])
-    dmas("Y", "l_nx", [], ["nt"], [(T.nt[:], T.nx[:])])
-    dmas("Y", "l_sg", [], ["st"], [(T.st[:], T.sg[:])])
-    dmas("Y", "l_zz", [], ["z8"], [(T.z8[:], T.zz[:])])
-    dmas("Y", "l_al", [], ["at"], [(T.at[:, 0:W], T.al[:])])
-    dmas("Y", "l_rp", [], ["rpi"], [(T.rpi[:], T.rp[:])])
-
-    IO = T["io"]
-    op("G", [], ["io2"], lambda: g.iota(IO[:, 512:528], [[-1, 16]], 16, 1))
-    op("G", [], ["io1"], lambda: g.iota(IO[:, 0:176], [[-16, 11], [0, 16]], 48 + 128, 1))
-    op("G", [], ["io3"], lambda: g.iota(IO[:, 176:320], [[1, 144]], 256 - 16, -1))
-    op("V", [], ["dd"], lambda: V.memset(T.dd[:, 0:8, :], 1.0))
-    op("G", ["dd"], ["bw%d" % s for s in range(8, 16)],
-       lambda: g.affine_select(T.bw[:, 8:16, 48:176], T.dd[:, 0:8, :], [[-1, 8], [-16, 8], [0, 16]], OP.is_equal, 0.0, -8, 1))
-    op("G", [], ["io4"], lambda: g.iota(IO[:, 320:512], [[1, 192]], 2048 + 128 - 63, -16))
-    op("G", ["dd"], ["bwx"],
-       lambda: g.affine_select(T.bw[:, 8:16, 0:48], T.dd[:, 0:8, 0:48], [[-1, 8], [-16, 3], [0, 16]], OP.is_equal, 0.0, -88, 1))
-    ts(T.ia[:, 512:528], IO[:, 512:528], 15, None, OP.bitwise_and, None, ["io2"], ["ia2"])
-    ts(T.qa[:, 0:1], T.ia[:, 512:513], -1.0 / 32, 1e-17, OP.add, OP.max, ["ia2"], ["qa"])
-    act(T.lq[:, 0:1], T.qa[:, 0:1], AF.Ln, ["qa"], ["lq"], scale=QS)
-    ts(T.ia[:, 0:176], IO[:, 0:176], 127, None, OP.bitwise_and, None, ["io1"], ["ia1"])
-    ts(T.rm[:], T.ia[:, 512:528], 0.0, None, OP.is_equal, None, ["ia2"], ["rm"])
-    ts(T.gw[:], T.ia[:, 0:176], 16.0, None, OP.is_lt, None, ["ia1"], ["gw"])
-    ts(T.ia[:, 176:320], IO[:, 176:320], 127, None, OP.bitwise_and, None, ["io3"], ["ia3"])
-    def bw_(s): ts(T.bw[:, s, :], T.gw[:], T.rm[:, s:s + 1], None, OP.mult, None, ["gw", "rm"], ["bw%d" % s])
-    ts(T.iw[:], T.ia[:, 176:320], 0.0, None, OP.is_equal, None, ["ia3"], ["iw"])
-    bw_(0)
-    tt(T.em[:], T.iw[:, 16:144], T.iw[:, 15:143], OP.subtract, ["iw"], ["em"])
-    bw_(1)
-    cp(T.cu0[:], T.cei[:], ["cei"], ["cu0"])
-    tt(T.em[:, 0:128:16], T.iw[:, 16:144:16], T.iw[:, 31:144:16], OP.add, ["iw"], ["em"])
-    for s in range(2, 8): bw_(s)
-    BW = ["bw%d" % s for s in range(16)]
-    op("G", BW, ["dd"], lambda: g.affine_select(T.dd[:], T.bw[:, :, 48:176], [[0, 16], [-1, 128]], OP.is_equal, 0.0, 0, 1))
-    act(T.lu[:], T.ut[:], AF.Ln, ["ut"], ["lu"], scale=1.0 / 16, bias=1e-5)
-    act(T.uh0[:, 0:512], T.lu[:], AF.Copy, ["lu"], ["uhi"])
-    cp(T.ib[:], T.iw[:, 16:144], ["iw"], ["ib"])
-    tt(T.uh0[:, 512:1024], T.lu[:], T.uh0[:, 0:512], OP.subtract, ["lu", "uhi"], ["uh0"])
-
-    def a_(t, q):
-        o = T["cu%d" % t][:, ql(q)]
-        if t == 0: act(T.lg[:, qc(q)], T.mt[:].indirect(o), AF.Ln, ["mt", "cu0"], ["lg%d" % q], scale=CM)
-        else: act(T.lg[:, qc(q)], T.lm[:].indirect(o), AF.Identity, ["lm", "cu%d" % t], ["lg%d" % q], bias=math.log(CM))
-    def pu(t, q, a, z):
-        b = PB[q]; o = 48 - (16 * t if q >= 2 else 0)
-        for j in range(2):
-            mm(B(b)[:], T.bw[:, 4 * t + q, o:o + 128], T["uh%d" % t][:, qc(j)], a and j == 0, z and j == 1,
-               ["uh%d" % t, "uhi", "bw%d" % (4 * t + q)] + (["bwx"] if t else []), ["b%d" % b])
-    def ps(t, q):
-        b = PB[q]
-        for i in range(16):
-            mm(B(b)[:, i:Q:16], T.bw[:, i, 48:176], T.lg[:, Q * q + i:Q * q + Q:16], t == 0 and i == 0, t > 0 and i == 15,
-               ["bw%d" % i, "lg%d" % q], ["b%d" % b])
-    def p1(t, q): ps(t, q); pu(t, q, False, True)
-    def b_(t, q):
-        act(T.sb[:, qc(q)], B(PB[q])[:], AF.Sign, ["b%d" % PB[q], "lq"], ["sb%d" % q], scale=-1.0, bias=T.lq[:, 0:1])
-    def c_(t, q):
-        tt(T.pr[:, qc(q)], T.et[:].indirect(T["cu%d" % t][:, ql(q)]), T.sb[:, qc(q)], OP.mult, allq("et") + ["cu%d" % t, "sb%d" % q], ["pr%d" % q])
-    def c2_(t): ts(T.c2[:], T["cu%d" % t][:], 2048.0, None, OP.add, None, ["cu%d" % t], ["c2"])
-    def way(h):
-        for i in range(16):
-            mm(B(6 + h)[:, 128:192], T.az[:, 15 - i:143 - i], T.pr[:, H * h + i:H * h + H:16], i == 0, i == 15, ["az"] + hq("pr", h), ["b%d" % (6 + h)])
-    def sm(h):
-        c = slice(64 * h, 64 * h + 64)
-        tt(T.ci[:, c], B(6 + h)[:, 128:192], T.c2[:, c], OP.add, ["b%d" % (6 + h), "c2"], ["ci%d" % h])
-        ts(T.cm[:, c], T.ci[:, c], W - 1, None, OP.bitwise_and, None, ["ci%d" % h], ["cm%d" % h])
-        cp(T.du[:, c], T.cm[:, c], ["cm%d" % h], ["du%d" % h])
-    def d_(t, h):
-        n = "rg%d" % (t % 2); o = T.du[:, 64 * h:64 * h + 64]
-        if t == 0: act(T[n][:, H * h:H * h + H], T.rt[:].indirect(o), AF.Copy, allq("rt") + ["du%d" % h], hq(n, h))
-        else: act(T[n][:, H * h:H * h + H], T["lr%d" % t][:].indirect(o), AF.Exp, ["lr%d" % t, "du%d" % h], hq(n, h))
-    def hero(t, h):
-        n = "rg%d" % (t % 2); c = slice(64 * h, 64 * h + 64)
-        zl = T.zo[:, c] if t == 0 else T["zl%d" % t][:, c]
-        mm(B(6)[:, c], T.nb[:], zl, True, False, ["nb", "zl%d" % t], ["b6"])
-        for i in range(16):
-            mm(B(6)[:, c], T.dd[:, i, :], T[n][:, H * h + i:H * h + H:16], False, i == 15, ["dd"] + hq(n, h), ["b6"])
-    def lists(t):
-        ts(T.par[:], T.cm[:], 1, None, OP.bitwise_and, None, ["cm0", "cm1"], ["par"])
-        tt(T.ei[:], T.par[:, 40:88], T.rp2[:, 48 * t:48 * t + 48], OP.add, ["par", "rp2"], ["ei"])
-        tt(T.lo[:], T.cm[:], T.par[:], OP.subtract, ["cm0", "cm1", "par"], ["lo"])
-        cp(T.eu[:], T.ei[:], ["ei"], ["eu"])
-    def post(t):
-        n = "nl%d" % (t % 2); th = 1.0 / 512
-        if t in PS:
-            act(T.sn[:], B(6)[:, 0:128], AF.Sign, ["b6"], ["sn"], scale=-1.0, bias=th)
-            act(T[n][:], T.sn[:], AF.Relu, ["sn"], [n])
-            act(T.n2k[:], T.sn[:], AF.Relu, ["sn"], ["n2k"], scale=float(W))
-        else:
-            ts(T[n][:], B(6)[:, 0:128], th, None, OP.is_le, None, ["b6"], [n])
-            ts(T.n2k[:], B(6)[:, 0:128], th, float(W), OP.is_le, OP.mult, ["b6"], ["n2k"])
-        if t in CFG["fs"]: act(T.fac[:], T.fsn[:], AF.Relu, ["fsn"], ["fac"], scale=math.log(2.0))
-        if t < 3:
-            tt(T.xx[:], T.par[:], T[n][:], OP.is_equal, ["par", n], ["xx"])
-            for h in range(2):
-                c = slice(64 * h, 64 * h + 64); o = B(7)[:, 256 + 64 * h:320 + 64 * h]
-                l = T.iw[:, 0:128] if h else T.iw[:, 16:144]
-                mm(o, l, T.lo[:, c], True, False, ["iw", "lo"], ["b7"])
-                mm(o, l, T.xx[:, c], False, True, ["xx"], ["b7"])
-        tt(T.ixf[:], T.cm[:], T.n2k[:], OP.max, ["cm0", "cm1", "n2k"], ["ixf"])
-        cp(T.ix[:], T.ixf[:], ["ixf"], ["ix"])
-        if t < 3:
-            s = "cs%d" % (t + 1)
-            cp(T[s][:], B(7)[:, 256:384], ["b7"], [s])
-            send(HOP, "aC%d" % (t + 1), [s], T["cu%d" % (t + 1)][:], [T[s][:]])
-    def rn(t, q, b):
-        n = "rg%d" % (t % 2); m = "nl%d" % (t % 2); k = "b%d" % b
-        mm(B(b)[:], T.nb[:], T[n][:, qc(q)], True, False, ["nb", n + str(q)], [k])
-        for i in range(16):
-            mm(B(b)[:, i:Q:16], T.bw[:, i, 48:176], T[m][:, ql(q)], False, i == 15, [m], [k])
-    def fg(h):
-        act(T.ag[:, H * h:H * h + H], T.at[:].indirect(T.ix[:, 64 * h:64 * h + 64]), AF.Copy, ["at", "atx", "ix"], hq("ag", h), scale=-2.0)
-    def fq(q):
-        act(T.ag[:, qc(q)], T.at[:].indirect(T.ix[:, ql(q)]), AF.Copy, ["at", "atx", "ix"], ["ag%d" % q], scale=-2.0)
-    def e_(t, q, b):
-        if t: tt(B(b)[:], T["wi%d" % t][:, qc(q)], B(b)[:], OP.mult, ["wi%s%d" % ("U" if q >= 2 else "L", t)], ["b%d" % b])
-    def f_(q, b): tt(B(b)[:], T.ag[:, qc(q)], B(b)[:], OP.mult, ["ag%d" % q], ["b%d" % b])
-    def g_(t, q, b): ts(T["wo%d" % t][:, qc(q)], B(b)[:], 0.125, 4.0, OP.max, OP.min, ["b%d" % b], ["wo%d_%d" % (t, q)])
-    def fac(t):
-        n = "rg%d" % (t % 2)
-        if t in CFG["fs"]: act(T.fsn[:], T[n][:, LO:LO + R], AF.Sign, [n + "1", n + "2"], ["fsn"], bias=-1.0625)
-        else: ts(T.fac[:], T[n][:, LO:LO + R], 1.0, math.log(2.0), OP.is_gt, OP.mult, [n + "1", n + "2"], ["fac"])
-    def reports(t):
-        tt(T.mn[:], T.lm[:].indirect(T.eu[:]), T.fac[:], OP.subtract, ["lm", "eu", "fac"], ["mn"])
-        tt(T.lm[:].indirect(T.eu[:]), T.mn[:], T.mlo[:], OP.max, ["eu", "mn", "mlo"], ["lm"])
-        k = "lr%d" % (t + 1)
-        dmas("G", "sL%d" % (t + 1), ["lm"], [k], [(T[k][:], T.lm[:])], accum_op=OP.add)
-    def kp(q, b): mm(B(b)[:], T.ib[:], T.mt[:, qc(q)], True, True, ["ib", "mt"], ["b%d" % b])
-    def k_(q, b): tt(T.rt[:, qc(q)], T.st[:, qc(q)], B(b)[:], OP.mult, ["st", "b%d" % b], ["rt%d" % q])
-    def zl_(t):
-        for h in range(2):
-            for i in range(16):
-                o = 63 - (16 * t if h else 0) - i; c0 = W * t + H * h
-                mm(B(7)[:, 384 + 64 * h:448 + 64 * h], T.zw[0:8, o:o + 128], T.z8[0:8, c0 + i:c0 + H:16], i == 0, i == 15, ["zw", "z8"], ["b7"])
-        act(T.zo[:, 128 * t:128 * t + 128], B(7)[:, 384:512], AF.Copy, ["b7"], ["zo%d" % t if t else "zl0"], scale=1.0 / 256)
-    def turn(dst, src, n, sem, rk, wk):
-        dmas("Y", sem, [rk], [wk], [(dst[16 * n:128, H:W], src[0:128 - 16 * n, :]), (dst[0:16 * n, H:W], src[128 - 16 * n:128, :])])
-    def send_w(t, h):
-        wo = T["wo%d" % t]; c = slice(H * h, H * h + H); ks = ["wo%d_%d" % (t, 2 * h), "wo%d_%d" % (t, 2 * h + 1)]
-        if h:
-            send(HOP, "aWU%d" % (t + 1), ks, T["wd%d" % (t + 1)][:], [wo[:, c]])
-            turn(T["wi%d" % (t + 1)], T["wd%d" % (t + 1)], 1, "rW%d" % (t + 1), "wd%d" % (t + 1), "wiU%d" % (t + 1))
-        else:
-            send(HOP, "aWL%d" % (t + 1), ks, T["wi%d" % (t + 1)][:, c], [wo[:, c]])
-    def send_t(h):
-        c = slice(H * h, H * h + H); ks = ["wo1_%d" % (2 * h), "wo1_%d" % (2 * h + 1)]
-        if h:
-            send(2 * HOP, "aTU", ks + ["wiU1"], T.td[:], [T.wo1[:, c], T.wi1[:, c]])
-            turn(T.ta, T.td, 2, "rT", "td", "taU")
-        else:
-            send(2 * HOP, "aTL", ks + ["wiL1", CFG["tl"]], T.ta[:, c], [T.wo1[:, c], T.wi1[:, c]])
-    def fill(t): dmas("Y", "cL%d" % t, ["ls"], ["lr%d" % t], [(T["lr%d" % t][:], T.ls[:])])
-
-    def ep(q, b): mm(B(b)[:], T.em[:], T.nt[:, qc(q)], True, True, ["em", "nt"], ["b%d" % b])
-    KB = CFG["kb"]
-    def consts():
-        ts(T.az[:], T.iw[:], 0.0, None, OP.mult, None, ["iw"], ["az"])
-        ts(T.ia[:, 320:512], IO[:, 320:512], 127, None, OP.bitwise_and, None, ["io4"], ["ia4"])
-        ts(T.zw[:], T.ia[:, 320:512], 0.0, None, OP.is_equal, None, ["ia4"], ["zw"])
-        ts(T.az[:, 15:143:16], T.gw[:, 48:176:16], -0.5, None, OP.mult, None, ["gw"], ["az"])
-        c2_(0)
-    def lns():
-        act(T.ls[:], T.st[:], AF.Ln, ["st"], ["ls"], bias=1e-18)
-        fill(1); fill(2); fill(3)
-    PB[:] = CFG["pb0"]
-    for x in CFG["first"].split():
-        k = int(x[1])
-        {"a": lambda: a_(0, k), "p": lambda: p1(0, k), "b": lambda: b_(0, k), "c": lambda: c_(0, k), "w": lambda: way(k), "s": lambda: sm(k),
-         "d": lambda: d_(0, k), "e": lambda: ep(k, 4 + k), "K": lambda: kp(k, KB[k]), "k": lambda: k_(k, KB[k]), "x": consts, "l": lns, "z": lambda: zl_(0),
-         "S": lambda: act(T.et[:, qc(k)], B(4 + k)[:], AF.Copy, ["b%d" % (4 + k)], ["et%d" % k]),
-         "V": lambda: cp(T.et[:, qc(k)], B(4 + k)[:], ["b%d" % (4 + k)], ["et%d" % k])}[x[0]]()
-    PB[:] = (2, 3, 2, 3)
-    for t in (1, 2, 3): send(HOP * t, "aU%d" % t, ["uh0"], T["uh%d" % t][:], [T.uh0[:]])
-    ts(T.nb[:], T.iw[:, 16:144], -1.0, None, OP.mult, None, ["iw"], ["nb"])
-    ts(T.rp2[:], T.rpi[:], 2.0, None, OP.mult, None, ["rpi"], ["rp2"])
-    sm(1); d_(0, 1); lists(0)
-    op("V", [], ["atx"], lambda: V.memset(T.at[:, W:W + 16], -1.0))
-    op("V", [], ["mlo"], lambda: V.memset(T.mlo[:], math.log(0.0625)))
-    act(T.lm[:], T.mt[:], AF.Ln, ["mt"], ["lm"])
-    hero(0, 0); hero(0, 1); fac(0)
-
-    for t in range(3):
-        n = t + 1
-        post(t)
-        if t:
-            send_w(t - 1, 0)
-        fg(1); rn(t, 2, 0); zl_(n); rn(t, 3, 1); rn(t, 0, 4); rn(t, 1, 5); fg(0)
-        send(HOP * n, "aZ%d" % n, ["zo%d" % n], T["zl%d" % n][:], [T.zo[:, 128 * n:128 * n + 128]])
-        reports(t)
-        def up():
-            send_w(t, 1)
-            if t == 1: send_t(1)
-        rest = [lambda: e_(t, 2, 0), lambda: e_(t, 3, 1), lambda: f_(2, 0), lambda: f_(3, 1), lambda: g_(t, 2, 0), lambda: (g_(t, 3, 1), up()),
-                lambda: e_(t, 0, 4), lambda: e_(t, 1, 5), lambda: f_(0, 4), lambda: f_(1, 5), lambda: g_(t, 0, 4), lambda: g_(t, 1, 5)]
-        if t == 0: rest = rest[2:6] + rest[8:]
-        c2_(n)
-        for x in CFG["ord%d" % t].split():
-            if x == "F": rest.pop(0)()
-            else:
-                k = int(x[1])
-                {"a": lambda: a_(n, k), "u": lambda: pu(n, k, True, False), "p": lambda: ps(n, k), "b": lambda: b_(n, k), "c": lambda: c_(n, k),
-                 "w": lambda: way(k), "s": lambda: sm(k), "d": lambda: d_(n, k), "h": lambda: hero(n, k)}[x[0]]()
-        for fn in rest: fn()
-        if n < 3: lists(n); fac(n)
-
-    send_t(0); send_w(2, 0)
-    post(3)
-    dmas("G", "accU", ["wiU3"], ["taU"], [(T.ta[:, H:W], T.wi3[:, H:W])], accum_op=OP.add)
-    dmas("G", "accL", ["wiL3"], ["taL"], [(T.ta[:, 0:H], T.wi3[:, 0:H])], accum_op=OP.add)
-    bank = {2: 4, 3: 5, 0: 0, 1: 1}
-    for q in (2, 3, 0, 1):
-        rn(3, q, bank[q]); fq(q)
-    def home(q):
-        dst = T.fd[q - 2] if q >= 2 else T.fl[:, qc(q)]
-        send(-3 * HOP, "aF%d" % q, ["wo3_%d" % q, "taU" if q >= 2 else "taL"], dst, [T.wo3[:, qc(q)], T.ta[:, qc(q)]])
-    for a, b in ((2, 3), (0, 1)):
-        e_(3, a, bank[a]); e_(3, b, bank[b]); f_(a, bank[a]); f_(b, bank[b])
-        g_(3, a, bank[a]); home(a); g_(3, b, bank[b]); home(b)
-    for q in (2, 3):
-        dmas("Y", "outs", ["f%d" % q], [], [(T.tl[0:80, qc(q)], T.fd[q - 2, 48:128, :]), (T.tl[80:128, qc(q)], T.fd[q - 2, 0:48, :])])
-    dmas("S", "outs", ["f0"], [], [(T.tl[:, qc(0)], T.fl[:, qc(0)])])
-    dmas("Y", "outs", ["f1"], [], [(T.tl[:, qc(1)], T.fl[:, qc(1)])])
-    for s in cnt: wait("G", (s, cnt[s]))
+    for i in order_of(nodes, first):
+        x = nodes[i]; e = x["e"]; s = x["sem"]; need = {}
+        for d in x["deps"]:
+            if x.get("own") or not e == nodes[d]["e"] == "P": need[tok[d][0]] = max(need.get(tok[d][0], 0), tok[d][1])
+        for k in need: wait(e, k, need[k])
+        for fn in x["calls"]:
+            if x["inc"] > 0: fn().then_inc(T.sem[s], x["inc"])
+            else: fn()
+            cnt[s] = cnt.get(s, 0) + abs(x["inc"])
+        tok[i] = (s, cnt[s])
+    cnt["sent"] = sent[0]
+    for s in cnt: wait("G", s, cnt[s])

import math
from concourse.bass import DstId, RemoteDMATransfer
from concourse.mybir import AluOpType as OP, ActivationFunctionType as AF

W = 2048; NR = 8; HOP = 3; R = 768
ROT = 32
U0 = 32; U1 = 96
R0 = 8
PK = 64 + 1024
LN2H = 0.693359375
H2 = [(0, 64), (64, 128)]
CFG = {
    "cp": H2,
    "gp": {},
    "rp": [(8, 56)], "sp": [(8, 24), (24, 40), (40, 56)],
    "wp": [(0, 32), (32, 64), (64, 96), (96, 128)],
    "fp": [(0, 32), (32, 64), (64, 96), (96, 120), (120, 128)],
    "send": [H2, H2, H2], "tp": H2, "home": [(0, 64), (64, 96), (96, 120), (120, 128)],
    "tm": "f2", "lo": "zns", "nadd": 1, "dv": 12, "fine": "uRklsi",
    "sg": ["0123", "12", "12", "123"],
    "vg": ["a0 c0", "", "", ""],
    "after": {"al1": "ft", "al2": "lr3", "al3": "fac0", "f2": "lr1_0"},
    "pc": -25, "pr": 12, "pw": 115, "ps": 100, "pu": [-5, 35, 60], "pt": 50, "pl": 8, "pn": 14,
    "cyc": 0.85e-3, "pe": 0.43e-3, "ga": 1.56, "sc": 3.8, "wake": 0.08, "fix": 2.2, "bw": 550e3, "fixv": 0.05, "fixs": 0.07, "gdma": 1.5, "gis": 0.8, "rbw": 450e3,
    "win": 0.05, "al": 0.2, "lead": 0.3,
    "ord": {
        "V": ["a0 s0 s1 s1c s1b s0c s0b o1 o0 c0 K0 z0 K2 z1 K1 i1 i0 K3 i0b i0c l0 l0b l0c l1 i1b l0d l1b i1c r0 m0 x0 S0 t0 x1 S1 t1 S2 f0 f1 k0 k1 v1+ f2 v0+",
              "s0 s0b s0c f3' o0 k3' s1 s1b s1c o1 k2' z0 i0 i0b i0c l0 z1 l0d l0b i1 l0c i1b l1 i1c r0 l1b m0 x0 S0 t0 x1 S1 t1 S2 e0 e1 f0 f1 k0 v0+ k1",
              "s0 s0b s0c e2' v1 o0 e3' s1 s1c s1b f3' o1 f2' z0 k2' i0 i0b l0 i0c k3' z1 l0b l0d i1 l0c i1b i1c r0 l1 m0 l1b x0 S0 t0 x1 S1 t1 S2 e0 e2 f0 f2 k0 v0+ k2",
              "s0 v1 s0b s0c e1' o0 f1' s1 s1c s1b k1' o1 e3' z0 i0 i0b i0c l0 z1 i1 i1b i1c l1 f3' l0b l1b k3' x0 t0 x1 e0 e1 t1 f0 f1 k0 k1 e2 f2 e3 k2 f3 k3 f3x k3x"],
        "S": ["M0 a1 u1 u1b M1 c1 N1 N0 u1b+ u1+ E0 d0 d1 g0 u1b++ u1++ g1 A0 A1 A2 A3", "a0 a1 c0 c1 d0 d1 g0 u1b++ u1++ g1 A2 A1",
              "a0 a1 c0 c1 d0 d1 g0 g1 A1 A2", "a0 a1 c0 c1 d0 d1 g0 g1 A1 A2 A3"],
        "P": ["K0 K1 u0 K3 u0b u0c u0d h0 K2 h1 u0+ o1 o0 u0b+ q1 u0c+ q0 y0 y1 u0d+ z1 z0 u0++ u0b++ u0c++ u0d++ g0 R1 R0 g1 x0 R2 x1 R1b R0b R2b R3 u0+++ u0b+++ R3b u0c+++",
              "h0 u0d++ o0 h1 o1 q0 y0 q1 z0 y1 z1 R0 g0 R1 g1 x0 R2 x1 R2b R0b R1b",
              "h0 R3' o0 h1 q0 R3b' o1 y0 z0 q1 y1 z1 g0 R1 g1 x0 R0 x1 R2 R0b R2b R3 R1b R3b",
              "h0 o0 h1 q0 o1 y0 q1 z0 y1 z1 R1 g0 g1 x0 R1b R0 x1 R0b R3 R2 R3b R2b"],
        "G": ["u1+ t0 t1 L0 W0 u1++ W1 u1+++", "t0 t1 L0 T0 W0 W1 T1", "t0 t1 L0 W0 T0 W1 T1", "W0 W1 W2 W3"]},
}

CFG.update(ct=1, dc=3, mid=1, ff=0.3, qs=0)
CFG["ord"] = {'V': ['C0 C1 Z0 C2 C3 Z2 Z1 Z3 C5 D1 s1 s1c s1b K2 s0 o1 s0b K0 s0c o0 c0 K1 z0 K3 i0 i0b z1 i0c D3 l0 C7 i1 l0b i1b l1 C6 i1c D2 r0 l0d l0c m0 x0 l1b t0 S0 x1 t1 S1 S2 f1 k1 f2 f0 k0 f3', "s0 v0 s0b s0c v1 o0 k3' s1 s1b s1c o1 k2' z0 i0 i0b i0c l0 l0b z1 l0c l0d i1 i1b i1c l1 r0 l1b m0 x0 S0 x1 t0 S1 t1 S2 e0 e1 f0 f1 k0 k1", "s0 v0 s0c s0b e2' o0 e3' s1 v1 s1c s1b f3' o1 f2' z0 k2' i0 i0b i0c k3' z1 l0 l0b i1 l0c i1b l0d l1 i1c l1b r0 x0 m0 t0 S0 x1 S1 t1 S2 e0 e2 v0+ f2 f0", "s0 v1 s0b s0c e1' o0 f1' k0' s1 s1b s1c k1' o1 z0 k2' i0 i0b l0 i0c e3' z1 f3' l0b i1 i1b i1c x0 k3' l1 t0 e1 l1b e0 f1 x1 f0 k1 k0 t1 e2 e3 f2 k2 f3 k3 f3x k3x"], 'S': ['C1 C2 a0 a1 C3 u1b u1 M0 c1 u1b+ u1+ M1 N0 d0 d1 g0 N1 g1 E0 A1 u1b++ A0 A2 A3 u1++', 'a0 a1 c0 c1 d0 d1 g0 g1 u1b++ A2 A1', 'a0 a1 c0 c1 d0 u1+ g0 d1 g1 A1 A2', 'a0 a1 c0 c1 d0 g0 d1 A1 g1 A2 A3'], 'P': ['u0 K1 K2 u0b u0c u0d h0 h1 K0 u0+ o1 u0b+ o0 u0c+ q0 u0d+ q1 K3 y0 y1 z0 z1 g0 g1 x0 u0++ u0b++ u0c++ x1 u0d++ R1 R0 R3 R1b R2 R2b R0b u0+++ R3b', 'h0 u0b++ o0 h1 q0 o1 y0 q1 z0 y1 z1 u0c++ R0 g0 u0d++ g1 x0 x1 R0b R1 R1b R3 R3b R2 R2b', 'h0 o0 h1 q0 o1 y0 q1 z0 y1 z1 g0 x0 R0 g1 x1 R1 R2 R2b R1b R3 R0b', "h0 o0 h1 q0 R3b' o1 y0 q1 z0 y1 z1 g0 R1 R1b x0 R0 R2 g1 R0b R3 R2b x1 R3b"], 'G': ['C0 C1 C4 C2 u1+ C3 t0 t1 L0 W0 W1', 't0 t1 u1+ L0 W0 T0 W1', "t0 u1+ t1 L0 T1' W0 T0 W1 T1 W0+ W1+ W2+ W3+", '']}

H4 = [(0, 32), (32, 64), (64, 96), (96, 128)]; H5 = [(0, 32), (32, 64), (64, 96), (96, 112), (112, 128)]
CFG.update({'fp': H5, 'send': [H4, H4, H4], 'tp': H4, 'home': H5, 'tm': 'f2', 'lo': 'zsnra', 'dv': 12, 'sg': ['01', '0123', '0123', '0123'], 'vg': ['a0 c0', '', '', ''],
            'after': {'al1': 'ft', 'al2': 'fac1', 'al3': 'fac0', 'f2': 'lr1_0'}, 'fix': 2.0, 'bw': 500e3, 'fixv': 0.06, 'gdma': 1.0, 'gis': 0.5, 'rbw': 500e3,
            'al': 0.3, 'ct': 1, 'dc': 0, 'mid': 2, 'ff': 0.3, 'qs': 0})
CFG["ord"] = {'V': ['C0 C1 C2 D1 C4 C3 D2 K2 C5 a0 s1 K1 s0 s0c K0 s1c s1b s0b o1 C6 o0 K3 c0 z0 C7 i0 i0b l0 i0c l0d z1 D3 i1 i1b l0b i1c l1 l0c r0 m0 x0 S0 x1 t0 l1b S1 t1 S2 e2 f1 f0 k0', "s0 s0b s0c k1' o0 f2' s1 s1c s1b k2' o1 e3' z0 f3' i0 i0b l0 i0c l0b z1 k3' i1 l0d i1b l0c i1c l1 r0 l1b m0 x0 S0 t0 x1 S1 t1 S2 e0 e1 f0 e2 k0", "s0 f1' s0c s0b k1' o0 s1 f2' s1b s1c e3' o1 k2' z0 f3' i0 i0b l0 i0c l0d z1 k3' i1 i1b l1 i1c l0b r0 l0c m0 x0 S0 t0 x1 l1b S1 t1 S2 e0 e1 f0 k0", "s0 s0c s0b f1' o0 k1' s1 s1b s1c e2' o1 f2' z0 k2' i0 i0b l0 i0c e3' l0b z1 f3' i1 i1b l1 i1c k3' x0 l1b t0 e0 e1 f0 x1 k0 f1 t1 k1 e2 f2 k2 e3 f3 k3 f3x k3x"], 'S': ['C1 C2 a1 u1 u1b M0 C3 M1 u1b+ u1+ N0 c1 N1 d0 d1 g0 u1b++ g1 E0 A0 j0 j1 A1', 'a0 a1 u1+ c0 c1 d0 d1 g0 u1b++ u1++ g1 j0 A1 A0 A2 j1', "a0 a1 A3' c0 c1 d0 d1 g0 g1 j0 A0 A1 j1 A2", "a0 a1 c0 A3' c1 d0 g0 d1 A0 g1 A1 A2 A3"], 'P': ['K2 K1 K0 u0 u0b u0c u0d h1 u0+ u0b+ h0 K3 o1 o0 u0c+ u0d+ q0 u0++ q1 y0 z0 y1 z1 u0b++ g0 u0c++ u0d++ g1 x0 x1 R3 R1 R1b R0 R0b R2', "h0 R2b' o0 h1 R3b' u0++ o1 q0 y0 u0b++ q1 z0 y1 z1 u0c++ g0 u0d++ R0 g1 x0 R1 x1 R0b R2 R1b R2b", "h0 R3' h1 o0 R3b' o1 q0 y0 z0 q1 y1 z1 g0 R0 g1 x0 x1 R0b R3 R1 R1b R2 R3b", "h0 o0 h1 R2b' q0 o1 y0 z0 q1 y1 z1 g0 R0 R0b x0 R1 R1b g1 R3 x1 R2 R2b R3b"], 'G': ['C0 C1 C3 C4 C2 u1+ t0 t1 j0 j1 L0 u1++ W0 W1 W2', "t0 W3' t1 j1 j0 L0 T1 T0 W0 W1 W2 W3 u1++ T3", "t0 j0 t1 T2' j1 L0 W0 W1 W2 T0 T2 W3 T3 T1 W0+ W1+ W2+ W3+ W4+", '']}

CFG.update(ydma=1.0, oq="YSYSY", lo="Sm Yc Yu Sz Ys Y0 Y1 Y2 Y3 Yr Ya"); CFG["after"]["al1"] = "ft3"
CFG["ord"] = {'V': ['C0 C1 C2 D1 C4 C3 C5 D2 a0 s1 K0 K1 s1b s0 s1c K2 s0c s0b o1 K3 o0 c0 C6 z0 i0 i0b C7 i0c z1 D3 i1 l0 i1b l0b i1c l0d r0 l1 l0c l1b m0 x0 S0 t0 x1 S1 t1 S2 e2 f0 f1 k0', "s0 s0c s0b k1' o0 f2' s1 s1b s1c k2' o1 e3' z0 f3' i0 i0b l0 i0c l0b l0d z1 k3' i1 i1b l0c i1c r0 l1 m0 l1b x0 S0 t0 x1 S1 t1 S2 e2 e0 f0 e1 k0", "s0 s0c s0b f1' o0 k1' s1 f2' s1b s1c e3' o1 k2' z0 f3' i0 i0b l0 i0c z1 k3' i1 l0b i1b l1 i1c l0c r0 l0d m0 x0 S0 t0 l1b x1 S1 t1 S2 e0 f0 e1 k0", "s0 s0b s0c f1' o0 k1' s1 e2' s1c s1b f2' o1 z0 k2' i0 i0b i0c e3' z1 l0 i1 f3' i1b l1 i1c l0b x0 k3' l1b t0 e0 e1 f0 x1 k0 f1 t1 k1 e2 f2 k2 e3 f3 k3 f3x k3x"], 'S': ['C1 C3 C2 a1 u1 u1b M0 M1 u1+ u1b+ c1 N1 N0 d0 d1 g0 E0 g1 u1b++ j0 A1 A0 j1 u1++', 'a0 a1 c0 c1 d0 d1 g0 g1 u1b++ u1++ A0 A1 j1 j0 A3', "a0 a1 A2' c0 c1 d0 d1 g0 g1 j0 A0 A1 j1 A2", "a0 a1 c0 A3' c1 d0 g0 d1 A0 g1 A1 A2 A3 O1 O3"], 'P': ['K0 K3 K2 K1 u0 u0b u0c u0d h1 u0+ u0b+ h0 u0c+ o1 o0 u0d+ q0 u0++ y0 q1 z0 y1 u0b++ z1 u0c++ g0 u0d++ g1 x0 R3 x1 R1 R1b R0 R0b R2 u0+++', "h0 R2b' o0 h1 R3b' o1 q0 y0 u0b++ z0 q1 y1 u0c++ z1 u0d++ g0 g1 x0 R2 R1 x1 R2b R0 R0b R1b", "h0 o0 h1 R3' R3b' q0 o1 y0 q1 z0 y1 z1 g0 g1 x0 R1 R0 x1 R1b R0b R2 R2b", "h0 o0 h1 R3' o1 q0 y0 q1 z0 R3b' y1 z1 g0 R0 R0b x0 R1 R1b g1 R2 x1 R3 R2b R3b"], 'G': ['C0 C1 C2 C3 C4 u1+ t0 j0 t1 j1 L0 u1++ W1 W0 W2 W3', 't0 t1 j0 j1 L0 T0 W0 T1 u1++ W2 W1 T3 W3', "t0 j0 t1 j1 L0 T2' W0 T0 W1 T1 W2 T2 W3 T3 W0+ W1+ W2+ W3+ W4+", '']}

CFG.update(pe0=20, sg=["12", "123", "12", "123"])
CFG["ord"] = {'V': ['C0 C1 C2 D2 C3 D1 C4 a0 s1 C5 s0 s0b K0 s0c s1c s1b o0 K2 D3 o1 c0 K1 C7 z0 K3 i0 i0b i0c z1 C6 l0 i1 l0b l0d i1b i1c l1 l0c r0 l1b m0 x0 S0 t0 x1 S1 t1 S2 e0 f0 k0 f1', "s0 s0b s0c k1' o0 f2' s1 s1c s1b k2' o1 e3' z0 f3' i0 i0b l0 i0c z1 k3' i1 l0b i1b i1c l0c l1 r0 l0d m0 l1b x0 S0 t0 x1 S1 t1 S2 e0 e2 f0 e1 k0", "s0 s0c s0b f1' o0 k1' f2' s1 s1c s1b e3' o1 k2' z0 f3' i0 i0b l0 i0c l0b z1 k3' i1 l0c i1b i1c l1 r0 l0d m0 l1b x0 S0 t0 x1 S1 t1 S2 e0 e1 f0 k0", "s0 s0b s0c f1' o0 e2' k1' s1 s1b s1c f2' o1 z0 k2' i0 i0b i0c e3' z1 f3' i1 l0 i1b l0b l1 i1c x0 k3' t0 l1b e0 f0 e1 x1 k0 f1 t1 k1 e2 f2 k2 e3 f3 k3 f3x k3x"], 'S': ['C1 a1 C2 u1 u1b M0 M1 C3 u1b+ u1+ c1 N0 N1 d0 d1 g0 E0 g1 j0 u1b++ A1 u1++ j1 A2', 'a0 a1 c0 c1 d0 d1 g0 g1 u1b++ u1++ j0 A1 j1 A2', "a0 a1 A3' c0 c1 d0 d1 g0 g1 A1 j0 A2 j1", 'a0 a1 c0 c1 d0 g0 d1 A1 g1 A2 A3 O1 O3'], 'P': ['K3 K0 K1 u0 K2 u0b u0c u0d h1 u0+ h0 u0b+ u0c+ o0 o1 u0d+ q0 q1 y0 z0 y1 u0++ z1 u0b++ u0c++ g0 u0d++ g1 x0 R0 x1 R0b R1 R2 R3 R2b R1b', "h0 u0++ o0 h1 R3b' o1 q0 y0 q1 z0 y1 z1 u0b++ u0c++ g0 u0d++ g1 x0 x1 R2 R2b R0 R0b R1 R1b R3", "h0 o0 h1 q0 R3b' o1 y0 z0 q1 y1 z1 g0 R1 g1 x0 R0 x1 R2 R1b R2b R0b R3 R3b", 'h0 o0 q0 h1 o1 y0 z0 q1 y1 z1 g0 R0 x0 R1 R0b R1b g1 R3 x1 R2 R2b R3b'], 'G': ['C0 C1 C3 C2 u1+ C4 t0 j0 t1 j1 L0 W1 W0 W2 u1++ W3', 't0 t1 j0 j1 L0 T0 W0 W1 W2 T1 u1++ T3 W3', "t0 T2' t1 j0 j1 L0 T0 W0 W1 T1 W2 T2 W3 T3 W0+ W1+ W2+ W3+ W4+", '']}

CFG.update(sg=["12", "12", "12", "123"])
CFG["ord"] = {'V': ['C0 C1 C2 C3 C5 C4 a0 s1 D1 K0 s0 D2 s0c s0b D3 s1b s1c o0 K2 K1 o1 c0 K3 C7 z0 i0 i0b l0 i0c z1 i1 C6 i1b l0b l1 i1c l1b l0c r0 l0d m0 x0 S0 t0 x1 S1 t1 S2 e0 f1 f0 k1 f2', "s0 s0c s0b k0' o0 s1 s1c s1b k2' o1 e3' z0 f3' i0 i0b l0 i0c l0b z1 k3' i1 i1b l0c i1c l1 l0d l1b r0 m0 x0 S0 t0 x1 S1 t1 S2 e0 e2 e1 f0 f2 k0", "s0 s0c s0b f1' o0 k1' s1 s1c s1b e3' o1 k2' z0 f3' i0 i0b i0c l0 l0b z1 k3' i1 i1b l1 i1c r0 l0c l0d l1b m0 x0 S0 t0 x1 S1 t1 S2 e0 f0 e1 k0", "s0 s0b s0c f1' o0 k1' s1 s1b s1c e2' o1 f2' z0 k2' i0 i0b i0c e3' z1 f3' l0 i1 l1 i1b l0b i1c x0 k3' t0 e0 l1b f0 e1 k0 x1 f1 t1 k1 e2 f2 k2 e3 f3 k3 f3x k3x"], 'S': ['C1 C2 a1 u1 u1b M0 M1 N0 u1b+ u1+ c1 C3 N1 d0 d1 g0 E0 g1 j0 u1++ A1 u1b++ j1 A2', 'a0 a1 c0 c1 d0 d1 g0 u1b++ u1++ g1 j0 A1 A2 j1', 'a0 a1 c0 c1 d0 d1 g0 g1 j0 A1 j1 A2', 'a0 a1 c0 c1 d0 g0 d1 A1 g1 A2 A3 O1 O3'], 'P': ['K2 K0 K1 K3 u0 u0b u0c u0d h1 h0 u0+ o0 u0b+ u0c+ o1 u0d+ q0 q1 y0 u0++ z0 y1 u0b++ z1 g0 g1 x0 u0c++ u0d++ R0 x1 R1 R2 R2b R1b R0b R3 R3b', 'h0 o0 h1 u0++ o1 q0 y0 q1 z0 y1 u0b++ z1 u0c++ u0d++ g0 R0 g1 x0 R2 x1 R2b R1 R1b R0b R3', "h0 o0 h1 R3b' o1 q0 y0 q1 z0 y1 z1 R0 R1 g0 g1 x0 R0b x1 R2 R2b R1b", "h0 o0 h1 q0 R3' o1 y0 q1 z0 y1 R3b' z1 g0 R0 x0 R1 R0b R1b g1 R2 x1 R2b R3 R3b"], 'G': ['C0 C1 C3 C2 u1+ C4 t0 j0 t1 j1 L0 W0 W1 W2 u1++ W3', 't0 t1 j0 j1 L0 T0 W0 W1 W2 T1 u1++ T3 W3', "t0 T2' t1 j0 j1 L0 T0 W0 W1 T1 W2 T2 W3 T3 W0+ W1+ W2+ W3+ W4+", '']}

CFG["ord"]["V"][0] = "C0 C1 C2 D2 C3 D1 C4 a0 s1 C5 s0 s0b K0 s0c s1c s1b o0 K2 D3 o1 c0 K1 C7 z0 K3 i0 i0b i0c z1 C6 l0 i1 l0b l0d i1b i1c l1 l0c r0 l1b m0 x0 S0 t0 x1 S1 t1 S2 e0 f1 f0 k1 f2"
CFG["ord"]["S"][0] = "C1 a1 C2 u1 u1b M0 M1 C3 u1b+ u1+ c1 N0 N1 d0 d1 g0 E0 g1 j0 u1b++ A1 u1++ j1 A2"
CFG["ord"]["P"][0] = "K3 K0 K1 u0 K2 u0b u0c u0d h1 u0+ h0 u0b+ u0c+ o0 o1 u0d+ q0 q1 y0 z0 y1 u0++ z1 u0b++ u0c++ g0 u0d++ g1 x0 R0 x1 R0b R1 R1b R2 R2b R3 R3b"
CFG["ord"]["G"][0] = "C0 C1 C3 C2 u1+ C4 t0 j0 t1 j1 L0 W1 W0 W2 u1++ W3"

SCRATCH = {
    "io": ("sbuf", [128, 400], "int32"), "ia": ("sbuf", [128, 416], "int32"),
    "rm": ("sbuf", [128, 16], "float32"), "m4": ("sbuf", [128, 4], "float32"), "mz": ("sbuf", [128, 4], "float32"), "cl": ("sbuf", [128, 4], "float32"),
    "iw": ("sbuf", [128, 192], "bfloat16"), "ir": ("sbuf", [128, 192], "bfloat16"), "nw": ("sbuf", [128, 192], "bfloat16"), "kw": ("sbuf", [128, 192], "bfloat16"),
    "hw": ("sbuf", [128, 192], "float16"), "h2": ("sbuf", [128, 144], "bfloat16"), "cq": ("sbuf", [128, 128], "bfloat16"),
    "nv": ("sbuf", [128, 192], "bfloat16"), "cz": ("sbuf", [128, 128], "bfloat16"),
    "fk": ("sbuf", [128, 128], "float32"), "rw": ("sbuf", [128, 140], "float16"), "on": ("sbuf", [128, 512], "bfloat16"), "ok": ("sbuf", [128, 128], "bfloat16"),
    "zw": ("sbuf", [128, 4, 192], "bfloat16"), "sq": ("sbuf", [128, 4, 128], "bfloat16"), "dq": ("sbuf", [128, 4, 128], "bfloat16"),
    "bw": ("sbuf", [128, 16, 176], "bfloat16"), "dd": ("sbuf", [128, 16, 128], "bfloat16"),
    "cei": ("sbuf", [128, 128], "int32"), "rpi": ("sbuf", [128, 144], "int32"), "rp2": ("sbuf", [128, 144], "int32"),
    "uz": ("sbuf", [128, W], "bfloat16"),
    "mt": ("sbuf", [128, W], "bfloat16"), "st": ("sbuf", [128, W], "bfloat16"), "rt": ("sbuf", [128, W], "bfloat16"),
    "ft": ("sbuf", [128, 4 * W], "bfloat16"), "at": ("sbuf", [128, 4, W + 16], "bfloat16"),
    "mg": ("sbuf", [128, W], "bfloat16"), "cg": ("sbuf", [128, W], "bfloat16"), "ag": ("sbuf", [128, W], "bfloat16"),
    "zc": ("sbuf", [128, 512], "float16"),
    "xf": ("sbuf", [128, 128], "float32"), "pb": ("sbuf", [128, 128], "bfloat16"), "qo": ("sbuf", [128, 128], "bfloat16"), "of": ("sbuf", [128, 128], "uint16"),
    "ci": ("sbuf", [128, 128], "int32"), "cm": ("sbuf", [128, 128], "int32"), "du": ("sbuf", [128, 128], "uint16"),
    "par": ("sbuf", [128, 128], "int32"), "lo": ("sbuf", [128, 128], "float16"), "xx": ("sbuf", [128, 128], "bfloat16"),
    "ei": ("sbuf", [128, 48], "int32"), "eu": ("sbuf", [128, 48], "uint16"),
    "fac": ("sbuf", [128, R], "float16"), "mn": ("sbuf", [128, R], "float32"), "mlo": ("sbuf", [128, 384], "float32"),
    "lm": ("sbuf", [128, W], "float32"), "lr1": ("sbuf", [128, W], "float32"), "lr2": ("sbuf", [128, W], "float32"), "lr3": ("sbuf", [128, W], "float32"),
    "fl": ("sbuf", [128, W], "float32"), "ta": ("sbuf", [128, W], "float32"), "tb": ("sbuf", [128, W], "float32"),
}
for _t in range(4):
    SCRATCH["pk%d" % _t] = ("sbuf", [128, 2, PK], "bfloat16")
    SCRATCH["cu%d" % _t] = ("sbuf", [128, 128], "uint16")
    SCRATCH["cx%d" % _t] = ("sbuf", [128, 2, 128], "uint16")
    SCRATCH["cf%d" % _t] = ("sbuf", [128, 128], "float32")
    SCRATCH["wo%d" % _t] = ("sbuf", [128, W], "float32")
    SCRATCH["uo%d" % _t] = ("sbuf", [128, 2, 128], "bfloat16")
    if _t:
        SCRATCH["ul%d" % _t] = ("sbuf", [128, 2, 128], "bfloat16")
        SCRATCH["ct%d" % _t] = ("sbuf", [128, 128], "float32")
        SCRATCH["wi%d" % _t] = ("sbuf", [128, W], "float32")
for _b in range(8):
    SCRATCH["b%d" % _b] = ("psum", [128, 4, 128] if _b == 3 else [128, 512], "float32")

SEMAPHORES = (["eV", "eS", "eP", "eG", "sent", "outs"]
              + ["l_" + n for n in ("cei", "u8", "mt", "ft0", "ft1", "ft2", "ft3", "st", "z8", "rpi", "at0", "al1", "al2", "al3")]
              + ["%s%d" % (n, t) for n in ("aU", "cL") for t in (1, 2, 3)] + ["sL%d_%d" % (t, j) for t in (1, 2, 3) for j in range(2)]
              + ["%s%d_%d" % (n, t, k) for n in ("aC", "aD", "aW", "aT", "aM") for t in (1, 2, 3) for k in range(4)] + ["aF%d" % k for k in range(6)])


def order_of(nodes, first):
    C = CFG; n = len(nodes); wake = C["wake"]
    pred = [x["deps"] | x.get("soft", set()) for x in nodes]
    succ = [[] for _ in nodes]; left = [len(p) for p in pred]
    for i in range(n):
        for d in pred[i]: succ[d].append(i)
    tail = [-x["rank"] for x in nodes]
    for i in range(n - 1, -1, -1):
        if not C["ord"]: tail[i] = max([tail[i]] + [tail[j] for j in succ[i]])
        elif not nodes[i]["tag"]: tail[i] = max([-999] + [tail[j] for j in succ[i]])
    ready = {e: {} for e in "VSPGY"}; free = {e: 0.0 for e in ready}; fin = [0.0] * n; dma = 0.0; out = []
    for i in range(n):
        if not left[i]: ready[nodes[i]["e"]][i] = 0.0
    def at(q, j):
        return max(ready[q][j], dma - 0.7 * C["fix"] - C["lead"]) if nodes[j]["dma"] else ready[q][j]
    while len(out) < n:
        if len(out) < first:
            i = len(out); e = nodes[i]["e"]
        else:
            e = min((q for q in ready if ready[q]), key=lambda q: max(free[q], min(at(q, j) for j in ready[q])))
            t0 = max(free[e], min(at(e, j) for j in ready[e]))
            i = max((j for j in ready[e] if at(e, j) <= t0 + C["win"]), key=lambda j: (tail[j], -j))
            d = max(nodes[i]["dur"], nodes[i]["dma"])
            for j in ready[e]:
                if tail[j] > tail[i] and at(e, j) <= t0 + C["al"] * d: i = j
        x = nodes[i]; t = max(free[e], ready[e].pop(i)); free[e] = fin[i] = t + x["dur"]
        if x["dma"]:
            dma = max(t + 0.7 * C["fix"], dma) + x["dma"]; fin[i] = dma + 0.3 * C["fix"]
        out.append(i)
        for j in succ[i]:
            left[j] -= 1
            if not left[j]:
                q = nodes[j]["e"]
                ready[q][j] = max([fin[d] + (0.0 if q == nodes[d]["e"] == "P" else wake) for d in nodes[j]["deps"]] + [0.0])
    return out


def rank_program(g, core, T, topo):
    rank = T.rank_of(core)
    if rank is None:
        return
    C = CFG; CP = C["cp"]; WP = C["wp"]
    qs = {"V": g.vector, "S": g.scalar, "P": g.tensor, "G": g, "Y": g.sync}
    nodes = []; wr = {}; rd = {}; pr = [999]; sent = [0]; tag = [None]

    def node(e, reads, writes, dur, calls, sem=None, dma=0.0, inc=1):
        deps = set()
        for k in reads:
            if k in wr: deps.add(wr[k])
            if k[0] == "b" and len(k) == 2:
                deps.update(j for j in rd.get(k, []) if nodes[j]["e"] != e)
        for k in writes:
            if k in wr: deps.add(wr[k])
            deps.update(rd.get(k, []))
        for k in reads: rd.setdefault(k, []).append(len(nodes))
        for k in writes:
            wr[k] = len(nodes); rd[k] = []
        nodes.append({"e": e, "deps": deps, "dur": dur, "calls": calls, "sem": sem or "e" + e, "dma": dma, "inc": inc, "rank": pr[0], "tag": tag[0]})

    def dmas(e, sem, reads, writes, size, pairs, **kw):
        node(e, reads, writes, (C["gdma"] if e == "G" else C["ydma"]) * len(pairs), [(lambda o=o, i=i: qs[e].dma_start(o, i, **kw)) for o, i in pairs],
             sem, size / C["bw"] * (2 if kw else 1), 16)

    def send(hops, sem, reads, writes, size, dst, srcs, fold=1, more=()):
        dsts = [(hops, dst)] + list(more); to = [T.cores[(rank + h) % NR] for h, _ in dsts]
        m = topo.mask(core, to[0])
        for x in to: m &= topo.mask(core, x)
        ne = bin(m).count("1")
        def call():
            if len(srcs) == 1:
                g.remote_dma(dst, srcs[0], T.sem[sem], T.sem.sent, topo.addr(to[0])[1], topo.addr(to[0])[0], m)
            else:
                g.remote_dma_fused([RemoteDMATransfer(dst_ids=[DstId(rid=topo.addr(x)[0], pnc=topo.addr(x)[1]) for x in to], dma_engine_mask=m,
                                                      remote_sem=T.sem[sem], srcs=srcs, dsts=[d for _, d in dsts], alu_op=fold)], local_sem=T.sem.sent)
        node("G", reads, writes, C["gis"] + (0 if sent[0] else 2), [call], sem, size * (len(dsts) + C["ff"] * (len(srcs) - 1)) / C["rbw"] + 0.05, -ne * len(dsts))
        sent[0] += ne

    V = g.vector; S = g.scalar; P = g.tensor; cyc = C["cyc"]
    def name(t, k): tag[0] = (t, k)
    def vs(e, r, w, n, fn): node(e, r, w, n * cyc + C["fixv" if e == "V" else "fixs"], [fn])
    def ts(o, i, a, b, o0, o1, r, w, n=16):
        if o1 is None: vs("V", r, w, n, lambda: V.tensor_scalar(o, i, a, None, o0))
        else: vs("V", r, w, n, lambda: V.tensor_scalar(o, i, a, b, o0, o1))
    def tt(o, a, b, o0, r, w, n=16): vs("V", r, w, n, lambda: V.tensor_tensor(o, a, b, o0))
    def cp(o, i, r, w, n=16): vs("V", r, w, n, lambda: V.tensor_copy(o, i))
    def fill_(o, v, w, n=16): vs("V", [], w, n, lambda: V.memset(o, v))
    def act(o, i, f, r, w, n=16, **kw): vs("S", r, w, n, lambda: S.activation(o, i, f, **kw))
    def mms(l, r, w, n): node("P", r, w, n * C["pe"], [(lambda x=x: P.matmul(*x)) for x in l])
    def iota(o, pat, base, ch, w, n): node("G", [], w, 0.13 + 2 * n * cyc, [lambda: g.iota(o, pat, base, ch)])
    def pick(o, i, pat, base, r, w, n): node("G", r, w, 0.17 + 2 * n * cyc, [lambda: g.affine_select(o, i, pat, OP.is_equal, 0.0, base, 1)])
    def B(b): return T["b%d" % b]
    def ks(n, p): return ["%s:%d" % (n, j) for j in range(p[0] // 8, (p[1] + 7) // 8)]
    def lc(p): return slice(p[0], p[1])
    def wc(p): return slice(16 * p[0], 16 * p[1])
    def wn(p): return 16 * (p[1] - p[0])
    def gn(p): return wn(p) * C["ga"]
    def up(p): return U0 <= p[0] < U1
    def cut(p, at): return [(a, b) for a, b in zip([p[0]] + [x for x in at if p[0] < x < p[1]], [x for x in at if p[0] < x < p[1]] + [p[1]])]
    def after(k): return [C["after"][k]] if k in C["after"] else []
    ALL = (0, 128); HALF = 128 * W * 2

    LOADS = {"c": ("cei", 65536, T.cei[:], T.ce), "m": ("mt", HALF, T.mt[:], T.mj), "u": ("u8", HALF // 4, T.uz[0:32, :], T.uu),
             "z": ("z8", HALF // 4, T.uz[64:96, :], T.zz), "s": ("st", HALF, T.st[:], T.sg), "r": ("rpi", 73728, T.rpi[:], T.rp), "a": ("at0", HALF, T.at[:, 0, 0:W], T.al)}
    for j in range(4):
        LOADS[str(j)] = ("ft%d" % j, HALF, T.ft[j:128:4, :], T.nx)
    for e, x in C["lo"].split():
        k, n, o, i = LOADS[x]; dmas(e, "l_" + k, [], [k], n, [(o, i[:])])
    first = len(nodes)
    def load_al(t):
        n = 16 * t
        dmas("Y", "l_al%d" % t, after("al%d" % t), ["at%d" % t], HALF, [(T.at[0:128 - n, t, 0:W], T.al[n:128, :]), (T.at[128 - n:128, t, 0:W], T.al[0:n, :])])

    IO = T["io"]; IA = T.ia; AND = OP.bitwise_and; EQ = OP.is_equal; ID = T.iw[:, 16:144]; dv = C["dv"]
    name(0, "C0")
    fill_(T.on[:], 1.0, ["on"], 256)
    fill_(T.ok[:], 128.0, ["ok"], 64)
    fill_(T.mz[0:64, :], 1.0, ["mz0"]); fill_(T.mz[64:128, :], -1.0 / 128, ["mz1"])
    iota(IO[:, 16:208], [[1, 192]], 240, -1, ["ioC"], 192)
    iota(IO[:, 0:16], [[-1, 16]], 16, 1, ["ioA"], 16)
    iota(IO[:, 208:400], [[1, 192]], 512 - 63, -4, ["ioD"], 192)
    name(0, "C1")
    for i in range(dv, 16, 4):
        pick(T.dd[:, i:i + 4, :], T.on[:], [[-256, 4], [-16, 8], [255, 16]], -256 * i, ["on"], ["dd%d" % j for j in range(i, i + 4)], 512)
    ts(IA[:, 16:208], IO[:, 16:208], 127, None, AND, None, ["ioC"], ["iaC"], 192)
    ts(IA[:, 400:404], IO[:, 0:4], 3, None, AND, None, ["ioA"], ["ia3"])
    ts(T.iw[:], IA[:, 16:208], 0.0, None, EQ, None, ["iaC"], ["iw"], 192)
    ts(T.m4[:], IA[:, 400:404], 0.0, None, EQ, None, ["ia3"], ["m4"])
    for o, i, sc, k, n in ((T.fk[:], ID, W, "fk", 128), (T.kw[:], T.iw[:], W, "kw", 192), (T.nv[:], T.iw[:], -W, "nv", 192), (T.cz[:], ID, -128 * 768, "cz", 128)):
        act(o, i, AF.Copy, ["iw"], [k], n, scale=float(sc))
    name(0, "C2")
    for b in range(4):
        pick(T.sq[:, b, :], T.ok[:], [[-16, 8], [0, 4], [-1, 4]], -4 * b, ["ok"], ["sq%d" % b], 128)
    ts(IA[:, 208:400], IO[:, 208:400], 127, None, AND, None, ["ioD"], ["iaD"], 192)
    tt(T.mz[:], T.mz[:], T.m4[:], OP.mult, ["m4", "mz0", "mz1"], ["mz"])
    for a in range(4): act(T.dq[:, a, :], T.iw[:, 16 - a:144 - a], AF.Copy, ["iw", "m4"], ["dq%d" % a], 128, scale=T.m4[:, 0:1])
    act(T.cq[:], ID, AF.Copy, ["iw"], ["cq"], 128, scale=-128.0)
    for t in range(4):
        ts(T.zw[:, t, :], IA[:, 208:400], float(-4 * t % 128), T.mz[:, t:t + 1], EQ, OP.mult, ["iaD", "mz"], ["zw%d" % t], 192)
        name(0, "D%d" % (t + 1))
    name(0, "C3")
    for i in range(0, 16, 4):
        pick(T.bw[:, i:i + 4, 0:128], T.on[:], [[-1, 4], [-16, 8], [0, 16]], -i, ["on"], ["bw%d" % i], 512)
    cp(T.cu0[:, 0:128 - ROT], T.cei[:, ROT:128], ["cei"], ks("cu0", (0, 128 - ROT)), 96)
    cp(T.cu0[:, 128 - ROT:128], T.cei[:, 0:ROT], ["cei"], ks("cu0", (128 - ROT, 128)), 32)
    ts(T.cf0[:], T.cu0[:], 1.0 / W, None, OP.mult, None, ks("cu0", ALL), ks("cf0", ALL), 128)
    act(T.nw[:], T.iw[:], AF.Copy, ["iw"], ["nw"], 192, scale=-1.0)
    act(T.h2[:], T.iw[:, 0:144], AF.Copy, ["iw"], ["h2"], 144, scale=0.5)
    name(0, "C4")
    for i in range(0, 16, 8):
        pick(T.bw[:, i:i + 8, 128:176], T.on[:, 0:384], [[-1, 8], [-16, 3], [0, 16]], -i, ["on"], ["bx%d" % i], 384)
    if dv:
        ts(IA[:, 0:16], IO[:, 0:16], 15, None, AND, None, ["ioA"], ["iaA"])
        ts(T.rm[:], IA[:, 0:16], 0.0, None, EQ, None, ["iaA"], ["rm"])
    for i in range(dv): ts(T.dd[:, i, :], ID, T.rm[:, i:i + 1], None, OP.mult, None, ["iw", "rm"], ["dd%d" % i], 64)
    name(0, "C5")
    ts(IA[:, 404:405], IO[:, 0:1], 12, None, AND, None, ["ioA"], ["ia12"])
    cp(T.hw[:], T.iw[:], ["iw"], ["hw"], 96)
    cp(T.cl[:, 0:1], IA[:, 404:405], ["ia12"], ["q4"])
    ts(T.cl[:, 1:2], IA[:, 404:405], 128.0, -256.0, OP.mult, OP.add, ["ia12"], ["cl1"])
    ts(T.cl[:, 2:3], IA[:, 404:405], 128.0, 256.0, OP.mult, OP.add, ["ia12"], ["cl2"])
    ts(T.rw[:], IO[:, 16:156], T.cl[:, 0:1], 252.0, OP.add, EQ, ["ioC", "q4"], ["rw"], 140)
    name(0, "C6")
    nlo = max(wn(h) for h in C["sp"])
    fill_(T.mlo[:, 0:nlo], math.log(0.0625), ["mlo"], nlo)
    fill_(T.at[:, :, W:W + 16], -1.0, ["ax"], 32)
    name(0, "C8")
    if C["dc"]: fill_(T.lob[:], 0.125, ["lob"], 512); fill_(T.hib[:], 4.0, ["hib"], 512)
    name(0, "C7")
    ts(T.rp2[:], T.rpi[:], 2.0, None, OP.mult, None, ["rpi"], ["rp2"], 144)
    DD = ["dd%d" % i for i in range(16)]; BW = ["bw0", "bw4", "bw8", "bw12", "bx0", "bx8"]

    for q in range(4):
        c = slice(512 * q, 512 * q + 512); b = 4 + q; name(0, "K%d" % q)
        mms([(B(b)[:], ID, T.mt[:, c], True, True)], ["iw", "mt"], ["b%d" % b], 512)
        tt(T.rt[:, c], T.st[:, c], B(b)[:], OP.mult, ["st", "b%d" % b], ["rt%d" % q], 512)
    pr[0] = C["pl"]
    for h in range(2):
        c = slice(1024 * h, 1024 * h + 1024); name(0, "M%d" % h)
        act(T.lm[:, c], T.mt[:, c], AF.Ln, ["mt", "fn"], ["lm%d" % h], 1024 + (0 if h else 1500))
    pr[0] = C["pn"]
    for h in range(2):
        c = slice(1024 * h, 1024 * h + 1024); name(0, "N%d" % h)
        act(T.lr3[:, c], T.st[:, c], AF.Ln, ["st", "fn", "lm0"], ["ls%d" % h] + (["lr3"] if h else []), 1024, bias=1e-18)
    def exp_():
        name(0, "E0"); pr[0] = C["pe0"]
        act(T.ir[:], T.iw[:], AF.Exp, ["iw"] + after("e0"), ["ir", "fn", "fx"], 2000, scale=100.0, bias=-100.0)
    pr[0] = 999; tag[0] = None
    def fill(t): dmas("Y", "cL%d" % t, ["ls0", "ls1", "lr3"] + after("f%d" % t), ["lr%d" % t], 2 * HALF, [(T["lr%d" % t][:], T.lr3[:])])
    LM = ["lm0", "lm1"]

    def uz_(t):
        n = 64 if t else 128; uo = "uo%d" % t; name(t, "u0")
        for j in range(2):
            p0 = 64 * j
            for h in range(2 if t else 1):
                for i0 in range(0, 16, 16 if t else 8):
                    mms([(B(3)[:, j, n * h:n * h + n], T.zw[p0:p0 + 32, t, 63 - 16 * t * h - i:191 - 16 * t * h - i],
                          T.uz[p0:p0 + 32, 16 * n * h + i:16 * n * (h + 1):16], i == 0, i == 15) for i in range(i0, i0 + (16 if t else 8))],
                        ["zw%d" % t, "z8" if j else "u8"], ["b3"], 1024)
                    nodes[-1]["own"] = j == 1 and h == i0 == 0
        name(t, "u1")
        act(T[uo][:, :, 0:128 - ROT], B(3)[:, 0:2, ROT:128], AF.Copy, ["b3"], [uo + "a"], 192)
        act(T[uo][:, :, 128 - ROT:128], B(3)[:, 0:2, 0:ROT], AF.Copy, ["b3"], [uo + "b"], 64)
        if t: send(HOP * t, "aU%d" % t, [uo + "a", uo + "b"], ["ul%d" % t], 65536, T["ul%d" % t][:], [T[uo][:]])
    def ul(t, j, p): return (T["ul%d" % t] if t else T.uo0)[:, j, lc(p)], (["ul%d" % t] if t else ["uo0a", "uo0b"])

    def gather(t, tok, p, out, win, off, f, r, w, sc=1.0, bias=0.0):
        for h in cut(p, C["gp"].get(tok[0], [])):
            o = out(h); x = win.indirect(off[:, lc(h)]); k = ks(w, h)
            if f == AF.Exp: act(o, x, f, r + ["fx"], k, gn(h), bias=bias)
            elif "%s%d" % (tok[0], h[0]) not in C["vg"][t].split(): act(o, x, f, r, k, gn(h), scale=sc)
            elif sc == 1.0: cp(o, x, r, k, gn(h))
            else: ts(o, x, sc, None, OP.mult, None, r, k, gn(h))
    def hero(src, k, first): return [(B(k)[:, 0:64], T.dd[:, i, :], src(i), first and i == 0, i == 15) for i in range(16)]
    def sr_(b, p): return T[b][:, p[0] // 64, p[0] % 64:p[0] % 64 + p[1] - p[0]]
    def rho(b, p): return T[b][:, p[0] // 64, 64 + 16 * (p[0] % 64):64 + 16 * (p[0] % 64) + wn(p)]
    def alp(b, p): return T.ag[:, wc(p)]
    def way(t, k):
        p = CP[k]; c = lc(p); n = p[1] - p[0]; s = str(k); b = "b" + s; cu = "cu%d" % t; cf = "cf%d" % t; n64 = max(n, 64)
        name(t, "a" + s)
        if t == 0: gather(t, "a", p, lambda h: T.mg[:, wc(h)], T.mt[:], T[cu], AF.Copy, ks(cu, p) + ["mt"], "mg")
        else: gather(t, "a", p, lambda h: T.mg[:, wc(h)], T.lm[:], T[cu], AF.Exp, ks(cu, p) + LM, "mg", bias=3.2e-4)
        name(t, "h" + s)
        mms(hero(lambda i: T.mg[:, 16 * p[0] + i:16 * p[1]:16], k, True), DD + ks("mg", p), [b], 16 * n64)
        u, ur = ul(t, 0, p)
        name(t, "v" + s)
        if t and not C["ct"]: ts(T[cf][:, c], T[cu][:, c], 1.0 / W, None, OP.mult, None, ks(cu, p), ks(cf, p), n)
        name(t, "s" + s)
        tt(T.xf[:, c], B(k)[:, 0:n], u, OP.mult, [b] + ur, ["xf" + s], n)
        ts(T.pb[:, c], T.xf[:, c], 15.0, 191.53125, OP.min, OP.add, ["xf" + s], ["pb" + s], n)
        if C["qs"]: act(T.qo[:, c], T.pb[:, c], AF.Identity, ["pb" + s], ["qo" + s], n, bias=574.5)
        else: ts(T.qo[:, c], T.xf[:, c], 15.0, 766.03125, OP.min, OP.add, ["xf" + s], ["qo" + s], n)
        o = B(k)[:, 400:400 + n]; z = B(k)[:, 80:80 + 4 * n]
        name(t, "o" + s)
        mms([(o, T.fk[:], T[cf][:, c], True, False), (o, T.kw[:, 16:144], T.pb[:, c], False, False), (o, T.nv[:, 16:144], T.qo[:, c], False, True)],
            ["fk", "kw", "nv", "pb" + s, "qo" + s] + ks(cf, p), [b], 6 * n64)
        ts(T.of[:, c], o, 576.0 * W, None, OP.add, None, [b], ["of" + s], n)
        name(t, "q" + s)
        mms([(z, T.cz[:], T.on[:, 0:4 * n], True, False)] + [(B(k)[:, 80 + j:80 + 4 * n:4], T.sq[:, j, :], T.qo[:, c], False, False) for j in range(4)],
            ["sq%d" % j for j in range(4)] + ["cz", "on", "qo" + s], [b], 4 * n64 + 4 * n)
        name(t, "c" + s)
        gather(t, "c", p, lambda h: T.cg[:, wc(h)], T.ft[:], T.of, AF.Copy, ["ft0", "ft1", "ft2", "ft3", "of" + s], "cg")
        name(t, "y" + s)
        mms([(z, T.dq[:, a, :], T.cg[:, 16 * p[0] + a:16 * p[1]:4], False, a == 3) for a in range(4)], ["dq%d" % a for a in range(4)] + ks("cg", p), [b], 16 * n)
        name(t, "z" + s)
        ts(T.zc[:, 4 * p[0]:4 * p[1]], z, T.cl[:, 1:2], T.cl[:, 2:3], OP.max, OP.min, [b, "cl1", "cl2"], ["zc" + s], 4 * n)
        o = B(k)[:, 0:n]
        mms([(o, T.fk[:], T[cf][:, c], True, False), (o, T.cq[:], T.qo[:, c], False, False)]
            + [(o, T.rw[:, 12 - 4 * j:140 - 4 * j], T.zc[:, 4 * p[0] + j:4 * p[1]:4], False, j == 3) for j in range(4)],
            ["fk", "cq", "rw", "qo" + s, "zc" + s] + ks(cf, p), [b], 9 * n64)
        name(t, "i" + s)
        ts(T.ci[:, c], o, 128.0 * 768 - 256, None, OP.add, None, [b], ["ci" + s], n)
        ts(T.cm[:, c], T.ci[:, c], W - 1, None, AND, None, ["ci" + s], ["cm" + s], n)
        cp(T.du[:, c], T.cm[:, c], ["cm" + s], ["du" + s], n)
        name(t, "l" + s)
        ts(T.par[:, c], T.ci[:, c], 1, None, AND, None, ["ci" + s], ["par" + s], n)
        if k == 0 and t < 3:
            tt(T.ei[:], T.par[:, R0:R0 + 48], T.rp2[:, 48 * t:48 * t + 48], OP.add, ["par0", "rp2"], ["ei"], 96)
            cp(T.eu[:], T.ei[:], ["ei"], ["eu"], 48)
        tt(T.lo[:, c], T.cm[:, c], T.par[:, c], OP.subtract, ["cm" + s, "par" + s], ["lo" + s], 2 * n)
    def collide(t, k):
        p = CP[k]; c = lc(p); n = p[1] - p[0]; s = str(k); b = "b" + s; pk = "pk%d" % t; rg = "rg%d" % t; sr = "sr%d" % t; m = t + 1; n64 = max(n, 64)
        name(t, "d" + s)
        if t == 0: gather(t, "d", p, lambda h: rho(pk, h), T.rt[:], T.du, AF.Copy, ["rt0", "rt1", "rt2", "rt3", "du" + s], rg, sc=2.0)
        else: gather(t, "d", p, lambda h: rho(pk, h), T["lr%d" % t][:], T.du, AF.Exp, ["lr%d_%d" % (t, j) for j in range(C["nadd"])] + ["du" + s], rg, bias=math.log(2.0) + 3.2e-4)
        z, zr = ul(t, 1, p)
        name(t, "g" + s)
        mms([(B(k)[:, 0:n], ID, z, True, False)] + hero(lambda i: T[pk][:, k, 64 + i:1088:16], k, False), DD + ["iw"] + zr + ks(rg, p), [b], 17 * n64)
        act(sr_(pk, p), B(k)[:, 0:n], AF.Sign, [b], ks(sr, p), n, bias=-1.0 / 256)
        name(t, "x" + s)
        tt(T.xx[:, c], T.par[:, c], sr_(pk, p), OP.mult, ["par" + s] + ks(sr, p), ["xx" + s], 2 * n)
        l = []
        for h in cut(p, [U0, U1]) if t < 3 else []:
            o = B(k)[:, 80 + h[0] - p[0]:80 + h[1] - p[0]]; j = 0 if up(h) else 16
            l += [(o, T.hw[:, j:j + 128], T.lo[:, lc(h)], True, False), (o, T.h2[:, 16:144], T.on[:, lc(h)], False, False),
                  (o, T.h2[:, j:j + 128], sr_(pk, h), False, False), (o, T.nw[:, j:j + 128], T.xx[:, lc(h)], False, True)]
        for h in cut(p, [U0, U1] if t else []):
            o = B(k)[:, 80 + n + h[0] - p[0]:80 + n + h[1] - p[0]]; j = 16 + (16 * t if up(h) else 0)
            l += [(o, T.hw[:, j:j + 128], T.lo[:, lc(h)], True, False), (o, T.kw[:, 16:144], T.on[:, lc(h)], False, False),
                  (o, T.iw[:, j:j + 128], T.xx[:, lc(h)], False, False), (o, T.nv[:, j:j + 128], sr_(pk, h), False, True)]
        mms(l, ["hw", "iw", "nw", "kw", "nv", "h2", "on", "lo" + s, "xx" + s] + ks(sr, p), [b], 64 * len(l))
        cx = "cx%d" % t; name(t, "t" + s)
        if t == 3: ts(T[cx][:, 1, c], B(k)[:, 80 + n:80 + 2 * n], float(W), None, OP.min, None, [b], ks(cx, p), n)
        else:
            ts(T[cx][:, :, c], B(k)[:, 80:80 + 2 * n], float(W), None, OP.min, None, [b], ks(cx, p), 2 * n)
            send(HOP, "aC%d_%d" % (m, k), ks(cx, p), ks("cu%d" % m, p), 256 * n, T["cu%d" % m][:, c], [T[cx][:, 0, c]])
            if C["ct"]:
                name(t, "j" + s)
                act(T["ct%d" % m][:, c], B(k)[:, 80:80 + n], AF.Copy, [b], ["ct%d" % m + s], n, scale=1.0 / W)
                send(HOP, "aD%d_%d" % (m, k), ["ct%d" % m + s], ks("cf%d" % m, p), 512 * n, T["cf%d" % m][:, c], [T["ct%d" % m][:, c]])
    def reports(t):
        rg = "rg%d" % t
        def rl(h): return slice(h[0] - R0, h[1] - R0)
        def rc(h): return slice(16 * (h[0] - R0), 16 * (h[1] - R0))
        for j, h in enumerate(C["rp"]):
            name(t, "r%d" % j)
            ts(T.fac[:, rc(h)], rho("pk%d" % t, h), 2.0, LN2H, OP.is_gt, OP.mult, ks(rg, h), ks("fac", h) + ["fac%d" % t], wn(h) / 2)
            name(t, "m%d" % j)
            tt(T.mn[:, rc(h)], T.lm[:].indirect(T.eu[:, rl(h)]), T.fac[:, rc(h)], OP.subtract, LM + ["eu"] + ks("fac", h), ks("mn", h), gn(h))
        for j, h in enumerate(C["sp"]):
            name(t, "S%d" % j)
            tt(T.lm[:].indirect(T.eu[:, rl(h)]), T.mn[:, rc(h)], T.mlo[:, 0:wn(h)], OP.max, ["eu", "mlo"] + ks("mn", h), LM, wn(h) * C["sc"])
        k = "lr%d" % (t + 1); n = C["nadd"]
        for j in range(n):
            c = slice(W // n * j, W // n * (j + 1)); name(t, "L%d" % j)
            dmas("G", "sL%d_%d" % (t + 1, j), LM + [k] + (["lr1", "lr2"] if t == 2 else []), ["%s_%d" % (k, j)], 2 * HALF // n,
                 [(T[k][:, c], T.lm[:, c])], accum_op=OP.add)
    def weights(t, w):
        p = WP[w]; b = 4 + w; n = wn(p); j = 16 * t if up(p) else 0; k = "b%d" % b; c = wc(p); a = t if up(p) else 0
        pk = "pk%d" % t; rg = "rg%d" % t; sr = "sr%d" % t; ag = "ag"; wi = "wi%d" % t; wo = "wo%d" % t; ix = "cx%d" % t
        l = [(B(b)[:, i:n:16], T.bw[:, i, j:j + 128], sr_(pk, p), False, i == 15) for i in range(16)]
        name(t, "R%d" % w)
        mms([(B(b)[:, 0:n], T.nw[:, 16:144], T.on[:, 0:n], True, False), (B(b)[:, 0:n], T.ir[:, 16 + j:144 + j], rho(pk, p), False, False)],
            ["ir", "nw", "on"] + ks(rg, p), [k], 2 * n)
        mms(l, BW + ks(sr, p), [k], 1024)
        win = T.at[:, a, :].indirect(T[ix][:, 1, lc(p)]); r = ["at%d" % a, "ax"] + ks(ix, p); sg = str(w) in C["sg"][t]
        name(t, "A%d" % w)
        if sg: act(alp(pk, p), win, AF.Copy, r, ks(ag, p), gn(p))
        name(t, "e%d" % w)
        if sg and t: tt(B(b)[:, 0:n], T[wi][:, c], B(b)[:, 0:n], OP.mult, ks(wi, p), [k], n)
        elif t: tt(T[wo][:, c], win, T[wi][:, c], OP.mult, r + ks(wi, p), ks(wo, p), gn(p))
        elif not sg: cp(T[wo][:, c], win, r, ks(wo, p), gn(p))
        for h in [p] if t < 3 else [h for h in C["fp"] if p[0] <= h[0] < p[1]]:
            o = B(b)[:, 16 * (h[0] - p[0]):16 * (h[1] - p[0])]
            name(t, "f%d" % w + "x" * (h[0] > p[0]))
            if t < C["dc"]:
                tt(T[wo][:, wc(h)], alp(pk, h) if sg else T[wo][:, wc(h)], o, OP.mult, [k] + ks(ag if sg else wo, h), ks(wo, h), wn(h))
                continue
            tt(o, alp(pk, h) if sg else T[wo][:, wc(h)], o, OP.mult, ks(ag if sg else wo, h), [k], wn(h))
            name(t, "k%d" % w + "x" * (h[0] > p[0]))
            ts(T[wo][:, wc(h)], o, 0.125, 4.0, OP.max, OP.min, [k], ks(wo, h), wn(h))
    def onward(t):
        m = t + 1; tm = C["tm"]
        for j, p in enumerate(C["send"][t]):
            c = wc(p); name(t, "W%d" % j)
            if C["dc"]:
                n = wn(p); mid = T.wm[4 * t + j]; key = ["wm%d_%d" % (t, j)]; keep = ["tb", "ta"][t:t + 1]
                send(C["mid"], "aM%d_%d" % (m, j), ks("wo%d" % t, p) + ["lob"], key, 512 * n, mid, [T["wo%d" % t][:, c], T.lob[:, 0:n]], 2)
                name(t, "X%d" % j)
                send(HOP - C["mid"], "aW%d_%d" % (m, j), key + ["hib"], ks("wi%d" % m, p) + [k for x in keep for k in ks(x, p)], 512 * n,
                     T["wi%d" % m][:, c], [mid, T.hib[:, 0:n]], 3, [(HOP * (3 - t) - C["mid"], T[x][:, c]) for x in keep])
                continue
            send(HOP, "aW%d_%d" % (m, j), ks("wo%d" % t, p), ks("wi%d" % m, p), 512 * wn(p), T["wi%d" % m][:, c], [T["wo%d" % t][:, c]])
        pr[0] += C["pt"]
        for j, p in enumerate([] if C["dc"] else C["tp"]):
            c = wc(p); n = 512 * wn(p); name(t, "T%d" % j)
            if t == 1 and tm == "f2": send(HOP, "aT1_%d" % j, ks("wo1", p) + ks("wi1", p), ks("tb", p), n, T.tb[:, c], [T.wo1[:, c], T.wi1[:, c]])
            elif t == 1: send(2 * HOP, "aT1_%d" % j, ks("wo1", p) + ks("wi1", p), ks("ta", p), n, T.ta[:, c], [T.wo1[:, c], T.wi1[:, c]])
            if t == 2 and tm == "f2": send(HOP, "aT2_%d" % j, ks("wo2", p) + ks("tb", p), ks("ta", p), n, T.ta[:, c], [T.wo2[:, c], T.tb[:, c]])
            if t == 2 and tm == "acc": dmas("G", "aT2_%d" % j, ks("wi3", p), ks("ta", p), n, [(T.ta[:, c], T.wi3[:, c])], accum_op=OP.add)
    def home():
        for j, p in enumerate(C["home"]):
            c = wc(p); s0 = 16 * ((p[0] + ROT) % 128); src = ["wo3", "ta"] + (["wi3", "tb"] if C["dc"] else ["wi3"] if C["tm"] == "f3" else [])
            name(3, "W%d" % j)
            send(-3 * HOP, "aF%d" % j, [k for n in src for k in ks(n, p)], ks("fl", p), 512 * wn(p), T.fl[:, c], [T[n][:, c] for n in src])
            e = C["oq"][j]; tag[0] = (3, "O%d" % j) if e == "S" else None
            dmas(e, "outs", ks("fl", p), [], 512 * wn(p), [(T.tl[:, s0:s0 + wn(p)], T.fl[:, c])])

    uz_(0)
    pr[0] = C["pu"][0]; uz_(1)
    pr[0] = 999; tag[0] = None; fill(1)
    for t in range(4):
        for k in range(len(CP)): pr[0] = 100 * t + 10 * k; way(t, k)
        for k in range(len(CP)): pr[0] = 100 * t + 10 * k + C["pc"]; collide(t, k)
        if t == 0: exp_()
        pr[0] = 100 * t + C["pr"]
        if t < 3: reports(t)
        pr[0] = 999; tag[0] = None
        if t < 3: load_al(t + 1)
        if t == 0: fill(2)
        for n in (2, 3) if t == 0 else (): pr[0] = C["pu"][n - 1]; uz_(n)
        for w in range(len(WP)): pr[0] = 100 * t + C["pw"] + w; weights(t, w)
        pr[0] = 100 * t + C["ps"]
        if t < 3: onward(t)
        else: home()

    place = {}; seen = {}
    for x in nodes:
        if x["tag"]:
            k = (x["e"],) + x["tag"]; seen[k] = seen.get(k, -1) + 1
            if seen[k] and x["tag"][1][0] in C["fine"]: x["tag"] = (x["tag"][0], x["tag"][1] + "-bcdefg"[seen[k]])
    for e in C["ord"]:
        for t, line in enumerate(C["ord"][e]):
            for j, x in enumerate(line.split()): place[(e, t - x.count("'") + x.count("+"), x.strip("'+"))] = 100 * t + j
    last = {}
    for i in sorted((i for i, x in enumerate(nodes) if x["tag"] and place), key=lambda i: (place[(nodes[i]["e"],) + nodes[i]["tag"]], i)):
        x = nodes[i]; x["rank"] = place[(x["e"],) + x["tag"]]
        if x["e"] in last: x["soft"] = {last[x["e"]]}
        last[x["e"]] = i
    cnt = {}; tok = {}; waited = {e: {} for e in qs}
    def wait(e, s, v):
        if waited[e].get(s, 0) < v:
            qs[e].wait_ge(T.sem[s], v); waited[e][s] = v
    for i in order_of(nodes, first):
        x = nodes[i]; e = x["e"]; s = x["sem"]; need = {}
        for d in x["deps"]:
            if x.get("own") or not e == nodes[d]["e"] == "P": need[tok[d][0]] = max(need.get(tok[d][0], 0), tok[d][1])
        for k in need: wait(e, k, need[k])
        for fn in x["calls"]:
            if x["inc"] > 0: fn().then_inc(T.sem[s], x["inc"])
            else: fn()
            cnt[s] = cnt.get(s, 0) + abs(x["inc"])
        tok[i] = (s, cnt[s])
    cnt["sent"] = sent[0]
    for s in cnt: wait("G", s, cnt[s])
